import numpy as np, ml_dtypes
CORES = [48,51,52,55]
N = 4
BF = ml_dtypes.bfloat16
def gentries(a):
    return np.ascontiguousarray(a.reshape(8, 16, -1).transpose(0, 2, 1)).reshape(8, -1)
def gtable(e):
    e = np.asarray(e); return np.ascontiguousarray(e.reshape(8, -1, 16).transpose(0, 2, 1)).reshape(128, -1).astype(np.int32)
W, R, S, K, M = 4096, 1024, 256, 16, 97
V, STEP = W + R, (1, 1, 1, 1)
RO = len(STEP)
def tops(st, s):
    col = np.take_along_axis(st, s[:, :, None], 3); h = np.add.reduce((col > 0).astype(np.int64), axis=2)
    return col, h, np.take_along_axis(col, np.maximum(h - 1, 0)[:, :, None], 2)[:, :, 0]
def aim(b, c):
    return (c - M * b) & (W - 1)
def fill(h, v):
    return np.where(np.arange(16)[:, None] < h, v, 0)
def parts(rng):
    share = np.array([0.0, 0.0, 0.1, 0.1, 0.3, 0.5, 0.8, 0.92])
    q = np.stack([rng.permutation(share) for a in range(N)]).reshape(N, 8, 1, 1); lo = np.stack([rng.permutation(8) for a in range(N)]).reshape(N, 8, 1, 1)
    h = lo + ((17 - lo) * rng.random((N, 8, 1, V))).astype(np.int64); h = np.minimum(np.where(rng.random((N, 8, 1, V)) < q, 16, h), 16)
    v = np.minimum(1 + (255 * rng.random((N, 8, 16, V)) ** rng.choice(np.array([0.5, 1.0, 2.0]), (N, 8, 1, 1))).astype(np.int64), 255)
    first = np.argsort(rng.random((N, 8, 1, V)), axis=-1)[..., :S]; later = W + np.argsort(rng.random((N, 8, RO - 1, R)), axis=-1)[..., :S]
    return fill(h, v), np.concatenate([first, later], axis=2), rng.integers(0, W, (N, 8, RO, K, S))
def pack(st, tr, ca):
    return {"days": np.ascontiguousarray(st.reshape(N, 128, V)).astype(np.float32).astype(BF),
            "trucks": np.stack([gtable(a.reshape(8, -1)) for a in tr]), "cand": np.stack([gtable(a.reshape(8, -1)) for a in ca])}
def setup_inputs(rng):
    return pack(*parts(rng))
def setup_inputs_ties(rng):
    st, tr, ca = parts(rng)
    p = rng.integers(1, 254, (N, 8, 1, 1)); p[0, 0] = 1; p[0, 1] = 253
    v = p + rng.integers(0, 3, st.shape); v[:, 2] = np.broadcast_to(p[:, 2], v[:, 2].shape); st = np.where(st > 0, v, 0)
    ca[:, :, :, K // 2:] = ca[:, :, :, :K // 2]
    e = 1 + np.argsort(rng.random((N, 4, V - 2)), axis=-1)[..., :S]; e[..., 0] = 0; e[..., S - 1] = V - 1; tr[:, 0::2, 0] = e
    e = W + 1 + np.argsort(rng.random((N, 4, RO - 1, R - 2)), axis=-1)[..., :S]; e[..., 0] = V - 1; e[..., S - 1] = W; tr[:, 1::2, 1:] = e
    b = np.roll(tops(st, tr[:, :, 0])[2], STEP[0], axis=0); n = S // 4
    ca[:, :, 0, :, :n] = aim(b[:, :, None, :n], rng.choice(np.array([0, W - 1]), (N, 8, K, n)))
    return pack(st, tr, ca)
def setup_inputs_full(rng):
    st, tr, ca = parts(rng)
    st = fill(np.where(rng.random((N, 8, 1, V)) < 0.8, 16, 15), rng.integers(1, 256, (N, 8, 16, V)))
    for a in range(N):
        for g in range(8):
            x = st[a, g]; s = tr[a, g, 0]
            x[:, s] = np.where(x[:, s] == 0, 7, x[:, s]); x[15, rng.permutation(s)[:S // 2]] = 1
    b = np.roll(tops(st, tr[:, :, 0])[2], STEP[0], axis=0); n = S // 8
    for a in range(N):
        for g in range(8):
            x = st[a, g]; s = tr[a, g, 0]; i = rng.permutation(S); c = ca[a, g, 0]
            rest = rng.permutation(np.setdiff1d(np.arange(W), s)); early, late = rest[:n], rest[n:2 * n]
            x[:, early] = fill(15, 1); x[:, late] = fill(16, 255)
            room = np.setdiff1d(np.nonzero(x[15, :W] == 0)[0], early)
            j = i[:S // 2]; c[:, j] = aim(b[a, g, j], rng.choice(s[s < W], (K, S // 2)))
            j = i[:n]; c[K - 1, j] = aim(b[a, g, j], rng.choice(room, n))
            j = i[S // 2:S // 2 + n]; c[:, j] = aim(b[a, g, j], rng.choice(late, (K, n))); c[K - 1, j] = aim(b[a, g, j], early)
    return pack(st, tr, ca)
def setup_inputs_bare(rng):
    st, tr, ca = parts(rng)
    o = rng.permutation(8); h = rng.integers(0, 4, (N, 8, 1, V)); h[:, o[0]] = 0; h[:, o[1]] = 1; h[:, o[2]] = rng.integers(0, 3, (N, 1, V))
    st = fill(h, rng.integers(1, 256, (N, 8, 16, V)))
    b = np.roll(tops(st, tr[:, :, 0])[2], STEP[0], axis=0)
    for a in range(N):
        for g in o[3:6]:
            s = tr[a, g, 0]; ca[a, g, 0][0] = aim(b[a, g], rng.choice(s[s < W], S))
    return pack(st, tr, ca)
def setup_inputs_crowd(rng):
    st, tr, ca = parts(rng); goals = []; q = int(rng.integers(0, N)); z = (q + STEP[0]) % N
    for a in range(N):
        for g in range(8):
            x = st[a, g]
            if a == z:
                o = int(rng.integers(0, W - S + 1)); o = o - o % S if g < 2 else o
                run = o + rng.permutation(S); x[15, run] = 0
                if g % 2 == 1:
                    tr[a, g, 0] = rng.permutation(run); x[:, run] = fill(rng.integers(1, 16, S), rng.integers(1, 256, S))
            s = tr[a, g, 0]
            if g % 2 == 0 or a == q:
                x[1:, s] = np.where(x[1:, s] > 0, np.maximum(x[1:, s], 2), 0); x[0, s] = 1; x[1, s] = np.maximum(x[1, s], 2)
            if a == z:
                goals.append(run)
            else:
                free = rng.permutation(np.setdiff1d(np.arange(W), s))[:(1, 2, S // 2, 1)[g // 2]]
                if g < 6: x[:, free] = 0
                goals.append(free if g < 6 else s[s < W])
    b = np.roll(tops(st, tr[:, :, 0])[2], STEP[0], axis=0)
    for a in range(N):
        for g in range(8):
            c = ca[a, g, 0]; k = 0 if a == q else int(rng.integers(0, K))
            if a == z: c[:] = aim(b[a, g], goals[8 * a + g])
            elif g < 6: c[k] = aim(b[a, g], rng.choice(goals[8 * a + g], S))
            else: c[:] = aim(b[a, g], rng.choice(goals[8 * a + g], (K, S)))
    ca[:, ::2, 1:] = rng.integers(0, 8, (N, 4, RO - 1, K, S)) + rng.integers(0, W - 8, (N, 4, RO - 1, 1, 1))
    return pack(st, tr, ca)
def setup_inputs_spread(rng):
    st, tr, ca = parts(rng)
    h = np.minimum((17 * rng.random((N, 8, 1, V)) ** rng.choice(np.array([0.2, 0.5, 1.0, 3.0]), (N, 8, 1, 1))).astype(np.int64), 16)
    v = np.minimum(np.maximum((np.exp2(8 * rng.random((N, 8, 1, V))) * rng.random((N, 8, 16, V))).astype(np.int64), 1), 255)
    ca = np.minimum((W * rng.random((N, 8, RO, K, S)) ** rng.choice(np.array([0.5, 1.0, 2.0, 4.0]), (N, 8, RO, 1, 1))).astype(np.int64), W - 1)
    return pack(fill(h, v), tr, ca)
def check_inputs(d):
    bad = []; x = np.asarray(d["days"]).astype(np.float32)
    if not np.all((x >= 0) & (x <= 255) & (x == np.floor(x))): bad.append("days: whole numbers from 0 to 255")
    z = x.reshape(N, 8, 16, V) > 0
    if np.any(z[:, :, 1:] & ~z[:, :, :-1]): bad.append("days: no box above an empty tier")
    s = np.stack([gentries(a) for a in d["trucks"]]).astype(np.int64).reshape(N, 8, RO, S)
    if np.min(s) < 0 or np.max(s) > V - 1 or np.min(s[:, :, 1:]) < W: bad.append("range of trucks")
    o = np.sort(s, axis=-1)
    if np.any(o[..., 1:] == o[..., :-1]): bad.append("trucks: different stacks in a block")
    if np.min(d["cand"]) < 0 or np.max(d["cand"]) > W - 1: bad.append("range of cand")
    return bad
def reference(days, trucks, cand):
    st = np.asarray(days).astype(np.float32).astype(np.int64).reshape(N, 8, 16, V)
    tr = np.stack([gentries(a) for a in trucks]).astype(np.int64).reshape(N, 8, RO, S)
    ca = np.stack([gentries(a) for a in cand]).astype(np.int64).reshape(N, 8, RO, K, S)
    lower = np.tril(np.ones((S, S), bool), -1); s = tr[:, :, 0]
    for t in range(RO):
        col, h, b = tops(st, s)
        asks = np.any((col > 0) & (col < b[:, :, None]), axis=2)
        bb = np.roll(b, STEP[t], axis=0); ask = np.roll(asks, STEP[t], axis=0)
        c = (ca[:, :, t] + M * bb[:, :, None]) & (W - 1)
        cc = np.take_along_axis(st, c.reshape(N, 8, 1, K * S), 3).reshape(N, 8, 16, K, S)
        score = np.add.reduce(((cc > 0) & (cc < bb[:, :, None, None])).astype(np.int64), axis=2) + 16 * (cc[:, :, 15] > 0)
        best = np.argmin(score, axis=2)[:, :, None]
        dst = np.take_along_axis(c, best, 2)[:, :, 0]; low = np.take_along_axis(score, best, 2)[:, :, 0]
        clash = np.any((dst[..., :, None] == dst[..., None, :]) & ask[..., None, :] & lower, axis=3)
        land = ask & (low < 16) & ~clash
        gone = (b > 0) & (~asks | np.roll(land, -STEP[t], axis=0))
        st = st.copy()
        a, g, i = np.nonzero(gone); st[a, g, h[a, g, i] - 1, s[a, g, i]] = 0
        a, g, i = np.nonzero(land); v = dst[a, g, i]
        top = np.add.reduce((st[a, g, :, v] > 0).astype(np.int64), axis=1); st[a, g, top, v] = bb[a, g, i]
        if t + 1 < RO: s = np.where(land, dst, tr[:, :, t + 1])
    return {"y": st.reshape(N, 128, V).astype(np.float32).astype(BF)}

@@ -1,0 +1,495 @@
+from concourse.mybir import AluOpType, ActivationFunctionType
+
+W, R, S, K, M = 4096, 1024, 256, 16, 97
+V = W + R
+STEP = (1, 1, 1, 1)
+RO = len(STEP)
+NCH = 5
+CH = V // NCH
+EARLY = 2
+ENGINES = 16
+KLAST = 12
+SCHED = (("vg", 0), ("sg", 0, 4), ("z", 0), ("sg", 1, 8), ("vg", 2), ("z", 1), ("key", 0, 4), ("ss", 0, 4), ("vg", 6),
+         ("sg", 2, 12), ("key", 4, 8), ("z", 2), ("ss", 1, 8), ("vg", 10), ("key", 8, 12), ("ss", 2, 12), ("vg", 14),
+         ("key", 12, 16))
+
+BF, F32, I32, U16, F16 = "bfloat16", "float32", "int32", "uint16", "float16"
+SCRATCH = {
+    "XB": ("sbuf", [128, S + V], BF), "Y": ("sbuf", [128, V], BF), "mk": ("sbuf", [128, V], BF),
+    "trk": ("sbuf", [128, 64], I32), "cnd": ("sbuf", [128, 1024], I32),
+    "bin": ("sbuf", [128, 16 * RO], BF), "bout": ("sbuf", [128, 16 * RO], BF),
+    "vin": ("sbuf", [128, S * RO], BF), "vout": ("sbuf", [128, S * RO], BF),
+    "cmp": ("sbuf", [128, K * S], BF), "xg": ("sbuf", [128, 512 * 4], BF),
+    "eq": ("sbuf", [128, 16 * S], BF), "ab": ("sbuf", [128, S], BF),
+    "iq": ("sbuf", [128, 8], I32), "ix": ("sbuf", [128, 144], BF), "ig": ("sbuf", [128, 128], BF),
+    "ia": ("sbuf", [128, S], F32), "kc": ("sbuf", [128, S], BF), "i16": ("sbuf", [128, 16], F32),
+    "LE": ("sbuf", [128, 2048], BF), "LD": ("sbuf", [128, 2048], BF),
+    "cols": ("sbuf", [128, 64], F32), "pmi": ("sbuf", [128, 8], I32),
+    "BW": ("sbuf", [128, 144], BF), "BU": ("sbuf", [128, 144], BF), "BN": ("sbuf", [128, 144], BF),
+    "mats": ("sbuf", [128, 128 * 16], BF), "msk": ("sbuf", [128, S], BF), "rep": ("sbuf", [128, 16], U16),
+    "uf": ("sbuf", [128, 80], F32), "um": ("sbuf", [128, 80], F32), "su": ("sbuf", [128, 80], U16),
+    "uu": ("sbuf", [128, 64], U16),
+    "b97": ("sbuf", [128, 16], F32), "s32": ("sbuf", [128, S], I32), "c32": ("sbuf", [128, S], I32),
+    "cu": ("sbuf", [128, S], U16), "c16": ("sbuf", [128, S], F16),
+    "brow": ("sbuf", [128, 2 * S], BF), "nk": ("sbuf", [128, 64], BF),
+    "tr": ("sbuf", [128, 320], F32), "ki": ("sbuf", [128, 32], I32),
+    "dz16": ("sbuf", [128, 16], F16), "dzf": ("sbuf", [128, 16], F32), "du": ("sbuf", [128, 96], F32),
+    "row": ("sbuf", [128, S], F16), "nok": ("sbuf", [128, S], BF), "LB": ("sbuf", [128, 2 * S], BF),
+    "ne": ("sbuf", [128, S], BF), "colg": ("sbuf", [128, S], BF), "tl": ("sbuf", [128, 2 * S], BF),
+    "cm": ("sbuf", [128, 48], F32), "tmp": ("sbuf", [128, S], BF), "tmp2": ("sbuf", [128, S], BF),
+    "keep": ("sbuf", [128, S], BF), "cY": ("sbuf", [128, S], BF), "cX": ("sbuf", [128, S], BF),
+    "nes": ("sbuf", [128, S], BF), "dS": ("sbuf", [128, S], BF),
+    "cU": ("sbuf", [128, S], BF), "neU": ("sbuf", [128, S], BF), "tlU": ("sbuf", [128, 4 * S], BF),
+    "cuw": ("sbuf", [128, 32], F32), "abw": ("sbuf", [128, 96], F32), "th": ("sbuf", [128, 2 * S], BF),
+}
+BANKS = ("EXP", "DG", "KA", "KB", "ZA", "ZB", "CNT", "WR")
+for _b in BANKS:
+    SCRATCH[_b] = ("psum", [128, 512], F32)
+QUEUES = ("v", "s", "p", "g", "y")
+SEMAPHORES = (["q_" + q for q in QUEUES] + ["ask%d" % t for t in range(RO)] + ["ver%d" % t for t in range(RO)]
+              + ["sent"] + ["dma%d" % i for i in range(16)])
+
+A = AluOpType
+F = ActivationFunctionType
+
+
+def rank_program(g, core, T, topo):
+    rank = T.rank_of(core)
+    if rank is None:
+        return
+    n = len(T.cores)
+    Q = {"v": g.vector, "s": g.scalar, "p": g.tensor, "g": g, "y": g.sync}
+    ops = []
+    ndma = [0]
+
+    def ap(name, a=0, b=None, st=1):
+        if b is None:
+            b = SCRATCH[name][1][1]
+        p = T[name][:, a:b] if st == 1 else T[name][:, a:b:st]
+        return (p, [(name, a, b)])
+
+    def ind(win, off):
+        return (win[0].indirect(off[0]), win[1] + off[1], win[1], off[1])
+
+    def add(q, emit, ins, out, kind="c", sem=None):
+        rd, wr = [], []
+        for x in ins:
+            if isinstance(x, tuple):
+                rd += x[1]
+        if out is not None:
+            if len(out) == 4:
+                wr += out[2]
+                rd += out[3]
+            else:
+                wr += out[1]
+        ops.append((q, emit, rd, wr, kind, sem))
+
+    def val(x):
+        return x[0] if isinstance(x, tuple) else x
+
+    def vcopy(o, i):
+        add("v", lambda: g.vector.tensor_copy(o[0], i[0]), [i], o)
+
+    def vtt(o, a, b, op):
+        add("v", lambda: g.vector.tensor_tensor(o[0], a[0], b[0], op), [a, b], o)
+
+    def vts(o, a, s1, op0, s2=None, op1=None):
+        if op1 is None:
+            add("v", lambda: g.vector.tensor_scalar(o[0], a[0], val(s1), None, op0), [a, s1], o)
+        else:
+            add("v", lambda: g.vector.tensor_scalar(o[0], a[0], val(s1), val(s2), op0, op1), [a, s1, s2], o)
+
+    def vset(o, c):
+        add("v", lambda: g.vector.memset(o[0], c), [], o)
+
+    def act(o, i, func, bias=None, scale=None):
+        kw = {}
+        if bias is not None:
+            kw["bias"] = val(bias)
+        if scale is not None:
+            kw["scale"] = val(scale)
+        add("s", lambda: g.scalar.activation(o[0], i[0], func, **kw), [i, bias, scale], o)
+
+    def mm(o, l, r, start, stop):
+        add("p", lambda: g.tensor.matmul(o[0], l[0], r[0], start, stop), [l, r], o)
+
+    def mms(o, terms, start=True, stop=True):
+        for j, (l, r) in enumerate(terms):
+            mm(o, l, r, start and j == 0, stop and j == len(terms) - 1)
+
+    def iota(o, pattern, base, cm, small=True):
+        if small:
+            add("g", lambda: g.iota(o[0], pattern, base, cm, allow_small_or_imprecise_dtypes=True), [], o)
+        else:
+            add("g", lambda: g.iota(o[0], pattern, base, cm), [], o)
+
+    def dma(q, o, i):
+        sem = "dma%d" % ndma[0]
+        ndma[0] += 1
+        add(q, lambda: Q[q].dma_start(o[0], i[0]), [i], o, "d", sem)
+
+    def hbm(t, a, b):
+        return (t[:, a:b], [])
+
+    def emask(dst):
+        m = 0
+        for e in topo.engines(core, dst)[:ENGINES]:
+            m |= 1 << e
+        return m
+
+    def send(dst, o, i, sem):
+        rid, pid, _ = topo.addr(dst)
+        add("g", lambda: g.remote_dma(o[0], i[0], T.sem[sem], T.sem.sent, pid, rid, emask(dst)), [i], None, "r")
+
+    def arrives(o, sem):
+        add(None, None, [], o, "a", sem)
+
+    def col(j):
+        return ap("cols", j, j + 1)
+
+    def mat(j):
+        return ap("mats", 128 * j, 128 * (j + 1))
+    ID, NID, I256, I8K, GG, NG, D0, EMP, EMN, ZERO, T1, D1, U0, T2 = [mat(j) for j in range(14)]
+    (PM, QF, G16, G15, QM1, QP1, NZ0, NZ15, WCOL, B15, BY, BX, MB, QM2, GE2) = [col(4 * j) for j in range(15)]
+
+    def wrap(o, bname, src, a0, a1, start, stop):
+        for a in range(16):
+            mm(o, ap(bname, 15 - a, 143 - a), ap(src, a0 + a, a1, 16), start and a == 0, stop and a == 15)
+
+    def expand(bank, lname, src, alone, stop=True):
+        for a in range(16):
+            mm(ap(bank, a, S, 16), ap(lname, 128 * a, 128 * (a + 1)), src, alone, alone or (stop and a == 15))
+
+    X = ap("XB", S, S + V)
+    Y = ap("Y")
+
+    dma("s", ap("trk"), hbm(T.trucks, 0, 64))
+    dma("y", ap("XB", S, S + EARLY * CH), hbm(T.days, 0, EARLY * CH))
+    dma("y", ap("XB", S + EARLY * CH, S + V), hbm(T.days, EARLY * CH, V))
+    dma("y", ap("cnd"), hbm(T.cand, 0, 1024))
+
+    iota(ap("iq", 0, 1), [[0, 1]], 0, 1, small=False)
+    iota(ap("ix"), [[1, 144]], 0, 0)
+    iota(ap("ig"), [[16, 8], [0, 16]], 0, 0)
+    iota(ap("ia"), [[0, 16], [1, 16]], 0, 0)
+    iota(ap("i16"), [[16, 16]], 0, 0)
+    iota(ap("kc"), [[4096, 16], [0, 16]], 2048, 0)
+    vset(ZERO, 0.0)
+    vset(ap("XB", 0, S), 0.0)
+    vts(ap("pmi", 0, 1), ap("iq", 0, 1), 15, A.bitwise_and)
+    vcopy(QF, ap("iq", 0, 1))
+    vcopy(PM, ap("pmi", 0, 1))
+    vts(QM1, QF, -1.0, A.add)
+    vts(QP1, QF, 1.0, A.add)
+    vts(QM2, QF, -2.0, A.add)
+    vtt(G16, QF, PM, A.subtract)
+    vts(BX, PM, 0.0, A.not_equal, -256.0, A.mult)
+    vts(BY, PM, 0.0, A.not_equal, 256.0, A.mult)
+    vts(NZ15, PM, 15.0, A.not_equal)
+    vts(B15, PM, 15.0, A.is_equal, 256.0, A.mult)
+    vts(MB, PM, 0.5, A.add, 256.0, A.mult)
+    vts(GE2, PM, 2.0, A.is_ge, 256.0, A.mult)
+    vts(G15, G16, 15.0, A.add)
+    vts(WCOL, B15, 3840.0, A.mult, 65536.0, A.add)
+    vts(NZ0, NZ15, 256.0, A.mult)
+    ix = ap("ix", 0, 128)
+    vts(ID, ix, QF, A.is_equal)
+    vts(NID, ix, QF, A.is_equal, -1.0, A.mult)
+    vts(I256, ix, QF, A.is_equal, 256.0, A.mult)
+    vts(U0, ix, QM1, A.is_equal, BY, A.mult)
+    vts(GG, ap("ig"), G16, A.is_equal)
+    vts(ap("BU"), ap("ix"), G15, A.is_equal)
+    vts(ap("BN"), ap("ix"), G15, A.is_equal, -0.0625, A.mult)
+    vts(ap("BW"), ap("ix"), G15, A.is_equal, WCOL, A.mult)
+    vtt(D0, I256, U0, A.subtract)
+    act(ap("msk"), ap("ia"), F.Sigmoid, bias=MB, scale=-256.0)
+    vts(I8K, ix, QF, A.is_equal, 8192.0, A.mult)
+    vts(NG, ap("ig"), G16, A.is_equal, -1.0, A.mult)
+    vts(T1, ix, QP1, A.is_equal, NZ0, A.mult)
+    vts(T2, ix, QM2, A.is_equal, GE2, A.mult)
+    vts(ap("rep"), ap("ia", 0, 16), 0.0, A.mult, PM, A.add)
+    vtt(EMP, T1, I256, A.subtract)
+    vtt(EMN, I256, T1, A.subtract)
+    vtt(D1, U0, T2, A.subtract)
+    for a in range(16):
+        vts(ap("LE", 128 * a, 128 * (a + 1)), ap("ig"), float(a), A.add, QF, A.is_equal)
+    vcopy(ap("su", 0, 16), ap("trk", 0, 16))
+
+    conv_banks = ("ZA", "ZB", "KA", "KB")
+
+    def mask_chunk(c):
+        vts(ap("mk", c * CH, (c + 1) * CH), ap("XB", S + c * CH, S + (c + 1) * CH), 0.0, A.is_equal, 256.0, A.mult)
+
+    def conv(h):
+        bank = ap(conv_banks[h % 4])
+        mms(bank, [(ID, ap("XB", S + 512 * h, S + 512 * (h + 1))), (ID, ap("mk", 512 * h, 512 * (h + 1)))])
+        act(ap("Y", 512 * h, 512 * (h + 1)), bank, F.Copy)
+
+    def late_constants():
+        vcopy(ap("uf", 0, 64), ap("trk"))
+        vcopy(ap("uu"), ap("trk"))
+        vts(ap("uf", 64, 80), ap("i16"), PM, A.add)
+        vts(ap("um", 0, 64), ap("uf", 0, 64), -2048.0, A.add)
+        vts(ap("um", 64, 80), ap("uf", 64, 80), -2048.0 - S, A.add)
+        for a in range(16):
+            vtt(ap("LD", 128 * a, 128 * (a + 1)), ap("LE", 128 * a, 128 * (a + 1)), ID, A.subtract)
+
+    for c in range(EARLY):
+        mask_chunk(c)
+        conv(2 * c)
+        conv(2 * c + 1)
+
+    def su(t):
+        return ap("su", 16 * t, 16 * (t + 1))
+    land_neg, landb_neg = ap("LB", 0, S), ap("LB", S, 2 * S)
+    ne, colg, tv, lt = ap("ne"), ap("colg"), ap("tl", 0, S), ap("tl", S, 2 * S)
+
+    def send_ask(t):
+        send(T.cores[(rank + STEP[t]) % n], ap("bin", 16 * t, 16 * (t + 1)), ap("bout", 16 * t, 16 * (t + 1)), "ask%d" % t)
+
+    def first_ask():
+        vts(ne, ind(X, su(0)), 0.0, A.is_gt)
+        act(colg, ind(X, su(0)), F.Copy)
+        z, z2 = ap("DG", 0, S), ap("CNT", 0, S)
+        mms(z, [(ID, colg), (D0, ne)])
+        mms(z2, [(NID, colg), (I256, ne)], True, False)
+        vts(tv, z, -256.0, A.add, 0.0, A.max)
+        mm(z2, GG, tv, False, True)
+        vts(lt, z2, 256.0, A.is_gt)
+        wrap(ap("WR", 32, 64), "BU", "tl", 0, 2 * S, True, True)
+        vts(ap("cm", 0, 16), ap("WR", 48, 64), 256.0, A.mult)
+        vtt(ap("bout", 0, 16), ap("WR", 32, 48), ap("cm", 0, 16), A.min)
+        send_ask(0)
+
+    def next_ask(t):
+        vtt(lt, ind(Y, su(t)), ap("th", S, 2 * S), A.is_le)
+        act(colg, ind(Y, su(t)), F.Copy)
+        act(ne, colg, F.Sign, bias=256.0, scale=-1.0)
+        wrap(ap("WR", 32, 48), "BU", "tl", S, 2 * S, True, True)
+        vts(ap("cm", 0, 16), ap("WR", 32, 48), 1.0, A.min)
+        vtt(ap("cm", 16, 32), ap("cm", 0, 16), ap("abw", 64, 80), A.mult)
+        vtt(ap("bout", 16 * t, 16 * (t + 1)), ap("cm", 16, 32), ap("abw", 80, 96), A.add)
+        send_ask(t)
+
+    def x_follow(t):
+        vtt(ind(X, su(t)), ap("cX"), ap("keep"), A.mult)
+
+    def main(t):
+        last = t == RO - 1
+        b = ap("bin", 16 * t, 16 * (t + 1))
+        arrives(b, "ask%d" % t)
+        ex = ap("EXP", 0, S)
+        vts(ap("b97"), b, float(M), A.mult)
+        expand("EXP", "LE", b, True)
+        act(ap("nk"), ind(b, ap("rep", 0, 4)), F.Relu, bias=1048576.0, scale=-1048576.0)
+        act(ap("brow", 0, S), ex, F.Identity, bias=B15, scale=NZ15)
+        act(ap("brow", S, 2 * S), ex, F.Identity, bias=B15, scale=NZ15)
+        vtt(ap("s32"), ind(ap("b97"), ap("rep")), ap("cnd", S * t, S * (t + 1)), A.add)
+        vts(ap("c32"), ap("s32"), W - 1, A.bitwise_and)
+        vcopy(ap("cu"), ap("c32"))
+        vts(ap("c16"), ap("cu"), -2048.0, A.add)
+        zb = ("ZA", "ZB")
+        cnt = ap("CNT", 0, S)
+        na = 16 * KLAST
+        mm(cnt, ZERO, ap("kc"), True, False)
+        expand("CNT", "LE", ap("nk", 0, 16), False, False)
+        mm(ap("DG", 0, S), I8K, ap("msk"), True, False)
+        mm(ap("KA", 0, na), ID, ap("kc", 0, na), True, False)
+        mm(ap("KB", 0, S - na), ID, ap("kc", na, S), True, False)
+        for c in range(0, na, 64):
+            mm(ap("KA", c, c + 64), ID, ap("nk"), False, False)
+        mm(ap("KB", 0, S - na), ID, ap("nk", 0, S - na), False, False)
+        mm(ap("KA", 0, na), ID, ap("c16", 0, na), False, False)
+        mm(ap("KB", 0, S - na), ID, ap("c16", na, S), False, False)
+        last_a = max(i for i, s in enumerate(SCHED) if s[0] == "key" and s[1] < KLAST)
+        for i, s in enumerate(SCHED):
+            if s[0] == "sg":
+                act(ap("xg", 512 * s[1], 512 * (s[1] + 1)), ind(Y, ap("cu", 16 * s[2], 16 * s[2] + 32)), F.Copy)
+            elif s[0] == "z":
+                mms(ap(zb[s[1] % 2]), [(NID, ap("brow")), (ID, ap("xg", 512 * s[1], 512 * (s[1] + 1)))])
+            elif s[0] == "ss":
+                act(ap("cmp", S * s[2], S * (s[2] + 2)), ap(zb[s[1] % 2]), F.Sigmoid, bias=-128.0, scale=-256.0)
+            elif s[0] == "vg":
+                vtt(ap("cmp", S * s[1], S * (s[1] + 2)), ind(Y, ap("cu", 16 * s[1], 16 * s[1] + 32)), ap("brow"), A.is_lt)
+            elif s[1] < KLAST:
+                wrap(ap("KA", 16 * s[1], 16 * s[2]), "BW", "cmp", S * s[1], S * s[2], False, i == last_a)
+            else:
+                wrap(ap("KB", 0, S - na), "BW", "cmp", S * s[1], S * s[2], False, True)
+        cU, neU = ap("cU"), ap("neU")
+        if not last:
+            act(cU, ind(Y, ap("uu", 16 * (t + 1), 16 * (t + 2))), F.Copy)
+            act(neU, cU, F.Sign, bias=256.0, scale=-1.0)
+            mms(ap("ZA", 0, S), [(ID, cU), (D0, neU)])
+            mms(ap("ZA", S, 2 * S), [(ID, cU), (D1, neU)])
+        act(ap("cY"), ind(Y, su(t)), F.Copy)
+        act(ap("nes"), ap("cY"), F.Sign, bias=256.0, scale=-1.0)
+        if not last:
+            act(ap("tlU", 0, 2 * S), ap("ZA"), F.Relu, bias=-256.0)
+        vcopy(ap("tr", 0, 64), ap("KA", 0, 64))
+        vtt(ap("tr", 64, 128), ap("KA", 64, 128), ap("tr", 0, 64), A.min)
+        vtt(ap("tr", 128, 192), ap("KA", 128, 192), ap("tr", 64, 128), A.min)
+        vtt(ap("tr", 192, 256), ap("KB", 0, 64), ap("tr", 128, 192), A.min)
+        vtt(ap("tr", 256, 288), ap("tr", 192, 224), ap("tr", 224, 256), A.min)
+        vtt(ap("ki", 0, 16), ap("tr", 256, 272), ap("tr", 272, 288), A.min)
+        vts(ap("ki", 16, 32), ap("ki", 0, 16), 0x300FFF, A.bitwise_and)
+        vts(ap("dz16"), ap("ki", 16, 32), 4096.0, A.min, -2048.0, A.add)
+        vts(ap("dzf"), ap("ki", 16, 32), 4096.0, A.min, -2048.0, A.add)
+        vtt(ap("du", 0, 16), ap("dzf"), ap("um", 16 * (t + 1), 16 * (t + 2)), A.subtract)
+        expand("KA", "LE", ap("dz16"), True)
+        expand("DG", "LD", ap("dz16"), False)
+        vcopy(ap("row"), ap("KA", 0, S))
+        act(ap("nok"), ap("KA", 0, S), F.Sign, bias=-2048.0)
+        act(ap("ab"), ap("DG", 0, S), F.Abs)
+        ed = ap("eq", S * 15, S * 16)
+        act(ed, ap("ab"), F.Relu, bias=1.0, scale=-1.0)
+        for m in range(15):
+            e = ap("eq", S * m + 16 * (m + 1), S * (m + 1))
+            vts(e, ap("row", 16 * (m + 1), S), ap("dzf", m, m + 1), A.is_equal)
+            if m == 13:
+                mm(cnt, NG, ed, False, False)
+            mm(ap("CNT", 16 * (m + 1), S), NG, e, False, m == 14)
+        vo = ap("vout", S * t, S * (t + 1))
+        vtt(vo, cnt, ap("nok"), A.is_gt)
+        send(T.cores[(rank - STEP[t]) % n], ap("vin", S * t, S * (t + 1)), vo, "ver%d" % t)
+        vtt(land_neg, vo, ap("nok"), A.mult)
+        if not last:
+            mms(ap("ZB", 0, S), [(NID, cU), (I256, neU), (GG, ap("tlU", 0, S))])
+            mms(ap("ZB", S, 2 * S), [(NID, cU), (U0, neU), (GG, ap("tlU", S, 2 * S))])
+            act(ap("tlU", 2 * S, 4 * S), ap("ZB"), F.Relu, bias=-256.0)
+        wrap(ap("WR", 0, 16), "BN", "LB", 0, S, True, True)
+        vtt(landb_neg, ex, land_neg, A.mult)
+        mms(ap("KA", 0, S), [(D0, ap("nes")), (NID, ap("cY"))])
+        act(ap("dS"), ap("KA", 0, S), F.Relu, scale=-1.0 if last else 1.0)
+        vtt(ap("du", 16, 32), ap("WR", 0, 16), ap("du", 0, 16), A.mult)
+        if not last:
+            vcopy(ap("du", 48, 64), ap("WR", 0, 16))
+        vtt(ap("du", 32, 48), ap("du", 16, 32), ap("uf", 16 * (t + 1), 16 * (t + 2)), A.add)
+        vcopy(su(t + 1), ap("du", 32, 48))
+        if not last:
+            wrap(ap("EXP", 0, 64), "BU", "tlU", 0, 4 * S, True, True)
+            mms(ap("DG", 0, S), [(ID, ap("tlU", 0, S)), (I256, land_neg)])
+            act(ap("th", 0, S), ap("DG", 0, S), F.Relu)
+            mms(ap("ZA", 0, S), [(NID, landb_neg), (ID, land_neg), (ID, ap("th", 0, S))])
+            act(ap("th", S, 2 * S), ap("ZA", 0, S), F.Copy)
+        mms(ap("ZB", 0, S), [(I256, ap("nes")), (ID, ap("cY"))])
+        act(ap("cX"), ap("ZB", 0, S), F.Identity, bias=-256.0)
+        if not last:
+            lw = ap("du", 48, 64)
+            vts(ap("cuw"), ap("EXP", 32, 64), 256.0, A.mult)
+            vtt(ap("abw", 0, 32), ap("EXP", 0, 32), ap("cuw"), A.min)
+            vtt(ap("abw", 32, 48), ap("abw", 0, 16), ap("abw", 16, 32), A.subtract)
+            vtt(ap("du", 64, 80), lw, ap("abw", 16, 32), A.mult)
+            vtt(ap("abw", 48, 64), b, ap("abw", 32, 48), A.subtract)
+            vtt(ap("abw", 80, 96), ap("abw", 16, 32), ap("du", 64, 80), A.subtract)
+            vtt(ap("du", 80, 96), lw, ap("abw", 48, 64), A.mult)
+            vtt(ap("abw", 64, 80), ap("du", 80, 96), ap("abw", 32, 48), A.add)
+
+    first_ask()
+    for c in range(EARLY, NCH):
+        mask_chunk(c)
+    for h in range(2 * EARLY, 2 * NCH):
+        conv(h)
+    late_constants()
+    for t in range(RO):
+        main(t)
+        v = ap("vin", S * t, S * (t + 1))
+        zl = ap("KB", 0, S)
+        if t < RO - 1:
+            mms(zl, [(NID, landb_neg), (I256, land_neg)], True, False)
+            arrives(v, "ver%d" % t)
+            vtt(ap("tmp"), v, ap("dS"), A.mult)
+            vtt(ind(Y, su(t)), ap("cY"), ap("tmp"), A.add)
+            next_ask(t + 1)
+            mm(zl, EMN, ne, False, True)
+            vts(ap("tmp2"), zl, BY, A.add, 0.0, A.min)
+            vtt(ind(Y, su(t + 1)), colg, ap("tmp2"), A.add)
+            vts(ap("keep"), ap("tmp"), 0.0, A.is_equal)
+            x_follow(t)
+        else:
+            mm(zl, NID, landb_neg, True, False)
+            arrives(v, "ver%d" % t)
+            vtt(ap("keep"), v, ap("dS"), A.is_le)
+            x_follow(t)
+            dma("y", hbm(T.y, W, V), ap("XB", S + W, S + V))
+            xw = ap("XB", 0, S + W)
+            vts(ne, ind(xw, su(t + 1)), 0.0, A.is_gt)
+            act(colg, ind(xw, su(t + 1)), F.Copy)
+            mm(zl, EMP, ne, False, True)
+            vts(ap("tmp2"), zl, BX, A.add, 0.0, A.max)
+            vtt(ind(xw, su(t + 1)), colg, ap("tmp2"), A.add)
+            dma("s", hbm(T.y, 0, W), ap("XB", S, S + W))
+
+    emit_all(g, T, Q, ops)
+
+
+def emit_all(g, T, Q, ops):
+    hist = {}
+    need = []
+    signal = set()
+    known = {q: ({}, set()) for q in QUEUES}
+    clock = []
+    for j, (q, emit, rd, wr, kind, sem) in enumerate(ops):
+        deps = set()
+        for acc, is_w in ((rd, False), (wr, True)):
+            for (name, a, b) in acc:
+                bank = name in BANKS
+                for (a2, b2, i, w2) in hist.get(name, []):
+                    q2 = ops[i][0]
+                    if bank and q2 != q:
+                        deps.add(i)
+                    elif bank and q == "p":
+                        continue
+                    elif a < b2 and a2 < b and (is_w or w2):
+                        deps.add(i)
+        for acc, is_w in ((rd, False), (wr, True)):
+            for (name, a, b) in acc:
+                hist.setdefault(name, []).append((a, b, j, is_w))
+        if kind == "a":
+            need.append([])
+            clock.append(({}, {j}))
+            continue
+        eng, ext = known[q]
+        waits = []
+        for i in sorted(deps, reverse=True):
+            qi, ki = ops[i][0], ops[i][4]
+            if (ki == "c" and eng.get(qi, -1) >= i) or (ki != "c" and i in ext) or ki == "r":
+                continue
+            waits.append(i)
+            ce, cx = clock[i]
+            for e, x in ce.items():
+                if eng.get(e, -1) < x:
+                    eng[e] = x
+            ext.update(cx)
+        need.append(waits)
+        signal.update(waits)
+        ce, cx = dict(eng), set(ext)
+        if kind == "c":
+            ce[q] = j
+        else:
+            cx.add(j)
+        clock.append((ce, cx))
+    count = {q: 0 for q in QUEUES}
+    value = {}
+    waited = set()
+    nsent = 0
+    for j, (q, emit, rd, wr, kind, sem) in enumerate(ops):
+        if kind == "a":
+            value[j] = (sem, ENGINES)
+            continue
+        for i in need[j]:
+            Q[q].wait_ge(T.sem[value[i][0]], value[i][1])
+            waited.add(value[i][0])
+        ins = emit()
+        if kind == "c" and j in signal:
+            count[q] += 1
+            value[j] = ("q_" + q, count[q])
+            ins.then_inc(T.sem["q_" + q], 1)
+        elif kind == "d":
+            value[j] = (sem, 16)
+            ins.then_inc(T.sem[sem], 16)
+        elif kind == "r":
+            nsent += 1
+    g.wait_ge(T.sem.sent, nsent * ENGINES)
+    for j, (q, emit, rd, wr, kind, sem) in enumerate(ops):
+        if kind in ("d", "a") and sem not in waited:
+            g.wait_ge(T.sem[sem], value[j][1])

@@ -1,3 +1,4 @@
+from concourse.bass import DstId, RemoteDMATransfer
 from concourse.mybir import AluOpType, ActivationFunctionType
 
 W, R, S, K, M = 4096, 1024, 256, 16, 97
@@ -6,48 +7,61 @@ STEP = (1, 1, 1, 1)
 RO = len(STEP)
 NCH = 5
 CH = V // NCH
-EARLY = 2
+EARLY = 3
 ENGINES = 16
 KLAST = 12
-SCHED = (("vg", 0), ("sg", 0, 4), ("z", 0), ("sg", 1, 8), ("vg", 2), ("z", 1), ("key", 0, 4), ("ss", 0, 4), ("vg", 6),
-         ("sg", 2, 12), ("key", 4, 8), ("z", 2), ("ss", 1, 8), ("vg", 10), ("key", 8, 12), ("ss", 2, 12), ("vg", 14),
-         ("key", 12, 16))
+VP = S + 16
+BIG = 8192.0
+QB = 192.0
+SCHED = (("vg", 0), ("sg", 0, 4), ("dg",), ("old",), ("z", 0), ("sg", 1, 8), ("vg", 2), ("z", 1), ("key", 0, 4),
+         ("ss", 0, 4), ("pre", 2), ("vg", 6), ("sg", 2, 12), ("key", 4, 8), ("z", 2), ("nk",), ("ss", 1, 8),
+         ("vg", 10), ("key", 8, 12), ("ss", 2, 12), ("vg", 14), ("key", 12, 16))
 
 BF, F32, I32, U16, F16 = "bfloat16", "float32", "int32", "uint16", "float16"
+MATS = ("ID", "NID", "I256", "N256", "I8K", "I97", "N4K", "IH", "DG0", "DL", "NDL", "DJ", "GG", "NG", "GI", "G012",
+        "G34", "LE0", "U0", "T1", "T2", "D0", "ND0", "D1", "EMP", "EMN", "E0", "E1", "E2", "E3", "F0", "F1", "F2", "F3")
+WRAPS = ("BU", "B012", "BW", "QP", "QN")
+COLS = ("QF", "PM", "QM1", "QP1", "QM2", "G16", "G15", "BY", "BX", "NZ15", "B15", "MB", "GE2", "WCOL", "NZ0", "A4",
+        "T0", "T1", "T2", "M0", "M1", "M2", "M3", "L2", "C3", "CL", "PB", "CJ0", "CJ")
 SCRATCH = {
     "XB": ("sbuf", [128, S + V], BF), "Y": ("sbuf", [128, V], BF), "mk": ("sbuf", [128, V], BF),
-    "trk": ("sbuf", [128, 64], I32), "cnd": ("sbuf", [128, 1024], I32),
-    "bin": ("sbuf", [128, 16 * RO], BF), "bout": ("sbuf", [128, 16 * RO], BF),
-    "vin": ("sbuf", [128, S * RO], BF), "vout": ("sbuf", [128, S * RO], BF),
-    "cmp": ("sbuf", [128, K * S], BF), "xg": ("sbuf", [128, 512 * 4], BF),
-    "eq": ("sbuf", [128, 16 * S], BF), "ab": ("sbuf", [128, S], BF),
+    "trk": ("sbuf", [128, 64], I32), "cnd": ("sbuf", [128, 1024], I32), "p16": ("sbuf", [128, 1024], F16),
+    "fin": ("sbuf", [128, S], BF), "fout": ("sbuf", [128, S], BF),
+    "ain": ("sbuf", [128, S * RO], BF), "aout": ("sbuf", [128, S * RO], BF),
+    "uin": ("sbuf", [128, 6 * S * RO], BF), "uout": ("sbuf", [128, 7 * S * RO], BF),
+    "vin": ("sbuf", [128, S * RO], BF), "vout": ("sbuf", [128, VP * RO], BF),
+    "lin": ("sbuf", [128, S * RO], BF), "lout": ("sbuf", [128, S * RO], BF),
+    "jin": ("sbuf", [128, 48], U16), "jout": ("sbuf", [128, 48], U16),
+    "cmp": ("sbuf", [128, K * S], BF), "xg": ("sbuf", [128, 512 * 3], BF), "eq": ("sbuf", [128, 16 * S], BF),
     "iq": ("sbuf", [128, 8], I32), "ix": ("sbuf", [128, 144], BF), "ig": ("sbuf", [128, 128], BF),
-    "ia": ("sbuf", [128, S], F32), "kc": ("sbuf", [128, S], BF), "i16": ("sbuf", [128, 16], F32),
-    "LE": ("sbuf", [128, 2048], BF), "LD": ("sbuf", [128, 2048], BF),
-    "cols": ("sbuf", [128, 64], F32), "pmi": ("sbuf", [128, 8], I32),
-    "BW": ("sbuf", [128, 144], BF), "BU": ("sbuf", [128, 144], BF), "BN": ("sbuf", [128, 144], BF),
-    "mats": ("sbuf", [128, 128 * 16], BF), "msk": ("sbuf", [128, S], BF), "rep": ("sbuf", [128, 16], U16),
-    "uf": ("sbuf", [128, 80], F32), "um": ("sbuf", [128, 80], F32), "su": ("sbuf", [128, 80], U16),
-    "uu": ("sbuf", [128, 64], U16),
-    "b97": ("sbuf", [128, 16], F32), "s32": ("sbuf", [128, S], I32), "c32": ("sbuf", [128, S], I32),
-    "cu": ("sbuf", [128, S], U16), "c16": ("sbuf", [128, S], F16),
-    "brow": ("sbuf", [128, 2 * S], BF), "nk": ("sbuf", [128, 64], BF),
+    "ia": ("sbuf", [128, S], BF), "kc": ("sbuf", [128, S], BF), "i16": ("sbuf", [128, 16], F32),
+    "jr": ("sbuf", [128, S], BF), "i4": ("sbuf", [128, 64], BF), "r4": ("sbuf", [128, 4], F32),
+    "iv": ("sbuf", [128, 144], BF),
+    "cols": ("sbuf", [128, 4 * len(COLS)], F32), "pmi": ("sbuf", [128, 16], I32),
+    "mats": ("sbuf", [128, 128 * len(MATS)], BF), "wraps": ("sbuf", [128, 144 * len(WRAPS)], BF),
+    "mlt": ("sbuf", [128, S], BF), "meq": ("sbuf", [128, S], BF), "msk": ("sbuf", [128, S], BF),
+    "m4": ("sbuf", [128, 64], F32), "mn": ("sbuf", [128, 64], BF), "mb": ("sbuf", [128, 64], F32),
+    "rst": ("sbuf", [128, 64], F32), "rep": ("sbuf", [128, 8], U16), "uf": ("sbuf", [128, 64], F32),
+    "su": ("sbuf", [128, 80], U16), "uu": ("sbuf", [128, 48], U16), "uw": ("sbuf", [128, 256], F16),
+    "TG": ("sbuf", [128, 2 * R + S], BF), "tv": ("sbuf", [128, 2 * S], BF), "tg": ("sbuf", [128, 2 * S], BF),
+    "so": ("sbuf", [128, 64], F32), "s0": ("sbuf", [128, 80], U16),
+    "rr": ("sbuf", [128, S], BF), "bw": ("sbuf", [128, 16], BF), "b4": ("sbuf", [128, 64], BF),
+    "qq": ("sbuf", [128, S], BF), "cu": ("sbuf", [128, S], U16), "c16": ("sbuf", [128, S], F16),
+    "sc": ("sbuf", [128, 128], F32),
     "tr": ("sbuf", [128, 320], F32), "ki": ("sbuf", [128, 32], I32),
-    "dz16": ("sbuf", [128, 16], F16), "dzf": ("sbuf", [128, 16], F32), "du": ("sbuf", [128, 96], F32),
-    "row": ("sbuf", [128, S], F16), "nok": ("sbuf", [128, S], BF), "LB": ("sbuf", [128, 2 * S], BF),
-    "ne": ("sbuf", [128, S], BF), "colg": ("sbuf", [128, S], BF), "tl": ("sbuf", [128, 2 * S], BF),
-    "cm": ("sbuf", [128, 48], F32), "tmp": ("sbuf", [128, S], BF), "tmp2": ("sbuf", [128, S], BF),
-    "keep": ("sbuf", [128, S], BF), "cY": ("sbuf", [128, S], BF), "cX": ("sbuf", [128, S], BF),
-    "nes": ("sbuf", [128, S], BF), "dS": ("sbuf", [128, S], BF),
-    "cU": ("sbuf", [128, S], BF), "neU": ("sbuf", [128, S], BF), "tlU": ("sbuf", [128, 4 * S], BF),
-    "cuw": ("sbuf", [128, 32], F32), "abw": ("sbuf", [128, 96], F32), "th": ("sbuf", [128, 2 * S], BF),
+    "dz": ("sbuf", [128, 64], F32), "dm": ("sbuf", [128, 128], F16),
+    "row": ("sbuf", [128, S], F16), "ab": ("sbuf", [128, S], BF),
+    "ne": ("sbuf", [128, S], BF), "colg": ("sbuf", [128, S], BF), "tmp": ("sbuf", [128, S], BF),
+    "tmp2": ("sbuf", [128, S], BF), "nes": ("sbuf", [128, S], BF), "nn": ("sbuf", [128, S], BF),
+    "cY": ("sbuf", [128, 2 * S], BF), "cU": ("sbuf", [128, S], BF), "neU": ("sbuf", [128, S], BF),
+    "ge": ("sbuf", [128, VP], BF), "gj": ("sbuf", [128, S], BF),
 }
-BANKS = ("EXP", "DG", "KA", "KB", "ZA", "ZB", "CNT", "WR")
+BANKS = tuple("B%d" % i for i in range(8))
 for _b in BANKS:
     SCRATCH[_b] = ("psum", [128, 512], F32)
 QUEUES = ("v", "s", "p", "g", "y")
-SEMAPHORES = (["q_" + q for q in QUEUES] + ["ask%d" % t for t in range(RO)] + ["ver%d" % t for t in range(RO)]
-              + ["sent"] + ["dma%d" % i for i in range(16)])
+SEMAPHORES = (["q_" + q for q in QUEUES] + [m + str(t) for m in ("ask", "ver", "sel", "opt", "tag") for t in range(RO)]
+              + ["top", "sent"] + ["dma%d" % i for i in range(16)])
 
 A = AluOpType
 F = ActivationFunctionType
@@ -67,6 +81,10 @@ def rank_program(g, core, T, topo):
             b = SCRATCH[name][1][1]
         p = T[name][:, a:b] if st == 1 else T[name][:, a:b:st]
         return (p, [(name, a, b)])
+
+    def blk(name, t, w=S, stride=None, off=0):
+        a = t * (stride or w) + off
+        return ap(name, a, a + w)
 
     def ind(win, off):
         return (win[0].indirect(off[0]), win[1] + off[1], win[1], off[1])
@@ -99,6 +117,10 @@ def rank_program(g, core, T, topo):
         else:
             add("v", lambda: g.vector.tensor_scalar(o[0], a[0], val(s1), val(s2), op0, op1), [a, s1, s2], o)
 
+    def vmax4(o, i):
+        rst = ap("rst")
+        add("v", lambda: g.vector.tensor_tensor_scan(o[0], rst[0], i[0], 0.0, A.add, A.max), [rst, i], o)
+
     def vset(o, c):
         add("v", lambda: g.vector.memset(o[0], c), [], o)
 
@@ -115,7 +137,7 @@ def rank_program(g, core, T, topo):
 
     def mms(o, terms, start=True, stop=True):
         for j, (l, r) in enumerate(terms):
-            mm(o, l, r, start and j == 0, stop and j == len(terms) - 1)
+            mm(o, m[l], r, start and j == 0, stop and j == len(terms) - 1)
 
     def iota(o, pattern, base, cm, small=True):
         if small:
@@ -131,293 +153,457 @@ def rank_program(g, core, T, topo):
     def hbm(t, a, b):
         return (t[:, a:b], [])
 
-    def emask(dst):
-        m = 0
-        for e in topo.engines(core, dst)[:ENGINES]:
-            m |= 1 << e
-        return m
+    def send(*writes):
+        k = ENGINES // len(writes)
+        trs = []
+        for j, (step, o, i, sem) in enumerate(writes):
+            dst = T.cores[(rank + step) % n]
+            rid, pid, _ = topo.addr(dst)
+            mask = sum(1 << e for e in topo.engines(core, dst)[j * k:(j + 1) * k])
+            trs.append((o[0], i[0], T.sem[sem], pid, rid, mask))
+        if len(trs) == 1:
+            o, i, sem, pid, rid, mask = trs[0]
+            emit = lambda: g.remote_dma(o, i, sem, T.sem.sent, pid, rid, mask)
+        else:
+            emit = lambda: g.remote_dma_fused(
+                [RemoteDMATransfer(dst_ids=[DstId(rid=rid, pnc=pid)], dma_engine_mask=mask, remote_sem=sem, src=i, dst=o)
+                 for (o, i, sem, pid, rid, mask) in trs], local_sem=T.sem.sent)
+        add("g", emit, [w[2] for w in writes], None, "r")
 
-    def send(dst, o, i, sem):
-        rid, pid, _ = topo.addr(dst)
-        add("g", lambda: g.remote_dma(o[0], i[0], T.sem[sem], T.sem.sent, pid, rid, emask(dst)), [i], None, "r")
+    def arrives(o, sem, writes=1):
+        add(None, ENGINES // writes, [], o, "a", sem)
 
-    def arrives(o, sem):
-        add(None, None, [], o, "a", sem)
+    c = {k: ap("cols", 4 * j, 4 * j + 1) for j, k in enumerate(COLS)}
+    m = {k: ap("mats", 128 * j, 128 * (j + 1)) for j, k in enumerate(MATS)}
+    wr = {k: ap("wraps", 144 * j, 144 * (j + 1)) for j, k in enumerate(WRAPS)}
 
-    def col(j):
-        return ap("cols", j, j + 1)
+    def shift(name, a, top=15):
+        j = 144 * WRAPS.index(name) + top - a
+        return ap("wraps", j, j + 128)
 
-    def mat(j):
-        return ap("mats", 128 * j, 128 * (j + 1))
-    ID, NID, I256, I8K, GG, NG, D0, EMP, EMN, ZERO, T1, D1, U0, T2 = [mat(j) for j in range(14)]
-    (PM, QF, G16, G15, QM1, QP1, NZ0, NZ15, WCOL, B15, BY, BX, MB, QM2, GE2) = [col(4 * j) for j in range(15)]
-
-    def wrap(o, bname, src, a0, a1, start, stop):
-        for a in range(16):
-            mm(o, ap(bname, 15 - a, 143 - a), ap(src, a0 + a, a1, 16), start and a == 0, stop and a == 15)
-
-    def expand(bank, lname, src, alone, stop=True):
-        for a in range(16):
-            mm(ap(bank, a, S, 16), ap(lname, 128 * a, 128 * (a + 1)), src, alone, alone or (stop and a == 15))
+    def wrap(o, name, src, start, stop, parts=16):
+        buf, a0, a1 = src[1][0]
+        for a in range(parts):
+            mm(o, shift(name, a, parts - 1), ap(buf, a0 + a, a1, parts), start and a == 0, stop and a == parts - 1)
 
     X = ap("XB", S, S + V)
     Y = ap("Y")
-
-    dma("s", ap("trk"), hbm(T.trucks, 0, 64))
-    dma("y", ap("XB", S, S + EARLY * CH), hbm(T.days, 0, EARLY * CH))
-    dma("y", ap("XB", S + EARLY * CH, S + V), hbm(T.days, EARLY * CH, V))
-    dma("y", ap("cnd"), hbm(T.cand, 0, 1024))
-
-    iota(ap("iq", 0, 1), [[0, 1]], 0, 1, small=False)
-    iota(ap("ix"), [[1, 144]], 0, 0)
-    iota(ap("ig"), [[16, 8], [0, 16]], 0, 0)
-    iota(ap("ia"), [[0, 16], [1, 16]], 0, 0)
-    iota(ap("i16"), [[16, 16]], 0, 0)
-    iota(ap("kc"), [[4096, 16], [0, 16]], 2048, 0)
-    vset(ZERO, 0.0)
-    vset(ap("XB", 0, S), 0.0)
-    vts(ap("pmi", 0, 1), ap("iq", 0, 1), 15, A.bitwise_and)
-    vcopy(QF, ap("iq", 0, 1))
-    vcopy(PM, ap("pmi", 0, 1))
-    vts(QM1, QF, -1.0, A.add)
-    vts(QP1, QF, 1.0, A.add)
-    vts(QM2, QF, -2.0, A.add)
-    vtt(G16, QF, PM, A.subtract)
-    vts(BX, PM, 0.0, A.not_equal, -256.0, A.mult)
-    vts(BY, PM, 0.0, A.not_equal, 256.0, A.mult)
-    vts(NZ15, PM, 15.0, A.not_equal)
-    vts(B15, PM, 15.0, A.is_equal, 256.0, A.mult)
-    vts(MB, PM, 0.5, A.add, 256.0, A.mult)
-    vts(GE2, PM, 2.0, A.is_ge, 256.0, A.mult)
-    vts(G15, G16, 15.0, A.add)
-    vts(WCOL, B15, 3840.0, A.mult, 65536.0, A.add)
-    vts(NZ0, NZ15, 256.0, A.mult)
-    ix = ap("ix", 0, 128)
-    vts(ID, ix, QF, A.is_equal)
-    vts(NID, ix, QF, A.is_equal, -1.0, A.mult)
-    vts(I256, ix, QF, A.is_equal, 256.0, A.mult)
-    vts(U0, ix, QM1, A.is_equal, BY, A.mult)
-    vts(GG, ap("ig"), G16, A.is_equal)
-    vts(ap("BU"), ap("ix"), G15, A.is_equal)
-    vts(ap("BN"), ap("ix"), G15, A.is_equal, -0.0625, A.mult)
-    vts(ap("BW"), ap("ix"), G15, A.is_equal, WCOL, A.mult)
-    vtt(D0, I256, U0, A.subtract)
-    act(ap("msk"), ap("ia"), F.Sigmoid, bias=MB, scale=-256.0)
-    vts(I8K, ix, QF, A.is_equal, 8192.0, A.mult)
-    vts(NG, ap("ig"), G16, A.is_equal, -1.0, A.mult)
-    vts(T1, ix, QP1, A.is_equal, NZ0, A.mult)
-    vts(T2, ix, QM2, A.is_equal, GE2, A.mult)
-    vts(ap("rep"), ap("ia", 0, 16), 0.0, A.mult, PM, A.add)
-    vtt(EMP, T1, I256, A.subtract)
-    vtt(EMN, I256, T1, A.subtract)
-    vtt(D1, U0, T2, A.subtract)
-    for a in range(16):
-        vts(ap("LE", 128 * a, 128 * (a + 1)), ap("ig"), float(a), A.add, QF, A.is_equal)
-    vcopy(ap("su", 0, 16), ap("trk", 0, 16))
-
-    conv_banks = ("ZA", "ZB", "KA", "KB")
-
-    def mask_chunk(c):
-        vts(ap("mk", c * CH, (c + 1) * CH), ap("XB", S + c * CH, S + (c + 1) * CH), 0.0, A.is_equal, 256.0, A.mult)
-
-    def conv(h):
-        bank = ap(conv_banks[h % 4])
-        mms(bank, [(ID, ap("XB", S + 512 * h, S + 512 * (h + 1))), (ID, ap("mk", 512 * h, 512 * (h + 1)))])
-        act(ap("Y", 512 * h, 512 * (h + 1)), bank, F.Copy)
-
-    def late_constants():
-        vcopy(ap("uf", 0, 64), ap("trk"))
-        vcopy(ap("uu"), ap("trk"))
-        vts(ap("uf", 64, 80), ap("i16"), PM, A.add)
-        vts(ap("um", 0, 64), ap("uf", 0, 64), -2048.0, A.add)
-        vts(ap("um", 64, 80), ap("uf", 64, 80), -2048.0 - S, A.add)
-        for a in range(16):
-            vtt(ap("LD", 128 * a, 128 * (a + 1)), ap("LE", 128 * a, 128 * (a + 1)), ID, A.subtract)
-
-    for c in range(EARLY):
-        mask_chunk(c)
-        conv(2 * c)
-        conv(2 * c + 1)
+    ne, colg, tmp, tmp2, nes = ap("ne"), ap("colg"), ap("tmp"), ap("tmp2"), ap("nes")
+    rep4 = ap("rep", 4, 8)
 
     def su(t):
-        return ap("su", 16 * t, 16 * (t + 1))
-    land_neg, landb_neg = ap("LB", 0, S), ap("LB", S, 2 * S)
-    ne, colg, tv, lt = ap("ne"), ap("colg"), ap("tl", 0, S), ap("tl", S, 2 * S)
+        return blk("su", t, 16)
 
-    def send_ask(t):
-        send(T.cores[(rank + STEP[t]) % n], ap("bin", 16 * t, 16 * (t + 1)), ap("bout", 16 * t, 16 * (t + 1)), "ask%d" % t)
+    def uu(t):
+        return blk("uu", t - 1, 16)
+
+    def go(t):
+        return blk("vout", t, S, VP)
+
+    def land(t):
+        return blk("lout", t)
+
+    def uo(t, j, w=1):
+        return blk("uout", t, w * S, 7 * S, j * S)
+
+    def ui(t, j, w=1):
+        return blk("uin", t, w * S, 6 * S, (j - 1) * S)
+
+    def brow(t, w=S):
+        return uo(t, 0, w // S)
+
+    def cY(t):
+        return blk("cY", t % 2)
+
+    dma("s", ap("trk"), hbm(T.trucks, 0, 64))
+    for k in range(NCH):
+        dma("y", blk("XB", k, CH, CH, S), hbm(T.days, k * CH, (k + 1) * CH))
+    dma("y", blk("cnd", 0), hbm(T.cand, 0, S))
+    dma("y", ap("cnd", S, RO * S), hbm(T.cand, S, RO * S))
+
+    iota(ap("iq", 0, 1), [[0, 1]], 0, 1, small=False)
+    iota(ap("i16"), [[16, 16]], 0, 0)
+    iota(ap("ix"), [[1, 144]], 0, 0)
+    iota(ap("jr"), [[-1, S]], S, 0)
+    iota(ap("ia"), [[0, 16], [1, 16]], 0, 0)
+    iota(ap("ig"), [[16, 8], [0, 16]], 0, 0)
+    iota(ap("i4"), [[0, 16], [1, 4]], 0, 0)
+    iota(ap("r4"), [[4, 4]], 0, 0)
+    iota(ap("iv"), [[16, 9], [0, 4], [-1024, 4]], 3072, 0)
+    iota(ap("kc"), [[4096, 16], [0, 16]], 2048, 0)
+    pm, p1, m3, a4 = [ap("pmi", 4 * j, 4 * j + 1) for j in range(4)]
+    ix, ig = ap("ix", 0, 128), ap("ig")
+    vset(ap("TG"), 0.0)
+    vts(pm, ap("iq", 0, 1), 15, A.bitwise_and)
+    vcopy(c["QF"], ap("iq", 0, 1))
+    vts(p1, ap("iq", 0, 1), 1, A.bitwise_and)
+    vcopy(c["PM"], pm)
+    vts(m3, ap("iq", 0, 1), 3, A.bitwise_and)
+    vts(c["MB"], pm, -0.5, A.add, 256.0, A.mult)
+    for t in range(3):
+        vts(c["T%d" % t], pm, float(t), A.is_equal)
+    vtt(c["G16"], c["QF"], c["PM"], A.subtract)
+    vts(m["ID"], ix, c["QF"], A.is_equal)
+    vts(ap("so", 0, 16), ap("i16"), c["PM"], A.add, float(V), A.add)
+    vts(c["G15"], c["G16"], 15.0, A.add)
+    act(ap("mlt"), ap("ia"), F.Sigmoid, bias=c["MB"], scale=-256.0)
+
+    def tag_put(t, k):
+        for j in range(k):
+            vts(blk("tv", j), ap("jr"), c["T%d" % t], A.mult)
+        vcopy(ind(ap("TG"), uu(t) if t else ap("s0", 0, 32)), ap("tv", 0, k * S))
+
+    def tag_get(t, k, bank):
+        act(ap("tg", 0, k * S), ind(ap("TG"), uu(t + 1) if t else ap("s0", 32, 64)), F.Identity, scale=c["T%d" % t])
+        wrap(ap(bank, 0, 16 * k), "BU", ap("tg", 0, k * S), True, True)
+
+    def tag_out(t, k, bank):
+        vts(ap("jout", 16 * t, 16 * (t + k)), ap(bank, 0, 16 * k), -1.0, A.mult, float(S), A.add)
+        send((STEP[t], ap("jin", 16 * t, 16 * (t + k)), ap("jout", 16 * t, 16 * (t + k)), "tag%d" % t))
+
+    vts(ap("so", 16, 32), ap("trk", 0, 16), float(W), A.is_lt, BIG, A.mult)
+    vts(ap("uu"), ap("trk", 16, 64), -float(W), A.add)
+    vtt(ap("so", 32, 48), ap("so", 16, 32), ap("trk", 0, 16), A.add)
+    vts(wr["BU"], ap("ix"), c["G15"], A.is_equal)
+    vtt(ap("so", 48, 64), ap("so", 32, 48), ap("so", 0, 16), A.min)
+    vcopy(su(0), ap("trk", 0, 16))
+    vts(ap("s0", 0, 16), ap("so", 48, 64), -float(W), A.add)
+    for j, (b, o) in enumerate(((1, R + S), (1, 0), (2, R + S))):
+        vts(blk("s0", j + 1, 16), blk("trk", b, 16), float(o - W), A.add)
+    tag_put(0, 2)
+    tag_get(0, 2, "B7")
+
+    def constants_0():
+        vts(c["QM1"], c["QF"], -1.0, A.add)
+        vts(c["BY"], pm, 0.0, A.not_equal, 256.0, A.mult)
+        vts(m["I256"], ix, c["QF"], A.is_equal, 256.0, A.mult)
+        vts(m["U0"], ix, c["QM1"], A.is_equal, c["BY"], A.mult)
+        vts(m["GG"], ig, c["G16"], A.is_equal)
+        vts(m["NID"], ix, c["QF"], A.is_equal, -1.0, A.mult)
+        vtt(m["D0"], m["I256"], m["U0"], A.subtract)
+
+    conv_banks = ("B0", "B1", "B2", "B3")
+
+    def mask_chunk(k):
+        vts(blk("mk", k, CH), blk("XB", k, CH, CH, S), 0.0, A.is_equal, 256.0, A.mult)
+
+    def conv(k):
+        for h in (2 * k, 2 * k + 1):
+            bank = ap(conv_banks[h % 4])
+            mms(bank, [("ID", blk("XB", h, 512, 512, S)), ("ID", blk("mk", h, 512))])
+            act(blk("Y", h, 512), bank, F.Copy)
+
+    def constants_a():
+        vts(a4, pm, 2, A.arith_shift_right)
+        vts(c["QP1"], c["QF"], 1.0, A.add)
+        vts(c["QM2"], c["QF"], -2.0, A.add)
+        vts(c["NZ15"], pm, 15.0, A.not_equal)
+        vts(c["B15"], pm, 15.0, A.is_equal, 256.0, A.mult)
+        vts(c["GE2"], pm, 2.0, A.is_ge, 256.0, A.mult)
+        vcopy(c["A4"], a4)
+        vts(c["NZ0"], c["NZ15"], 256.0, A.mult)
+        vts(c["WCOL"], c["B15"], 3840.0, A.mult, 65536.0, A.add)
+        vts(c["BX"], c["BY"], -1.0, A.mult, -256.0, A.add)
+        vts(ap("rep", 0, 4), ap("r4"), 0.0, A.mult, c["PM"], A.add)
+        vts(rep4, ap("r4"), c["A4"], A.add)
+        vts(m["I97"], ix, c["QF"], A.is_equal, float(M), A.mult)
+        vts(m["N4K"], ix, c["QF"], A.is_equal, -float(W), A.mult)
+        vts(wr["BW"], ap("ix"), c["G15"], A.is_equal, c["WCOL"], A.mult)
+        vts(m["I8K"], ix, c["QF"], A.is_equal, BIG, A.mult)
+        vts(m["NG"], ig, c["G16"], A.is_equal, -1.0, A.mult)
+        vts(c["QM2"], c["QF"], -2.0, A.add)
+        vts(m["T2"], ix, c["QM2"], A.is_equal, c["GE2"], A.mult)
+        vts(ap("meq"), ap("ia"), c["PM"], A.is_equal, -0.25, A.mult)
+        vtt(m["D1"], m["U0"], m["T2"], A.subtract)
+
+    def constants_b():
+        vtt(ap("msk"), ap("mlt"), ap("meq"), A.add)
+        for s in range(4):
+            vts(c["M%d" % s], m3, float(s), A.is_equal)
+        vtt(m["GI"], m["GG"], m["ID"], A.add)
+        vts(ap("m4"), ap("i4"), c["A4"], A.is_equal)
+        vts(ap("mn"), ap("i4"), c["A4"], A.not_equal, -2.0, A.mult)
+        vts(ap("mb"), ap("i4"), c["A4"], A.not_equal, -2 * BIG, A.mult)
+        vts(ap("rst"), ap("i4"), 0.0, A.is_equal, -8 * BIG, A.mult)
+        vts(ap("uf", 0, 48), ap("trk", 16, 64), -float(W), A.add)
+        vts(ap("uf", 48, 64), ap("so", 0, 16), -1.0, A.mult, float(V), A.add)
+        for s in range(4):
+            vts(m["E%d" % s], m["GG"], c["M%d" % s], A.mult)
+            vts(m["F%d" % s], m["GI"], c["M%d" % s], A.mult)
+        vts(wr["QP"], ap("iv"), c["G16"], A.is_equal, BIG / 16, A.mult)
+        vts(wr["QN"], ap("iv"), c["G16"], A.is_equal, -BIG / 16, A.mult)
+        vts(m["ND0"], m["D0"], -1.0, A.mult)
+        vts(m["DG0"], ix, c["QF"], A.is_equal, c["T0"], A.mult)
+
+    def constants_c():
+        vts(m["T1"], ix, c["QP1"], A.is_equal, c["NZ0"], A.mult)
+        vts(m["N256"], ix, c["QF"], A.is_equal, -256.0, A.mult)
+        vts(c["L2"], pm, 2.0, A.is_le)
+        vts(c["C3"], pm, 3.0, A.is_ge)
+        vts(c["CL"], c["T0"], 2 * BIG, A.mult, -BIG, A.add)
+        vts(c["PB"], p1, BIG, A.mult, -BIG, A.add)
+        vts(c["CJ0"], p1, -2 * BIG / 256, A.mult, BIG / 256, A.add)
+        vtt(m["EMN"], m["I256"], m["T1"], A.subtract)
+        vtt(c["CJ"], c["CJ0"], c["BY"], A.mult)
+        vts(m["LE0"], ig, c["QF"], A.is_equal)
+        vts(m["DL"], ix, c["QF"], A.is_equal, c["CL"], A.mult)
+        vts(m["DJ"], ix, c["QF"], A.is_equal, c["CJ"], A.mult)
+        vts(m["G012"], ig, c["G16"], A.is_equal, c["L2"], A.mult)
+        vts(m["G34"], ig, c["G16"], A.is_equal, c["C3"], A.mult)
+        vts(wr["B012"], ap("ix"), c["G15"], A.is_equal, c["L2"], A.mult)
+        for t in range(RO):
+            vtt(blk("uw", t, 64), ind(blk("uf", t, 16), rep4), ap("mb"), A.add)
+        vset(ap("ge", S, VP), 0.0)
+        vset(ap("vout", S, VP), 0.0)
+        vts(m["NDL"], m["DL"], -1.0, A.mult)
+
+    def constants_d():
+        vts(m["EMP"], m["EMN"], -1.0, A.mult)
+        vts(m["IH"], ix, c["QF"], A.is_equal, 0.5, A.mult)
+        vset(ap("XB", 0, S), 0.0)
+
+    def p_half(t):
+        vts(blk("p16", t), blk("cnd", t), -2048.0, A.add)
 
     def first_ask():
-        vts(ne, ind(X, su(0)), 0.0, A.is_gt)
         act(colg, ind(X, su(0)), F.Copy)
-        z, z2 = ap("DG", 0, S), ap("CNT", 0, S)
-        mms(z, [(ID, colg), (D0, ne)])
-        mms(z2, [(NID, colg), (I256, ne)], True, False)
-        vts(tv, z, -256.0, A.add, 0.0, A.max)
-        mm(z2, GG, tv, False, True)
-        vts(lt, z2, 256.0, A.is_gt)
-        wrap(ap("WR", 32, 64), "BU", "tl", 0, 2 * S, True, True)
-        vts(ap("cm", 0, 16), ap("WR", 48, 64), 256.0, A.mult)
-        vtt(ap("bout", 0, 16), ap("WR", 32, 48), ap("cm", 0, 16), A.min)
-        send_ask(0)
+        act(ne, colg, F.Sign)
+        mms(ap("B4", 0, S), [("ID", colg), ("D0", ne)])
+        mms(ap("B5", 0, S), [("NID", colg), ("I256", ne)], True, False)
+        act(ap("fout"), ap("B4", 0, S), F.Relu, bias=-256.0)
+        send((STEP[0], ap("fin"), ap("fout"), "top"))
+        mms(ap("B5", 0, S), [("GG", ap("fout"))], False, True)
+        act(blk("aout", 0), ap("B5", 0, S), F.Relu, bias=-256.0)
+        send((STEP[0], blk("ain", 0), blk("aout", 0), "ask0"))
 
-    def next_ask(t):
-        vtt(lt, ind(Y, su(t)), ap("th", S, 2 * S), A.is_le)
-        act(colg, ind(Y, su(t)), F.Copy)
-        act(ne, colg, F.Sign, bias=256.0, scale=-1.0)
-        wrap(ap("WR", 32, 48), "BU", "tl", S, 2 * S, True, True)
-        vts(ap("cm", 0, 16), ap("WR", 32, 48), 1.0, A.min)
-        vtt(ap("cm", 16, 32), ap("cm", 0, 16), ap("abw", 64, 80), A.mult)
-        vtt(ap("bout", 16 * t, 16 * (t + 1)), ap("cm", 16, 32), ap("abw", 80, 96), A.add)
-        send_ask(t)
+    s1, s2 = ap("B3", 0, S), ap("B7", 0, S)
+    na = 16 * KLAST
+    kb = ap("B4", 0, S - na)
+    cU, neU = ap("cU"), ap("neU")
 
-    def x_follow(t):
-        vtt(ind(X, su(t)), ap("cX"), ap("keep"), A.mult)
+    def preload(t):
+        mms(s1, [("ID", blk("p16", t))], True, False)
+        mms(s2, [("ID", blk("p16", t))], True, False)
 
-    def main(t):
-        last = t == RO - 1
-        b = ap("bin", 16 * t, 16 * (t + 1))
-        arrives(b, "ask%d" % t)
-        ex = ap("EXP", 0, S)
-        vts(ap("b97"), b, float(M), A.mult)
-        expand("EXP", "LE", b, True)
-        act(ap("nk"), ind(b, ap("rep", 0, 4)), F.Relu, bias=1048576.0, scale=-1048576.0)
-        act(ap("brow", 0, S), ex, F.Identity, bias=B15, scale=NZ15)
-        act(ap("brow", S, 2 * S), ex, F.Identity, bias=B15, scale=NZ15)
-        vtt(ap("s32"), ind(ap("b97"), ap("rep")), ap("cnd", S * t, S * (t + 1)), A.add)
-        vts(ap("c32"), ap("s32"), W - 1, A.bitwise_and)
-        vcopy(ap("cu"), ap("c32"))
+    def day_a(t):
+        if t == 0:
+            src = ap("fin")
+            arrives(src, "top")
+        else:
+            src = ap("rr")
+            arrives(blk("lin", t - 1), "sel%d" % (t - 1), 2)
+            mms(ap("B0", 0, S), [("DL", blk("lin", t - 1))], False, True)
+            act(src, ap("B0", 0, S), F.Relu, bias=c["PB"])
+        wrap(ap("B0", 0, 16), "B012" if t else "BU", src, True, True)
+        mms(ap("B1", 0, S), [("G012" if t else "GG", src)])
+
+    def day_b(t):
+        act(ap("bw"), ap("B0", 0, 16), F.Copy)
+        act(ap("b4"), ind(ap("bw"), ap("rep", 0, 4)), F.Copy)
+        for bank in ("B3", "B7"):
+            for k in range(4):
+                mms(blk(bank, k, 64), [("I97", ap("b4"))], False, bank == "B3" and k == 3)
+        if t + 1 < RO:
+            act(neU, cU, F.Sign, bias=256.0, scale=-1.0)
+        act(ap("qq"), s1, F.Identity, bias=QB + 2.0 ** -13, scale=1.0 / W)
+        mms(s2, [("N4K", ap("qq"))], False, True)
+        for h in range(2):
+            act(uo(t, h), ap("B1", 0, S), F.Identity, bias=c["B15"], scale=c["NZ15"])
+        if t + 1 < RO:
+            mms(ap("B3", 0, S), [("ID", cU), ("D0", neU)])
+            mms(ap("B3", S, 2 * S), [("ID", cU), ("D1", neU)])
+
+    def score(t):
+        zb = ("B0", "B1", "B0")
+        vts(ap("cu"), s2, 2048.0 + W * QB, A.add)
         vts(ap("c16"), ap("cu"), -2048.0, A.add)
-        zb = ("ZA", "ZB")
-        cnt = ap("CNT", 0, S)
-        na = 16 * KLAST
-        mm(cnt, ZERO, ap("kc"), True, False)
-        expand("CNT", "LE", ap("nk", 0, 16), False, False)
-        mm(ap("DG", 0, S), I8K, ap("msk"), True, False)
-        mm(ap("KA", 0, na), ID, ap("kc", 0, na), True, False)
-        mm(ap("KB", 0, S - na), ID, ap("kc", na, S), True, False)
-        for c in range(0, na, 64):
-            mm(ap("KA", c, c + 64), ID, ap("nk"), False, False)
-        mm(ap("KB", 0, S - na), ID, ap("nk", 0, S - na), False, False)
-        mm(ap("KA", 0, na), ID, ap("c16", 0, na), False, False)
-        mm(ap("KB", 0, S - na), ID, ap("c16", na, S), False, False)
+        mms(ap("B2", 0, na), [("ID", ap("kc", 0, na))], True, False)
+        mms(kb, [("ID", ap("kc", na, S))], True, False)
+        for bank in zb[:2]:
+            mms(ap(bank), [("NID", brow(t, 2 * S))], True, False)
+        mms(ap("B2", 0, na), [("ID", ap("c16", 0, na))], False, False)
+        mms(kb, [("ID", ap("c16", na, S))], False, False)
         last_a = max(i for i, s in enumerate(SCHED) if s[0] == "key" and s[1] < KLAST)
         for i, s in enumerate(SCHED):
-            if s[0] == "sg":
-                act(ap("xg", 512 * s[1], 512 * (s[1] + 1)), ind(Y, ap("cu", 16 * s[2], 16 * s[2] + 32)), F.Copy)
+            if s[0] == "pre":
+                mms(ap(zb[s[1]]), [("NID", brow(t, 2 * S))], True, False)
+            elif s[0] == "old":
+                if t:
+                    mms(ap("B6", 0, S), [("ID", cY(t - 1)), ("ID", tmp)])
+            elif s[0] == "dg":
+                mms(ap("B5", 0, S), [("I8K", ap("msk"))], True, False)
+            elif s[0] == "sg":
+                act(blk("xg", s[1], 512), ind(Y, ap("cu", 16 * s[2], 16 * s[2] + 32)), F.Copy)
             elif s[0] == "z":
-                mms(ap(zb[s[1] % 2]), [(NID, ap("brow")), (ID, ap("xg", 512 * s[1], 512 * (s[1] + 1)))])
+                mms(ap(zb[s[1]]), [("ID", blk("xg", s[1], 512))], False, True)
             elif s[0] == "ss":
-                act(ap("cmp", S * s[2], S * (s[2] + 2)), ap(zb[s[1] % 2]), F.Sigmoid, bias=-128.0, scale=-256.0)
+                act(ap("cmp", S * s[2], S * (s[2] + 2)), ap(zb[s[1]]), F.Sigmoid, bias=-128.0, scale=-256.0)
             elif s[0] == "vg":
-                vtt(ap("cmp", S * s[1], S * (s[1] + 2)), ind(Y, ap("cu", 16 * s[1], 16 * s[1] + 32)), ap("brow"), A.is_lt)
+                vtt(ap("cmp", S * s[1], S * (s[1] + 2)), ind(Y, ap("cu", 16 * s[1], 16 * s[1] + 32)), brow(t, 2 * S), A.is_lt)
+            elif s[0] == "nk":
+                arrives(blk("ain", t), "ask%d" % t)
+                mms(ap("B6", S, 2 * S), [("GG", blk("ain", t))] + ([("G34", ap("rr"))] if t else []))
             elif s[1] < KLAST:
-                wrap(ap("KA", 16 * s[1], 16 * s[2]), "BW", "cmp", S * s[1], S * s[2], False, i == last_a)
+                wrap(ap("B2", 16 * s[1], 16 * s[2]), "BW", ap("cmp", S * s[1], S * s[2]), False, i == last_a)
             else:
-                wrap(ap("KB", 0, S - na), "BW", "cmp", S * s[1], S * s[2], False, True)
-        cU, neU = ap("cU"), ap("neU")
+                wrap(kb, "BW", ap("cmp", S * s[1], S * s[2]), False, True)
+
+    def reserve(t):
+        act(cU, ind(ap("Y", W, V), uu(t)), F.Copy)
+
+    def choose(t):
+        last = t == RO - 1
+        cnt, dg, wg, nw = ap("B1", 0, S), ap("B5", 0, S), ap("B7", 0, 64), ap("B0", 0, 64)
+        dzf, dzb, dzq = ap("dz", 0, 16), ap("dz", 16, 32), ap("dz", 32, 48)
+        nk = uo(t, 6)
+        act(nk, ap("B6", S, 2 * S), F.Relu, bias=1.0, scale=-1.0)
+        mms(nw, [("I8K", ap("mn"))], True, False)
+        wrap(nw, "QP", nk, False, True, 4)
+        mms(cnt, [("I8K", nk)], True, False)
         if not last:
-            act(cU, ind(Y, ap("uu", 16 * (t + 1), 16 * (t + 2))), F.Copy)
-            act(neU, cU, F.Sign, bias=256.0, scale=-1.0)
-            mms(ap("ZA", 0, S), [(ID, cU), (D0, neU)])
-            mms(ap("ZA", S, 2 * S), [(ID, cU), (D1, neU)])
-        act(ap("cY"), ind(Y, su(t)), F.Copy)
-        act(ap("nes"), ap("cY"), F.Sign, bias=256.0, scale=-1.0)
+            act(uo(t, 2, 2), ap("B3"), F.Relu, bias=-256.0)
+            mms(ap("B3", 0, S), [("NID", cU), ("GG", uo(t, 2))])
+            mms(ap("B3", S, 2 * S), [("NID", cU), ("ND0", neU), ("GG", uo(t, 3))])
+        act(cY(t), ind(Y, su(t)), F.Copy)
+        if t:
+            act(ap("nn"), ap("B6", 0, S), F.Sign, bias=256.0, scale=-1.0)
         if not last:
-            act(ap("tlU", 0, 2 * S), ap("ZA"), F.Relu, bias=-256.0)
-        vcopy(ap("tr", 0, 64), ap("KA", 0, 64))
-        vtt(ap("tr", 64, 128), ap("KA", 64, 128), ap("tr", 0, 64), A.min)
-        vtt(ap("tr", 128, 192), ap("KA", 128, 192), ap("tr", 64, 128), A.min)
-        vtt(ap("tr", 192, 256), ap("KB", 0, 64), ap("tr", 128, 192), A.min)
+            act(uo(t, 4, 2), ap("B3"), F.Relu)
+            send((STEP[t + 1], ui(t, 1, 6), uo(t, 1, 6), "opt%d" % t))
+        vcopy(ap("tr", 0, 64), ap("B2", 0, 64))
+        vtt(ap("tr", 64, 128), ap("B2", 64, 128), ap("tr", 0, 64), A.min)
+        vtt(ap("tr", 128, 192), ap("B2", 128, 192), ap("tr", 64, 128), A.min)
+        vtt(ap("tr", 192, 256), ap("B4", 0, 64), ap("tr", 128, 192), A.min)
         vtt(ap("tr", 256, 288), ap("tr", 192, 224), ap("tr", 224, 256), A.min)
         vtt(ap("ki", 0, 16), ap("tr", 256, 272), ap("tr", 272, 288), A.min)
-        vts(ap("ki", 16, 32), ap("ki", 0, 16), 0x300FFF, A.bitwise_and)
-        vts(ap("dz16"), ap("ki", 16, 32), 4096.0, A.min, -2048.0, A.add)
-        vts(ap("dzf"), ap("ki", 16, 32), 4096.0, A.min, -2048.0, A.add)
-        vtt(ap("du", 0, 16), ap("dzf"), ap("um", 16 * (t + 1), 16 * (t + 2)), A.subtract)
-        expand("KA", "LE", ap("dz16"), True)
-        expand("DG", "LD", ap("dz16"), False)
-        vcopy(ap("row"), ap("KA", 0, S))
-        act(ap("nok"), ap("KA", 0, S), F.Sign, bias=-2048.0)
-        act(ap("ab"), ap("DG", 0, S), F.Abs)
+        vts(ap("ki", 16, 32), ap("ki", 0, 16), 0x100FFF, A.bitwise_and)
+        vmax4(ap("sc", 0, 64), nw)
+        vts(dzf, ap("ki", 16, 32), float(W), A.min, -2048.0, A.add)
+        vtt(ap("dm", 0, 64), ind(dzf, rep4), ap("m4"), A.mult)
+        vtt(dzb, dzf, ap("sc", 3, 64, 4), A.subtract)
+        for s in range(4):
+            mm(ap("B2", s, S, 4), m["E%d" % s], ap("dm", 0, 64), True, True)
+        vcopy(ap("dm", 64, 128), ind(dzb, rep4))
+        for s in range(4):
+            mms(ap("B5", s, S, 4), [("F%d" % s, ap("dm", 0, 64))], False, False)
+        for s in range(4):
+            mms(ap("B5", s, S, 4), [("NID", ap("dm", 64, 128))], False, s == 3)
+        vcopy(ap("row"), ap("B2", 0, S))
+        act(ap("ab"), dg, F.Abs)
         ed = ap("eq", S * 15, S * 16)
         act(ed, ap("ab"), F.Relu, bias=1.0, scale=-1.0)
-        for m in range(15):
-            e = ap("eq", S * m + 16 * (m + 1), S * (m + 1))
-            vts(e, ap("row", 16 * (m + 1), S), ap("dzf", m, m + 1), A.is_equal)
-            if m == 13:
-                mm(cnt, NG, ed, False, False)
-            mm(ap("CNT", 16 * (m + 1), S), NG, e, False, m == 14)
-        vo = ap("vout", S * t, S * (t + 1))
-        vtt(vo, cnt, ap("nok"), A.is_gt)
-        send(T.cores[(rank - STEP[t]) % n], ap("vin", S * t, S * (t + 1)), vo, "ver%d" % t)
-        vtt(land_neg, vo, ap("nok"), A.mult)
-        if not last:
-            mms(ap("ZB", 0, S), [(NID, cU), (I256, neU), (GG, ap("tlU", 0, S))])
-            mms(ap("ZB", S, 2 * S), [(NID, cU), (U0, neU), (GG, ap("tlU", S, 2 * S))])
-            act(ap("tlU", 2 * S, 4 * S), ap("ZB"), F.Relu, bias=-256.0)
-        wrap(ap("WR", 0, 16), "BN", "LB", 0, S, True, True)
-        vtt(landb_neg, ex, land_neg, A.mult)
-        mms(ap("KA", 0, S), [(D0, ap("nes")), (NID, ap("cY"))])
-        act(ap("dS"), ap("KA", 0, S), F.Relu, scale=-1.0 if last else 1.0)
-        vtt(ap("du", 16, 32), ap("WR", 0, 16), ap("du", 0, 16), A.mult)
-        if not last:
-            vcopy(ap("du", 48, 64), ap("WR", 0, 16))
-        vtt(ap("du", 32, 48), ap("du", 16, 32), ap("uf", 16 * (t + 1), 16 * (t + 2)), A.add)
-        vcopy(su(t + 1), ap("du", 32, 48))
-        if not last:
-            wrap(ap("EXP", 0, 64), "BU", "tlU", 0, 4 * S, True, True)
-            mms(ap("DG", 0, S), [(ID, ap("tlU", 0, S)), (I256, land_neg)])
-            act(ap("th", 0, S), ap("DG", 0, S), F.Relu)
-            mms(ap("ZA", 0, S), [(NID, landb_neg), (ID, land_neg), (ID, ap("th", 0, S))])
-            act(ap("th", S, 2 * S), ap("ZA", 0, S), F.Copy)
-        mms(ap("ZB", 0, S), [(I256, ap("nes")), (ID, ap("cY"))])
-        act(ap("cX"), ap("ZB", 0, S), F.Identity, bias=-256.0)
-        if not last:
-            lw = ap("du", 48, 64)
-            vts(ap("cuw"), ap("EXP", 32, 64), 256.0, A.mult)
-            vtt(ap("abw", 0, 32), ap("EXP", 0, 32), ap("cuw"), A.min)
-            vtt(ap("abw", 32, 48), ap("abw", 0, 16), ap("abw", 16, 32), A.subtract)
-            vtt(ap("du", 64, 80), lw, ap("abw", 16, 32), A.mult)
-            vtt(ap("abw", 48, 64), b, ap("abw", 32, 48), A.subtract)
-            vtt(ap("abw", 80, 96), ap("abw", 16, 32), ap("du", 64, 80), A.subtract)
-            vtt(ap("du", 80, 96), lw, ap("abw", 48, 64), A.mult)
-            vtt(ap("abw", 64, 80), ap("du", 80, 96), ap("abw", 32, 48), A.add)
-
-    first_ask()
-    for c in range(EARLY, NCH):
-        mask_chunk(c)
-    for h in range(2 * EARLY, 2 * NCH):
-        conv(h)
-    late_constants()
-    for t in range(RO):
-        main(t)
-        v = ap("vin", S * t, S * (t + 1))
-        zl = ap("KB", 0, S)
-        if t < RO - 1:
-            mms(zl, [(NID, landb_neg), (I256, land_neg)], True, False)
-            arrives(v, "ver%d" % t)
-            vtt(ap("tmp"), v, ap("dS"), A.mult)
-            vtt(ind(Y, su(t)), ap("cY"), ap("tmp"), A.add)
-            next_ask(t + 1)
-            mm(zl, EMN, ne, False, True)
-            vts(ap("tmp2"), zl, BY, A.add, 0.0, A.min)
-            vtt(ind(Y, su(t + 1)), colg, ap("tmp2"), A.add)
-            vts(ap("keep"), ap("tmp"), 0.0, A.is_equal)
-            x_follow(t)
+        act(nes, cY(t), F.Sign, bias=256.0, scale=-1.0)
+        for j in range(15):
+            e = ap("eq", S * j + 16 * (j + 1), S * (j + 1))
+            vts(e, ap("row", 16 * (j + 1), S), ap("dz", 16 + j, 17 + j), A.is_equal)
+            if j == 13:
+                mms(cnt, [("NG", ed)], False, False)
+            mms(ap("B1", 16 * (j + 1), S), [("NG", e)], False, j == 14)
+        vts(go(t), cnt, -0.5, A.is_gt)
+        verdict = (-STEP[t], blk("vin", t), go(t), "ver%d" % t)
+        if last:
+            send(verdict)
         else:
-            mm(zl, NID, landb_neg, True, False)
-            arrives(v, "ver%d" % t)
-            vtt(ap("keep"), v, ap("dS"), A.is_le)
-            x_follow(t)
+            send(verdict, (STEP[t + 1], blk("lin", t), go(t), "sel%d" % t))
+        vts(land(t), cnt, 0.0, A.is_equal)
+        if not last:
+            if t:
+                mms(ap("B6", 0, S), [("NID", blk("lin", t - 1)), ("ID", ui(t - 1, 6)), ("ID", go(t))])
+                act(ap("ge", 0, S), ap("B6", 0, S), F.Relu)
+            mms(ap("B5", S, 2 * S), [("D0", nes), ("NID", cY(t))])
+            if t != 1:
+                arrives(ap("jin", 16 * t, 32 + 8 * t), "tag%d" % t)
+            act(ap("gj"), ind(ap("ge") if t else ap("vout", 0, VP), blk("jin", t, 16)), F.Copy)
+            act(dg, ap("B5", S, 2 * S), F.Relu)
+            if t == 1:
+                tag_get(2, 1, "B2")
+        else:
+            mms(dg, [("U0", nes), ("IH", nes)])
+        if t:
+            vtt(ind(X, su(t - 1)), cY(t - 1), ap("nn"), A.mult)
+        if t in (1, 2):
+            p_half(t + 1)
+        if t == 2:
+            constants_d()
+        mms(wg, [("ID", blk("uw", t, 64))], True, False)
+        wrap(wg, "QN", land(t), False, True, 4)
+        mms(ap("B4", 0, S), [("LE0", brow(t)), ("I256" if last else "N256", land(t))], True, False)
+        if last:
+            vts(dzq, dzf, -1.0, A.mult, -2048.0 - S, A.add)
+        else:
+            vts(dzq, dzf, -2048.0, A.add)
+        vmax4(ap("sc", 64, 128), wg)
+        vtt(ap("dz", 48, 64), ap("sc", 67, 128, 4), dzq, A.max)
+        if last:
+            vts(su(t + 1), ap("dz", 48, 64), -1.0, A.mult)
+        else:
+            vts(su(t + 1), ap("dz", 48, 64), float(W), A.add)
+            preload(t + 1)
+            arrives(ui(t, 1, 6), "opt%d" % t)
+            mms(ap("B0", 0, S), [("DJ", ap("gj")), ("DG0", ui(t, 1)), ("NDL", ui(t, 6))], True, False)
+            for j in range(4):
+                mm(ap("B0", 0, S), shift("BU", j + 1), ui(t, j + 2), False, False)
+            if t == 0:
+                tag_put(2, 1)
+            if t == 1:
+                tag_out(2, 1, "B2")
+
+    def settle(t):
+        v, dS, zl = blk("vin", t), ap("B5", 0, S), ap("B4", 0, S)
+        arrives(v, "ver%d" % t, 2 if t < RO - 1 else 1)
+        if t < RO - 1:
+            vtt(tmp, v, dS, A.mult)
+            vtt(ind(Y, su(t)), cY(t), tmp, A.add)
+            day_a(t + 1)
+            mms(dS, [("LE0", brow(t)), ("I256", land(t))], True, False)
+            vts(ne, ind(Y, su(t + 1)), 256.0, A.is_lt)
+            act(colg, ind(Y, su(t + 1)), F.Copy)
+            if t + 2 < RO:
+                reserve(t + 2)
+            mms(zl, [("EMN", ne)], False, True)
+            mms(dS, [("NID", colg)], False, True)
+            vts(tmp2, zl, c["BY"], A.add, 0.0, A.min)
+            vtt(ind(Y, su(t + 1)), colg, tmp2, A.add)
+            day_b(t + 1)
+            act(blk("aout", t + 1), dS, F.Relu, bias=-256.0)
+            send((STEP[t + 1], blk("ain", t + 1), blk("aout", t + 1), "ask%d" % (t + 1)))
+        else:
+            vtt(tmp, v, dS, A.is_lt)
+            vtt(ind(X, su(t)), cY(t), tmp, A.mult)
             dma("y", hbm(T.y, W, V), ap("XB", S + W, S + V))
             xw = ap("XB", 0, S + W)
             vts(ne, ind(xw, su(t + 1)), 0.0, A.is_gt)
             act(colg, ind(xw, su(t + 1)), F.Copy)
-            mm(zl, EMP, ne, False, True)
-            vts(ap("tmp2"), zl, BX, A.add, 0.0, A.max)
-            vtt(ind(xw, su(t + 1)), colg, ap("tmp2"), A.add)
+            mms(zl, [("EMP", ne)], False, True)
+            vts(tmp2, zl, c["BX"], A.add, 0.0, A.max)
+            vtt(ind(xw, su(t + 1)), colg, tmp2, A.add)
             dma("s", hbm(T.y, 0, W), ap("XB", S, S + W))
+
+    mask_chunk(0)
+    conv(0)
+    constants_0()
+    mask_chunk(1)
+    conv(1)
+    tag_out(0, 2, "B7")
+    mask_chunk(2)
+    conv(2)
+    constants_a()
+    first_ask()
+    for k in range(EARLY, NCH):
+        mask_chunk(k)
+        conv(k)
+    p_half(0)
+    preload(0)
+    constants_b()
+    constants_c()
+    p_half(1)
+    reserve(1)
+    day_a(0)
+    day_b(0)
+    for t in range(RO):
+        score(t)
+        choose(t)
+        settle(t)
 
     emit_all(g, T, Q, ops)
 
@@ -474,7 +660,7 @@ def emit_all(g, T, Q, ops):
     nsent = 0
     for j, (q, emit, rd, wr, kind, sem) in enumerate(ops):
         if kind == "a":
-            value[j] = (sem, ENGINES)
+            value[j] = (sem, emit)
             continue
         for i in need[j]:
             Q[q].wait_ge(T.sem[value[i][0]], value[i][1])

@@ -5,55 +5,59 @@ W, R, S, K, M = 4096, 1024, 256, 16, 97
 V = W + R
 STEP = (1, 1, 1, 1)
 RO = len(STEP)
-NCH = 5
-CH = V // NCH
-EARLY = 3
+LOADS = ((V // 2, V), (0, V // 2))
+FUSE = 2
+EDJ = 11
 ENGINES = 16
 KLAST = 12
 VP = S + 16
 BIG = 8192.0
 QB = 192.0
-SCHED = (("vg", 0), ("sg", 0, 4), ("dg",), ("old",), ("z", 0), ("sg", 1, 8), ("vg", 2), ("z", 1), ("key", 0, 4),
-         ("ss", 0, 4), ("pre", 2), ("vg", 6), ("sg", 2, 12), ("key", 4, 8), ("z", 2), ("nk",), ("ss", 1, 8),
-         ("vg", 10), ("key", 8, 12), ("ss", 2, 12), ("vg", 14), ("key", 12, 16))
+SCHED = (("pre", 0, 2), ("c",), ("pre", 1, 2), ("vg", 0, 2), ("sg", 0, 4, 2), ("old",), ("z", 0, 2), ("sg", 1, 8, 2),
+         ("vg", 2, 2), ("key", 0, 4), ("z", 1, 2), ("ss", 0, 4, 2), ("pre", 2, 1), ("vg", 6, 2), ("sg", 2, 12, 1),
+         ("key", 4, 8), ("z", 2, 1), ("nk",), ("ss", 1, 8, 2), ("vg", 10, 2), ("key", 8, 12), ("ss", 2, 12, 1),
+         ("vg", 13, 2), ("vg", 15, 1), ("key", 12, 16))
+START = (("mask", 0), ("add", V // 2, V), ("c0",), ("mask", 1), ("ask",), ("put", 0), ("get", 0), ("ca",), ("p", 0),
+         ("wrap", 0, 1, "B6"), ("put", 1), ("res",), ("da", 0), ("pre", 0), ("out", 0, 1, "B6"), ("db", 0), ("get", 1),
+         ("cb",), ("dc", 0), ("cc",), ("cs",), ("ch",))
+TAIL = (("p", 1),)
+HOP = (("put", 2), ("get", 2))
 
 BF, F32, I32, U16, F16 = "bfloat16", "float32", "int32", "uint16", "float16"
-MATS = ("ID", "NID", "I256", "N256", "I8K", "I97", "N4K", "IH", "DG0", "DL", "NDL", "DJ", "GG", "NG", "GI", "G012",
-        "G34", "LE0", "U0", "T1", "T2", "D0", "ND0", "D1", "EMP", "EMN", "E0", "E1", "E2", "E3", "F0", "F1", "F2", "F3")
+MATS = ("ID", "NID", "I256", "N256", "I8K", "I97", "N4K", "DG0", "DL", "NDL", "DJ", "GG", "G012", "G34", "LE0",
+        "U0", "T1", "NT2", "D0", "EMN", "E0", "E1", "E2", "E3", "F0", "F1", "F2", "F3")
 WRAPS = ("BU", "B012", "BW", "QP", "QN")
-COLS = ("QF", "PM", "QM1", "QP1", "QM2", "G16", "G15", "BY", "BX", "NZ15", "B15", "MB", "GE2", "WCOL", "NZ0", "A4",
-        "T0", "T1", "T2", "M0", "M1", "M2", "M3", "L2", "C3", "CL", "PB", "CJ0", "CJ")
+COLS = ("PM", "G16", "G15", "BX", "NZ15", "B15", "MB", "NG2", "WCOL", "A4", "GM", "QM", "L2", "C3", "CL", "PB", "CJ0",
+        "CJ")
 SCRATCH = {
-    "XB": ("sbuf", [128, S + V], BF), "Y": ("sbuf", [128, V], BF), "mk": ("sbuf", [128, V], BF),
+    "XB": ("sbuf", [128, S + V], BF), "Y": ("sbuf", [128, V], BF),
     "trk": ("sbuf", [128, 64], I32), "cnd": ("sbuf", [128, 1024], I32), "p16": ("sbuf", [128, 1024], F16),
     "fin": ("sbuf", [128, S], BF), "fout": ("sbuf", [128, S], BF),
-    "ain": ("sbuf", [128, S * RO], BF), "aout": ("sbuf", [128, S * RO], BF),
-    "uin": ("sbuf", [128, 6 * S * RO], BF), "uout": ("sbuf", [128, 7 * S * RO], BF),
-    "vin": ("sbuf", [128, S * RO], BF), "vout": ("sbuf", [128, VP * RO], BF),
-    "lin": ("sbuf", [128, S * RO], BF), "lout": ("sbuf", [128, S * RO], BF),
+    "uin": ("sbuf", [128, 4 * S * RO], BF), "uout": ("sbuf", [128, 6 * S * (RO + 1)], BF),
+    "vin": ("sbuf", [128, S * RO], BF), "lin": ("sbuf", [128, S * RO], BF), "vout": ("sbuf", [128, VP * RO], BF),
     "jin": ("sbuf", [128, 48], U16), "jout": ("sbuf", [128, 48], U16),
     "cmp": ("sbuf", [128, K * S], BF), "xg": ("sbuf", [128, 512 * 3], BF), "eq": ("sbuf", [128, 16 * S], BF),
-    "iq": ("sbuf", [128, 8], I32), "ix": ("sbuf", [128, 144], BF), "ig": ("sbuf", [128, 128], BF),
+    "iq": ("sbuf", [128, 8], I32), "qf": ("sbuf", [128, 4], F32), "ix": ("sbuf", [128, 144], BF),
+    "ig": ("sbuf", [128, 512], BF), "iw": ("sbuf", [128, 512], F32),
     "ia": ("sbuf", [128, S], BF), "kc": ("sbuf", [128, S], BF), "i16": ("sbuf", [128, 16], F32),
     "jr": ("sbuf", [128, S], BF), "i4": ("sbuf", [128, 64], BF), "r4": ("sbuf", [128, 4], F32),
-    "iv": ("sbuf", [128, 144], BF),
+    "iv": ("sbuf", [128, 144], BF), "oh": ("sbuf", [128, 32], F32),
     "cols": ("sbuf", [128, 4 * len(COLS)], F32), "pmi": ("sbuf", [128, 16], I32),
     "mats": ("sbuf", [128, 128 * len(MATS)], BF), "wraps": ("sbuf", [128, 144 * len(WRAPS)], BF),
-    "mlt": ("sbuf", [128, S], BF), "meq": ("sbuf", [128, S], BF), "msk": ("sbuf", [128, S], BF),
+    "mlt": ("sbuf", [128, S], BF), "meq": ("sbuf", [128, S], BF),
     "m4": ("sbuf", [128, 64], F32), "mn": ("sbuf", [128, 64], BF), "mb": ("sbuf", [128, 64], F32),
     "rst": ("sbuf", [128, 64], F32), "rep": ("sbuf", [128, 8], U16), "uf": ("sbuf", [128, 64], F32),
-    "su": ("sbuf", [128, 80], U16), "uu": ("sbuf", [128, 48], U16), "uw": ("sbuf", [128, 256], F16),
-    "TG": ("sbuf", [128, 2 * R + S], BF), "tv": ("sbuf", [128, 2 * S], BF), "tg": ("sbuf", [128, 2 * S], BF),
-    "so": ("sbuf", [128, 64], F32), "s0": ("sbuf", [128, 80], U16),
+    "su": ("sbuf", [128, 160], U16), "uu": ("sbuf", [128, 48], U16), "uw": ("sbuf", [128, 256], F16),
+    "TG": ("sbuf", [128, R + S], BF), "tv": ("sbuf", [128, S], BF), "tg": ("sbuf", [128, 3 * S], BF),
+    "so": ("sbuf", [128, 64], F32), "s0": ("sbuf", [128, 16], U16),
     "rr": ("sbuf", [128, S], BF), "bw": ("sbuf", [128, 16], BF), "b4": ("sbuf", [128, 64], BF),
-    "qq": ("sbuf", [128, S], BF), "cu": ("sbuf", [128, S], U16), "c16": ("sbuf", [128, S], F16),
-    "sc": ("sbuf", [128, 128], F32),
-    "tr": ("sbuf", [128, 320], F32), "ki": ("sbuf", [128, 32], I32),
+    "qq": ("sbuf", [128, S], BF), "cu": ("sbuf", [128, S], U16), "kf": ("sbuf", [128, S], F16),
+    "sc": ("sbuf", [128, 128], F32), "tr": ("sbuf", [128, 320], F32), "ki": ("sbuf", [128, 32], I32),
     "dz": ("sbuf", [128, 64], F32), "dm": ("sbuf", [128, 128], F16),
     "row": ("sbuf", [128, S], F16), "ab": ("sbuf", [128, S], BF),
-    "ne": ("sbuf", [128, S], BF), "colg": ("sbuf", [128, S], BF), "tmp": ("sbuf", [128, S], BF),
+    "ne": ("sbuf", [128, S], BF), "tl": ("sbuf", [128, 4 * S], BF), "tmp": ("sbuf", [128, S], BF),
     "tmp2": ("sbuf", [128, S], BF), "nes": ("sbuf", [128, S], BF), "nn": ("sbuf", [128, S], BF),
-    "cY": ("sbuf", [128, 2 * S], BF), "cU": ("sbuf", [128, S], BF), "neU": ("sbuf", [128, S], BF),
+    "cY": ("sbuf", [128, 2 * S], BF), "neU": ("sbuf", [128, S], BF),
     "ge": ("sbuf", [128, VP], BF), "gj": ("sbuf", [128, S], BF),
 }
 BANKS = tuple("B%d" % i for i in range(8))
@@ -174,8 +178,15 @@ def rank_program(g, core, T, topo):
         add(None, ENGINES // writes, [], o, "a", sem)
 
     c = {k: ap("cols", 4 * j, 4 * j + 1) for j, k in enumerate(COLS)}
+    c.update({k: ap("qf", j, j + 1) for j, k in enumerate(("QM2", "QM1", "QF", "QP1"))})
+    c.update({"T0": ap("oh", 0, 1), "T1": ap("oh", 1, 2), "T2": ap("oh", 2, 3), "T15": ap("oh", 15, 16),
+              "BY": ap("oh", 16, 17), "NZ0": ap("oh", 31, 32)})
     m = {k: ap("mats", 128 * j, 128 * (j + 1)) for j, k in enumerate(MATS)}
     wr = {k: ap("wraps", 144 * j, 144 * (j + 1)) for j, k in enumerate(WRAPS)}
+
+    def four(name):
+        j = 128 * MATS.index(name)
+        return ap("mats", j, j + 512)
 
     def shift(name, a, top=15):
         j = 144 * WRAPS.index(name) + top - a
@@ -188,11 +199,11 @@ def rank_program(g, core, T, topo):
 
     X = ap("XB", S, S + V)
     Y = ap("Y")
-    ne, colg, tmp, tmp2, nes = ap("ne"), ap("colg"), ap("tmp"), ap("tmp2"), ap("nes")
+    ne, tmp, tmp2, nes, neU = ap("ne"), ap("tmp"), ap("tmp2"), ap("nes"), ap("neU")
     rep4 = ap("rep", 4, 8)
 
     def su(t):
-        return blk("su", t, 16)
+        return blk("su", t, 16, 32)
 
     def uu(t):
         return blk("uu", t - 1, 16)
@@ -200,190 +211,185 @@ def rank_program(g, core, T, topo):
     def go(t):
         return blk("vout", t, S, VP)
 
-    def land(t):
-        return blk("lout", t)
-
     def uo(t, j, w=1):
-        return blk("uout", t, w * S, 7 * S, j * S)
+        return blk("uout", t, w * S, 6 * S, j * S)
 
     def ui(t, j, w=1):
-        return blk("uin", t, w * S, 6 * S, (j - 1) * S)
+        return blk("uin", t, w * S, 4 * S, (j - 1) * S)
 
     def brow(t, w=S):
-        return uo(t, 0, w // S)
+        return uo(t, 4, w // S)
 
     def cY(t):
         return blk("cY", t % 2)
 
     dma("s", ap("trk"), hbm(T.trucks, 0, 64))
-    for k in range(NCH):
-        dma("y", blk("XB", k, CH, CH, S), hbm(T.days, k * CH, (k + 1) * CH))
+    for a, b in LOADS:
+        dma("y", ap("XB", S + a, S + b), hbm(T.days, a, b))
     dma("y", blk("cnd", 0), hbm(T.cand, 0, S))
     dma("y", ap("cnd", S, RO * S), hbm(T.cand, S, RO * S))
 
     iota(ap("iq", 0, 1), [[0, 1]], 0, 1, small=False)
-    iota(ap("i16"), [[16, 16]], 0, 0)
+    iota(ap("qf"), [[1, 4]], -2, 1)
+    iota(ap("ia"), [[0, 16], [1, 16]], 0, 0)
+    iota(ap("i16"), [[16, 16]], V, 0)
     iota(ap("ix"), [[1, 144]], 0, 0)
     iota(ap("jr"), [[-1, S]], S, 0)
-    iota(ap("ia"), [[0, 16], [1, 16]], 0, 0)
-    iota(ap("ig"), [[16, 8], [0, 16]], 0, 0)
-    iota(ap("i4"), [[0, 16], [1, 4]], 0, 0)
-    iota(ap("r4"), [[4, 4]], 0, 0)
-    iota(ap("iv"), [[16, 9], [0, 4], [-1024, 4]], 3072, 0)
-    iota(ap("kc"), [[4096, 16], [0, 16]], 2048, 0)
+    iota(ap("ig"), [[1024, 4], [16, 8], [0, 16]], 0, 0)
     pm, p1, m3, a4 = [ap("pmi", 4 * j, 4 * j + 1) for j in range(4)]
-    ix, ig = ap("ix", 0, 128), ap("ig")
-    vset(ap("TG"), 0.0)
+    ix, ig = ap("ix", 0, 128), ap("ig", 0, 128)
     vts(pm, ap("iq", 0, 1), 15, A.bitwise_and)
-    vcopy(c["QF"], ap("iq", 0, 1))
-    vts(p1, ap("iq", 0, 1), 1, A.bitwise_and)
-    vcopy(c["PM"], pm)
-    vts(m3, ap("iq", 0, 1), 3, A.bitwise_and)
+    vset(ap("TG"), 0.0)
     vts(c["MB"], pm, -0.5, A.add, 256.0, A.mult)
-    for t in range(3):
-        vts(c["T%d" % t], pm, float(t), A.is_equal)
-    vtt(c["G16"], c["QF"], c["PM"], A.subtract)
-    vts(m["ID"], ix, c["QF"], A.is_equal)
-    vts(ap("so", 0, 16), ap("i16"), c["PM"], A.add, float(V), A.add)
-    vts(c["G15"], c["G16"], 15.0, A.add)
+    vcopy(c["PM"], pm)
     act(ap("mlt"), ap("ia"), F.Sigmoid, bias=c["MB"], scale=-256.0)
+    vts(ap("oh", 0, 16), ap("ia", 0, 16), c["PM"], A.is_equal)
+    vts(c["G15"], pm, -1.0, A.mult, c["QF"], A.add)
+    vts(ap("so", 0, 16), ap("i16"), c["PM"], A.add)
+    vts(m["ID"], ix, c["QF"], A.is_equal)
+    vts(ap("so", 16, 32), ap("trk", 0, 16), float(W), A.is_lt, BIG, A.mult)
+    vts(ap("uu"), ap("trk", 16, 64), -float(W), A.add)
+    vtt(ap("so", 32, 48), ap("so", 16, 32), ap("trk", 0, 16), A.add)
+    vts(wr["BU"], ap("ix"), -15.0, A.add, c["G15"], A.is_equal)
+    vtt(ap("so", 48, 64), ap("so", 32, 48), ap("so", 0, 16), A.min)
+    vcopy(su(0), ap("trk", 0, 16))
+    vts(ap("s0"), ap("so", 48, 64), -float(W), A.add)
+    c["G16"] = c["G15"]
 
-    def tag_put(t, k):
-        for j in range(k):
-            vts(blk("tv", j), ap("jr"), c["T%d" % t], A.mult)
-        vcopy(ind(ap("TG"), uu(t) if t else ap("s0", 0, 32)), ap("tv", 0, k * S))
+    def tag_put(t):
+        vts(ap("tv"), ap("jr"), c["T%d" % t], A.mult)
+        vcopy(ind(ap("TG"), uu(t) if t else ap("s0")), ap("tv"))
 
-    def tag_get(t, k, bank):
-        act(ap("tg", 0, k * S), ind(ap("TG"), uu(t + 1) if t else ap("s0", 32, 64)), F.Identity, scale=c["T%d" % t])
-        wrap(ap(bank, 0, 16 * k), "BU", ap("tg", 0, k * S), True, True)
+    def tag_get(t):
+        act(blk("tg", t), ind(ap("TG"), uu(t + 1)), F.Identity, scale=c["T%d" % t])
+
+    def tag_wrap(t, k, bank):
+        wrap(ap(bank, 0, 16 * k), "BU", ap("tg", t * S, (t + k) * S), True, True)
 
     def tag_out(t, k, bank):
         vts(ap("jout", 16 * t, 16 * (t + k)), ap(bank, 0, 16 * k), -1.0, A.mult, float(S), A.add)
         send((STEP[t], ap("jin", 16 * t, 16 * (t + k)), ap("jout", 16 * t, 16 * (t + k)), "tag%d" % t))
 
-    vts(ap("so", 16, 32), ap("trk", 0, 16), float(W), A.is_lt, BIG, A.mult)
-    vts(ap("uu"), ap("trk", 16, 64), -float(W), A.add)
-    vtt(ap("so", 32, 48), ap("so", 16, 32), ap("trk", 0, 16), A.add)
-    vts(wr["BU"], ap("ix"), c["G15"], A.is_equal)
-    vtt(ap("so", 48, 64), ap("so", 32, 48), ap("so", 0, 16), A.min)
-    vcopy(su(0), ap("trk", 0, 16))
-    vts(ap("s0", 0, 16), ap("so", 48, 64), -float(W), A.add)
-    for j, (b, o) in enumerate(((1, R + S), (1, 0), (2, R + S))):
-        vts(blk("s0", j + 1, 16), blk("trk", b, 16), float(o - W), A.add)
-    tag_put(0, 2)
-    tag_get(0, 2, "B7")
+    def scaled(name, src, k):
+        act(m[name] if name in m else wr[name], m[src] if src in m else wr[src], F.Identity, scale=k)
+
+    def diag(name, k):
+        scaled(name, "ID", k)
 
     def constants_0():
-        vts(c["QM1"], c["QF"], -1.0, A.add)
-        vts(c["BY"], pm, 0.0, A.not_equal, 256.0, A.mult)
-        vts(m["I256"], ix, c["QF"], A.is_equal, 256.0, A.mult)
-        vts(m["U0"], ix, c["QM1"], A.is_equal, c["BY"], A.mult)
+        vts(ap("oh", 16, 32), ap("ia", 0, 16), c["PM"], A.not_equal, 256.0, A.mult)
+        scaled("I256", "ID", 256.0)
+        scaled("NID", "ID", -1.0)
         vts(m["GG"], ig, c["G16"], A.is_equal)
-        vts(m["NID"], ix, c["QF"], A.is_equal, -1.0, A.mult)
+        vts(m["U0"], ix, c["QM1"], A.is_equal, c["BY"], A.mult)
         vtt(m["D0"], m["I256"], m["U0"], A.subtract)
-
-    conv_banks = ("B0", "B1", "B2", "B3")
+        iota(ap("r4"), [[4, 4]], 0, 0)
+        iota(ap("i4"), [[0, 16], [1, 4]], 0, 0)
 
     def mask_chunk(k):
-        vts(blk("mk", k, CH), blk("XB", k, CH, CH, S), 0.0, A.is_equal, 256.0, A.mult)
+        a, b = LOADS[k]
+        vts(ap("Y", a, b), ap("XB", S + a, S + b), 0.0, A.is_equal, 256.0, A.mult)
 
-    def conv(k):
-        for h in (2 * k, 2 * k + 1):
-            bank = ap(conv_banks[h % 4])
-            mms(bank, [("ID", blk("XB", h, 512, 512, S)), ("ID", blk("mk", h, 512))])
-            act(blk("Y", h, 512), bank, F.Copy)
+    def add_days(a, b):
+        o, i = ap("Y", a, b), ap("XB", S + a, S + b)
+        sem = "dma%d" % ndma[0]
+        ndma[0] += 1
+        add("g", lambda: g.dma_start(o[0], i[0], accum_op=A.add, max_dma_last_dim=4096), [i, o], o, "d", sem)
 
     def constants_a():
-        vts(a4, pm, 2, A.arith_shift_right)
-        vts(c["QP1"], c["QF"], 1.0, A.add)
-        vts(c["QM2"], c["QF"], -2.0, A.add)
-        vts(c["NZ15"], pm, 15.0, A.not_equal)
-        vts(c["B15"], pm, 15.0, A.is_equal, 256.0, A.mult)
-        vts(c["GE2"], pm, 2.0, A.is_ge, 256.0, A.mult)
-        vcopy(c["A4"], a4)
-        vts(c["NZ0"], c["NZ15"], 256.0, A.mult)
-        vts(c["WCOL"], c["B15"], 3840.0, A.mult, 65536.0, A.add)
-        vts(c["BX"], c["BY"], -1.0, A.mult, -256.0, A.add)
+        vts(c["NZ15"], c["NZ0"], 1.0 / 256, A.mult)
+        vts(c["B15"], c["T15"], 256.0, A.mult)
+        vts(c["WCOL"], c["T15"], 15 * 65536.0, A.mult, 65536.0, A.add)
         vts(ap("rep", 0, 4), ap("r4"), 0.0, A.mult, c["PM"], A.add)
-        vts(rep4, ap("r4"), c["A4"], A.add)
-        vts(m["I97"], ix, c["QF"], A.is_equal, float(M), A.mult)
-        vts(m["N4K"], ix, c["QF"], A.is_equal, -float(W), A.mult)
-        vts(wr["BW"], ap("ix"), c["G15"], A.is_equal, c["WCOL"], A.mult)
-        vts(m["I8K"], ix, c["QF"], A.is_equal, BIG, A.mult)
-        vts(m["NG"], ig, c["G16"], A.is_equal, -1.0, A.mult)
-        vts(c["QM2"], c["QF"], -2.0, A.add)
-        vts(m["T2"], ix, c["QM2"], A.is_equal, c["GE2"], A.mult)
-        vts(ap("meq"), ap("ia"), c["PM"], A.is_equal, -0.25, A.mult)
-        vtt(m["D1"], m["U0"], m["T2"], A.subtract)
+        diag("I97", float(M))
+        diag("N4K", -float(W))
+        vts(wr["BW"], wr["BU"], c["WCOL"], A.mult)
 
     def constants_b():
-        vtt(ap("msk"), ap("mlt"), ap("meq"), A.add)
-        for s in range(4):
-            vts(c["M%d" % s], m3, float(s), A.is_equal)
-        vtt(m["GI"], m["GG"], m["ID"], A.add)
+        vts(a4, pm, 2, A.arith_shift_right)
+        vts(m3, pm, 3, A.bitwise_and)
+        diag("I8K", BIG)
+        vts(ap("kf"), ap("kc"), W / BIG, A.mult, (2048.0 + W * QB) / BIG, A.add)
+        vcopy(c["A4"], a4)
+        vts(c["GM"], m3, 1024.0, A.mult, c["G16"], A.add)
+        vts(c["QM"], m3, 1024.0, A.mult, c["QF"], A.add)
+        vts(c["NG2"], pm, 2.0, A.is_ge, -256.0, A.mult)
+        vts(rep4, ap("r4"), c["A4"], A.add)
         vts(ap("m4"), ap("i4"), c["A4"], A.is_equal)
         vts(ap("mn"), ap("i4"), c["A4"], A.not_equal, -2.0, A.mult)
-        vts(ap("mb"), ap("i4"), c["A4"], A.not_equal, -2 * BIG, A.mult)
         vts(ap("rst"), ap("i4"), 0.0, A.is_equal, -8 * BIG, A.mult)
+        vts(four("E0"), ap("ig"), c["GM"], A.is_equal)
+        vts(four("F0"), ap("iw"), c["QM"], A.is_equal)
+        vts(ap("meq"), ap("ia"), c["PM"], A.is_equal, -0.25, A.mult)
+        vts(m["NT2"], ix, c["QM2"], A.is_equal, c["NG2"], A.mult)
+        vts(wr["QP"], ap("iv"), c["G16"], A.is_equal, BIG / 16 / 256, A.mult)
+        diag("N256", -256.0)
+
+    def constants_h():
+        vts(ap("mb"), ap("i4"), c["A4"], A.not_equal, -2 * BIG, A.mult)
         vts(ap("uf", 0, 48), ap("trk", 16, 64), -float(W), A.add)
-        vts(ap("uf", 48, 64), ap("so", 0, 16), -1.0, A.mult, float(V), A.add)
-        for s in range(4):
-            vts(m["E%d" % s], m["GG"], c["M%d" % s], A.mult)
-            vts(m["F%d" % s], m["GI"], c["M%d" % s], A.mult)
-        vts(wr["QP"], ap("iv"), c["G16"], A.is_equal, BIG / 16, A.mult)
         vts(wr["QN"], ap("iv"), c["G16"], A.is_equal, -BIG / 16, A.mult)
-        vts(m["ND0"], m["D0"], -1.0, A.mult)
-        vts(m["DG0"], ix, c["QF"], A.is_equal, c["T0"], A.mult)
+        vset(ap("vout", S, VP), 0.0)
 
     def constants_c():
+        vts(p1, pm, 1, A.bitwise_and)
+        vts(c["CL"], c["T0"], 2 * BIG, A.mult, -BIG, A.add)
         vts(m["T1"], ix, c["QP1"], A.is_equal, c["NZ0"], A.mult)
-        vts(m["N256"], ix, c["QF"], A.is_equal, -256.0, A.mult)
+        vts(c["CJ0"], p1, -2 * BIG / 256, A.mult, BIG / 256, A.add)
+        vts(c["PB"], p1, BIG, A.mult, -BIG, A.add)
+        vtt(c["CJ"], c["CJ0"], c["BY"], A.mult)
         vts(c["L2"], pm, 2.0, A.is_le)
         vts(c["C3"], pm, 3.0, A.is_ge)
-        vts(c["CL"], c["T0"], 2 * BIG, A.mult, -BIG, A.add)
-        vts(c["PB"], p1, BIG, A.mult, -BIG, A.add)
-        vts(c["CJ0"], p1, -2 * BIG / 256, A.mult, BIG / 256, A.add)
-        vtt(m["EMN"], m["I256"], m["T1"], A.subtract)
-        vtt(c["CJ"], c["CJ0"], c["BY"], A.mult)
         vts(m["LE0"], ig, c["QF"], A.is_equal)
-        vts(m["DL"], ix, c["QF"], A.is_equal, c["CL"], A.mult)
-        vts(m["DJ"], ix, c["QF"], A.is_equal, c["CJ"], A.mult)
-        vts(m["G012"], ig, c["G16"], A.is_equal, c["L2"], A.mult)
-        vts(m["G34"], ig, c["G16"], A.is_equal, c["C3"], A.mult)
-        vts(wr["B012"], ap("ix"), c["G15"], A.is_equal, c["L2"], A.mult)
-        for t in range(RO):
-            vtt(blk("uw", t, 64), ind(blk("uf", t, 16), rep4), ap("mb"), A.add)
+        vtt(m["EMN"], m["I256"], m["T1"], A.subtract)
+
+    def constants_s():
+        diag("DG0", c["T0"])
+        diag("DL", c["CL"])
+        diag("DJ", c["CJ"])
+        vts(m["NDL"], m["DL"], -1.0 / 256, A.mult)
+        vts(m["G012"], m["GG"], c["L2"], A.mult)
+        vts(wr["B012"], wr["BU"], c["L2"], A.mult)
+        scaled("G34", "GG", c["C3"])
         vset(ap("ge", S, VP), 0.0)
-        vset(ap("vout", S, VP), 0.0)
-        vts(m["NDL"], m["DL"], -1.0, A.mult)
 
     def constants_d():
-        vts(m["EMP"], m["EMN"], -1.0, A.mult)
-        vts(m["IH"], ix, c["QF"], A.is_equal, 0.5, A.mult)
+        vts(c["BX"], c["BY"], -1.0, A.mult, -256.0, A.add)
         vset(ap("XB", 0, S), 0.0)
 
-    def p_half(t):
-        vts(blk("p16", t), blk("cnd", t), -2048.0, A.add)
+    def p_half(t, k=1):
+        vts(blk("p16", t, k * S, S), blk("cnd", t, k * S, S), -2048.0, A.add)
 
     def first_ask():
+        colg = uo(0, 0)
         act(colg, ind(X, su(0)), F.Copy)
         act(ne, colg, F.Sign)
         mms(ap("B4", 0, S), [("ID", colg), ("D0", ne)])
         mms(ap("B5", 0, S), [("NID", colg), ("I256", ne)], True, False)
         act(ap("fout"), ap("B4", 0, S), F.Relu, bias=-256.0)
         send((STEP[0], ap("fin"), ap("fout"), "top"))
+        add_days(0, V // 2)
+        iota(ap("kc"), [[1, 16], [0, 16]], 0, 0)
+        iota(ap("iv"), [[16, 9], [0, 4], [-1024, 4]], 3072, 0)
+        iota(ap("iw"), [[1024, 4], [1, 128]], 0, 0)
         mms(ap("B5", 0, S), [("GG", ap("fout"))], False, True)
-        act(blk("aout", 0), ap("B5", 0, S), F.Relu, bias=-256.0)
-        send((STEP[0], blk("ain", 0), blk("aout", 0), "ask0"))
+        act(uo(0, 2), ap("B5", 0, S), F.Relu, bias=-256.0)
+
+    def send_ask(t):
+        j, w = (1, 2) if t < RO - 1 else (2, 1)
+        send((STEP[t], ui(t, j, w), uo(t, j, w), "ask%d" % t))
+
+    def reserve():
+        act(uo(0, 1), ind(ap("Y", W, V), uu(1)), F.Copy)
+        send_ask(0)
 
     s1, s2 = ap("B3", 0, S), ap("B7", 0, S)
     na = 16 * KLAST
     kb = ap("B4", 0, S - na)
-    cU, neU = ap("cU"), ap("neU")
 
     def preload(t):
-        mms(s1, [("ID", blk("p16", t))], True, False)
         mms(s2, [("ID", blk("p16", t))], True, False)
+        mms(s1, [("ID", blk("p16", t))], True, False)
 
     def day_a(t):
         if t == 0:
@@ -391,11 +397,14 @@ def rank_program(g, core, T, topo):
             arrives(src, "top")
         else:
             src = ap("rr")
-            arrives(blk("lin", t - 1), "sel%d" % (t - 1), 2)
+            arrives(blk("lin", t - 1), "sel%d" % (t - 1), FUSE)
             mms(ap("B0", 0, S), [("DL", blk("lin", t - 1))], False, True)
             act(src, ap("B0", 0, S), F.Relu, bias=c["PB"])
+            mms(ap("B4", 0, S), [("LE0", brow(t - 1)), ("N256", go(t - 1)), ("ID", uo(t - 1, 3))], True, False)
+            preload(t)
         wrap(ap("B0", 0, 16), "B012" if t else "BU", src, True, True)
-        mms(ap("B1", 0, S), [("G012" if t else "GG", src)])
+        for h in range(2):
+            mms(blk("B1", h), [("G012" if t else "GG", src)])
 
     def day_b(t):
         act(ap("bw"), ap("B0", 0, 16), F.Copy)
@@ -403,73 +412,70 @@ def rank_program(g, core, T, topo):
         for bank in ("B3", "B7"):
             for k in range(4):
                 mms(blk(bank, k, 64), [("I97", ap("b4"))], False, bank == "B3" and k == 3)
-        if t + 1 < RO:
-            act(neU, cU, F.Sign, bias=256.0, scale=-1.0)
+
+    def day_c(t):
         act(ap("qq"), s1, F.Identity, bias=QB + 2.0 ** -13, scale=1.0 / W)
         mms(s2, [("N4K", ap("qq"))], False, True)
-        for h in range(2):
-            act(uo(t, h), ap("B1", 0, S), F.Identity, bias=c["B15"], scale=c["NZ15"])
-        if t + 1 < RO:
-            mms(ap("B3", 0, S), [("ID", cU), ("D0", neU)])
-            mms(ap("B3", S, 2 * S), [("ID", cU), ("D1", neU)])
+        act(brow(t, 2 * S), ap("B1"), F.Identity, bias=c["B15"], scale=c["NZ15"])
 
     def score(t):
         zb = ("B0", "B1", "B0")
         vts(ap("cu"), s2, 2048.0 + W * QB, A.add)
-        vts(ap("c16"), ap("cu"), -2048.0, A.add)
-        mms(ap("B2", 0, na), [("ID", ap("kc", 0, na))], True, False)
-        mms(kb, [("ID", ap("kc", na, S))], True, False)
-        for bank in zb[:2]:
-            mms(ap(bank), [("NID", brow(t, 2 * S))], True, False)
-        mms(ap("B2", 0, na), [("ID", ap("c16", 0, na))], False, False)
-        mms(kb, [("ID", ap("c16", na, S))], False, False)
+
         last_a = max(i for i, s in enumerate(SCHED) if s[0] == "key" and s[1] < KLAST)
         for i, s in enumerate(SCHED):
-            if s[0] == "pre":
-                mms(ap(zb[s[1]]), [("NID", brow(t, 2 * S))], True, False)
+            if s[0] == "c":
+                for bank, a, b in (("B2", 0, na), ("B4", na, S)):
+                    mms(ap(bank, 0, b - a), [("ID", blk("p16", t, b - a, S, a)), ("I8K", ap("kf", a, b)),
+                                             ("N4K", ap("qq", a, b))], True, False)
+                    for k in range((b - a) // 64):
+                        mms(blk(bank, k, 64), [("I97", ap("b4"))], False, False)
+            elif s[0] == "pre":
+                mms(ap(zb[s[1]], 0, S * s[2]), [("NID", brow(t, S * s[2]))], True, False)
             elif s[0] == "old":
                 if t:
                     mms(ap("B6", 0, S), [("ID", cY(t - 1)), ("ID", tmp)])
-            elif s[0] == "dg":
-                mms(ap("B5", 0, S), [("I8K", ap("msk"))], True, False)
             elif s[0] == "sg":
-                act(blk("xg", s[1], 512), ind(Y, ap("cu", 16 * s[2], 16 * s[2] + 32)), F.Copy)
+                act(blk("xg", s[1], S * s[3], 512), ind(Y, ap("cu", 16 * s[2], 16 * (s[2] + s[3]))), F.Copy)
             elif s[0] == "z":
-                mms(ap(zb[s[1]]), [("ID", blk("xg", s[1], 512))], False, True)
+                mms(ap(zb[s[1]], 0, S * s[2]), [("ID", blk("xg", s[1], S * s[2], 512))], False, True)
             elif s[0] == "ss":
-                act(ap("cmp", S * s[2], S * (s[2] + 2)), ap(zb[s[1]]), F.Sigmoid, bias=-128.0, scale=-256.0)
+                act(ap("cmp", S * s[2], S * (s[2] + s[3])), ap(zb[s[1]], 0, S * s[3]), F.Sigmoid, bias=-128.0, scale=-256.0)
             elif s[0] == "vg":
-                vtt(ap("cmp", S * s[1], S * (s[1] + 2)), ind(Y, ap("cu", 16 * s[1], 16 * s[1] + 32)), brow(t, 2 * S), A.is_lt)
+                vtt(ap("cmp", S * s[1], S * (s[1] + s[2])), ind(Y, ap("cu", 16 * s[1], 16 * (s[1] + s[2]))),
+                    brow(t, S * s[2]), A.is_lt)
             elif s[0] == "nk":
-                arrives(blk("ain", t), "ask%d" % t)
-                mms(ap("B6", S, 2 * S), [("GG", blk("ain", t))] + ([("G34", ap("rr"))] if t else []))
+                arrives(ui(t, 1, 2), "ask%d" % t)
+                mms(ap("B6", S, 2 * S), [("GG", ui(t, 2))] + ([("G34", ap("rr"))] if t else []))
             elif s[1] < KLAST:
                 wrap(ap("B2", 16 * s[1], 16 * s[2]), "BW", ap("cmp", S * s[1], S * s[2]), False, i == last_a)
             else:
                 wrap(kb, "BW", ap("cmp", S * s[1], S * s[2]), False, True)
 
-    def reserve(t):
-        act(cU, ind(ap("Y", W, V), uu(t)), F.Copy)
-
     def choose(t):
         last = t == RO - 1
         cnt, dg, wg, nw = ap("B1", 0, S), ap("B5", 0, S), ap("B7", 0, 64), ap("B0", 0, 64)
         dzf, dzb, dzq = ap("dz", 0, 16), ap("dz", 16, 32), ap("dz", 32, 48)
-        nk = uo(t, 6)
-        act(nk, ap("B6", S, 2 * S), F.Relu, bias=1.0, scale=-1.0)
+        nk, cU, zl = uo(t, 3), ui(t, 1), ap("B4", 0, S)
+        act(nk, ap("B6", S, 2 * S), F.Relu, bias=256.0, scale=-256.0)
         mms(nw, [("I8K", ap("mn"))], True, False)
         wrap(nw, "QP", nk, False, True, 4)
-        mms(cnt, [("I8K", nk)], True, False)
+        mms(dg, [("I8K", ap("mlt")), ("I8K", ap("meq"))], True, False)
         if not last:
-            act(uo(t, 2, 2), ap("B3"), F.Relu, bias=-256.0)
-            mms(ap("B3", 0, S), [("NID", cU), ("GG", uo(t, 2))])
-            mms(ap("B3", S, 2 * S), [("NID", cU), ("ND0", neU), ("GG", uo(t, 3))])
+            send((STEP[t + 1], ui(t, 3, 2), uo(t, 3, 2), "opt%d" % t))
+            act(neU, cU, F.Sign, bias=256.0, scale=-1.0)
+            mms(ap("B3", 0, S), [("ID", cU), ("D0", neU)])
+            mms(ap("B3", S, 2 * S), [("ID", cU), ("U0", neU), ("NT2", neU)])
         act(cY(t), ind(Y, su(t)), F.Copy)
+        act(nes, cY(t), F.Sign, bias=256.0, scale=-1.0)
+        if not last:
+            act(ap("tl", 0, 2 * S), ap("B3"), F.Relu, bias=-256.0)
         if t:
             act(ap("nn"), ap("B6", 0, S), F.Sign, bias=256.0, scale=-1.0)
-        if not last:
-            act(uo(t, 4, 2), ap("B3"), F.Relu)
-            send((STEP[t + 1], ui(t, 1, 6), uo(t, 1, 6), "opt%d" % t))
+        if t == 0:
+            for s in TAIL:
+                steps[s[0]](*s[1:])
+            vtt(blk("uw", t, 64), ind(blk("uf", t, 16), rep4), ap("mb"), A.add)
         vcopy(ap("tr", 0, 64), ap("B2", 0, 64))
         vtt(ap("tr", 64, 128), ap("B2", 64, 128), ap("tr", 0, 64), A.min)
         vtt(ap("tr", 128, 192), ap("B2", 128, 192), ap("tr", 64, 128), A.min)
@@ -477,96 +483,110 @@ def rank_program(g, core, T, topo):
         vtt(ap("tr", 256, 288), ap("tr", 192, 224), ap("tr", 224, 256), A.min)
         vtt(ap("ki", 0, 16), ap("tr", 256, 272), ap("tr", 272, 288), A.min)
         vts(ap("ki", 16, 32), ap("ki", 0, 16), 0x100FFF, A.bitwise_and)
-        vmax4(ap("sc", 0, 64), nw)
         vts(dzf, ap("ki", 16, 32), float(W), A.min, -2048.0, A.add)
         vtt(ap("dm", 0, 64), ind(dzf, rep4), ap("m4"), A.mult)
+        vmax4(ap("sc", 0, 64), nw)
         vtt(dzb, dzf, ap("sc", 3, 64, 4), A.subtract)
         for s in range(4):
             mm(ap("B2", s, S, 4), m["E%d" % s], ap("dm", 0, 64), True, True)
+        for name in ("E%d", "F%d"):
+            for s in range(4):
+                mms(ap("B5", s, S, 4), [(name % s, ap("dm", 0, 64))], False, False)
+        if not last:
+            mms(ap("B4", S, 2 * S), [("D0", nes), ("NID", cY(t))])
+        vcopy(ap("row"), ap("B2", 0, S))
         vcopy(ap("dm", 64, 128), ind(dzb, rep4))
         for s in range(4):
-            mms(ap("B5", s, S, 4), [("F%d" % s, ap("dm", 0, 64))], False, False)
-        for s in range(4):
             mms(ap("B5", s, S, 4), [("NID", ap("dm", 64, 128))], False, s == 3)
-        vcopy(ap("row"), ap("B2", 0, S))
+        if 0 < t < RO - 1:
+            mms(ap("B0", S, 2 * S), [("I256", blk("lin", t - 1)), ("NID", ui(t - 1, 3))])
         act(ap("ab"), dg, F.Abs)
-        ed = ap("eq", S * 15, S * 16)
-        act(ed, ap("ab"), F.Relu, bias=1.0, scale=-1.0)
-        act(nes, cY(t), F.Sign, bias=256.0, scale=-1.0)
+        act(blk("eq", 15), ap("ab"), F.Relu, bias=1.0, scale=-1.0)
+        if not last:
+            act(dg, ap("B4", S, 2 * S), F.Relu)
         for j in range(15):
             e = ap("eq", S * j + 16 * (j + 1), S * (j + 1))
             vts(e, ap("row", 16 * (j + 1), S), ap("dz", 16 + j, 17 + j), A.is_equal)
-            if j == 13:
-                mms(cnt, [("NG", ed)], False, False)
-            mms(ap("B1", 16 * (j + 1), S), [("NG", e)], False, j == 14)
-        vts(go(t), cnt, -0.5, A.is_gt)
+            mms(ap("B1", 16 * (j + 1), S), [("GG", e)], j == 0, j == 14)
+            if j == 14 and not last:
+                mms(ap("B3", 0, S), [("NID", cU), ("GG", blk("tl", 0))])
+                mms(ap("B3", S, 2 * S), [("NID", cU), ("U0", neU), ("N256", neU), ("GG", blk("tl", 1))])
+            if j == EDJ:
+                mms(ap("B1", 0, 16), [("GG", blk("eq", 15, 16, S))], False, False)
+                mms(ap("B1", 16, S), [("GG", blk("eq", 15, S - 16, S, 16))], False, False)
+        if t < 2:
+            p_half(t + 2)
+        vtt(go(t), cnt, nk, A.is_le)
         verdict = (-STEP[t], blk("vin", t), go(t), "ver%d" % t)
         if last:
             send(verdict)
-        else:
+        elif FUSE == 2:
             send(verdict, (STEP[t + 1], blk("lin", t), go(t), "sel%d" % t))
-        vts(land(t), cnt, 0.0, A.is_equal)
-        if not last:
-            if t:
-                mms(ap("B6", 0, S), [("NID", blk("lin", t - 1)), ("ID", ui(t - 1, 6)), ("ID", go(t))])
-                act(ap("ge", 0, S), ap("B6", 0, S), F.Relu)
-            mms(ap("B5", S, 2 * S), [("D0", nes), ("NID", cY(t))])
-            if t != 1:
-                arrives(ap("jin", 16 * t, 32 + 8 * t), "tag%d" % t)
-            act(ap("gj"), ind(ap("ge") if t else ap("vout", 0, VP), blk("jin", t, 16)), F.Copy)
-            act(dg, ap("B5", S, 2 * S), F.Relu)
-            if t == 1:
-                tag_get(2, 1, "B2")
         else:
-            mms(dg, [("U0", nes), ("IH", nes)])
-        if t:
-            vtt(ind(X, su(t - 1)), cY(t - 1), ap("nn"), A.mult)
-        if t in (1, 2):
-            p_half(t + 1)
-        if t == 2:
-            constants_d()
+            send(verdict)
+            send((STEP[t + 1], blk("lin", t), go(t), "sel%d" % t))
         mms(wg, [("ID", blk("uw", t, 64))], True, False)
-        wrap(wg, "QN", land(t), False, True, 4)
-        mms(ap("B4", 0, S), [("LE0", brow(t)), ("I256" if last else "N256", land(t))], True, False)
+        wrap(wg, "QP", nk, False, False, 4)
+        wrap(wg, "QN", go(t), False, True, 4)
         if last:
             vts(dzq, dzf, -1.0, A.mult, -2048.0 - S, A.add)
+            mms(dg, [("U0", nes), ("ID", nes)])
         else:
+            if t:
+                vtt(ap("ge", 0, S), go(t), ap("B0", S, 2 * S), A.is_gt)
             vts(dzq, dzf, -2048.0, A.add)
+            if t < 2:
+                arrives(ap("jin", 16 * t, 16 + 32 * t), "tag%d" % t)
+            act(ap("tl", 2 * S, 4 * S), ap("B3"), F.Relu)
+            act(ap("gj"), ind(ap("ge") if t else ap("vout", 0, VP), blk("jin", t, 16)), F.Copy)
         vmax4(ap("sc", 64, 128), wg)
         vtt(ap("dz", 48, 64), ap("sc", 67, 128, 4), dzq, A.max)
         if last:
             vts(su(t + 1), ap("dz", 48, 64), -1.0, A.mult)
+            mms(zl, [("LE0", brow(t)), ("I256", go(t)), ("NID", nk)], True, False)
         else:
             vts(su(t + 1), ap("dz", 48, 64), float(W), A.add)
-            preload(t + 1)
-            arrives(ui(t, 1, 6), "opt%d" % t)
-            mms(ap("B0", 0, S), [("DJ", ap("gj")), ("DG0", ui(t, 1)), ("NDL", ui(t, 6))], True, False)
-            for j in range(4):
-                mm(ap("B0", 0, S), shift("BU", j + 1), ui(t, j + 2), False, False)
             if t == 0:
-                tag_put(2, 1)
-            if t == 1:
-                tag_out(2, 1, "B2")
+                for s in HOP:
+                    steps[s[0]](*s[1:])
+            arrives(ui(t, 3, 2), "opt%d" % t)
+            mms(ap("B0", 0, S), [("DG0", ui(t, 4)), ("NDL", ui(t, 3))], True, False)
+            for j in range(4):
+                mm(ap("B0", 0, S), shift("BU", j + 1), blk("tl", j), False, False)
+            mms(ap("B0", 0, S), [("DJ", ap("gj"))], False, False)
+        if t:
+            vtt(ind(X, su(t - 1)), cY(t - 1), ap("nn"), A.mult)
+        if t == 1:
+            vts(ap("uf", 48, 64), ap("so", 0, 16), -1.0, A.mult, float(V), A.add)
+        if t == 2:
+            constants_d()
+        if not last:
+            vtt(blk("uw", t + 1, 64), ind(blk("uf", t + 1, 16), rep4), ap("mb"), A.add)
 
     def settle(t):
         v, dS, zl = blk("vin", t), ap("B5", 0, S), ap("B4", 0, S)
-        arrives(v, "ver%d" % t, 2 if t < RO - 1 else 1)
+        colg = uo(t + 1, 0)
+        arrives(v, "ver%d" % t, FUSE if t < RO - 1 else 1)
         if t < RO - 1:
             vtt(tmp, v, dS, A.mult)
             vtt(ind(Y, su(t)), cY(t), tmp, A.add)
             day_a(t + 1)
-            mms(dS, [("LE0", brow(t)), ("I256", land(t))], True, False)
             vts(ne, ind(Y, su(t + 1)), 256.0, A.is_lt)
             act(colg, ind(Y, su(t + 1)), F.Copy)
-            if t + 2 < RO:
-                reserve(t + 2)
             mms(zl, [("EMN", ne)], False, True)
-            mms(dS, [("NID", colg)], False, True)
+            mms(dS, [("LE0", brow(t)), ("I256", go(t)), ("NID", uo(t, 3)), ("NID", colg)])
+            if t + 2 < RO:
+                vcopy(uo(t + 1, 1), ind(ap("Y", W, V), uu(t + 2)))
             vts(tmp2, zl, c["BY"], A.add, 0.0, A.min)
             vtt(ind(Y, su(t + 1)), colg, tmp2, A.add)
+            if t == 0:
+                tag_wrap(1, 2, "B2")
             day_b(t + 1)
-            act(blk("aout", t + 1), dS, F.Relu, bias=-256.0)
-            send((STEP[t + 1], blk("ain", t + 1), blk("aout", t + 1), "ask%d" % (t + 1)))
+            if t == 0:
+                tag_out(1, 2, "B2")
+            day_c(t + 1)
+            act(uo(t + 1, 2), dS, F.Relu, bias=-256.0)
+            send_ask(t + 1)
         else:
             vtt(tmp, v, dS, A.is_lt)
             vtt(ind(X, su(t)), cY(t), tmp, A.mult)
@@ -574,32 +594,17 @@ def rank_program(g, core, T, topo):
             xw = ap("XB", 0, S + W)
             vts(ne, ind(xw, su(t + 1)), 0.0, A.is_gt)
             act(colg, ind(xw, su(t + 1)), F.Copy)
-            mms(zl, [("EMP", ne)], False, True)
+            mms(zl, [("T1", ne), ("N256", ne)], False, True)
             vts(tmp2, zl, c["BX"], A.add, 0.0, A.max)
             vtt(ind(xw, su(t + 1)), colg, tmp2, A.add)
             dma("s", hbm(T.y, 0, W), ap("XB", S, S + W))
 
-    mask_chunk(0)
-    conv(0)
-    constants_0()
-    mask_chunk(1)
-    conv(1)
-    tag_out(0, 2, "B7")
-    mask_chunk(2)
-    conv(2)
-    constants_a()
-    first_ask()
-    for k in range(EARLY, NCH):
-        mask_chunk(k)
-        conv(k)
-    p_half(0)
-    preload(0)
-    constants_b()
-    constants_c()
-    p_half(1)
-    reserve(1)
-    day_a(0)
-    day_b(0)
+    steps = {"mask": mask_chunk, "add": add_days, "c0": constants_0, "ca": constants_a, "cb": constants_b,
+             "put": tag_put, "get": tag_get, "wrap": tag_wrap, "out": tag_out, "ask": first_ask, "p": p_half,
+             "pre": preload, "da": day_a, "db": day_b, "dc": day_c, "res": reserve, "ch": constants_h,
+             "cc": constants_c, "cs": constants_s}
+    for s in START:
+        steps[s[0]](*s[1:])
     for t in range(RO):
         score(t)
         choose(t)

@@ -18,17 +18,17 @@ SCHED = (("pre", 0, 2), ("c",), ("pre", 1, 2), ("vg", 0, 2), ("sg", 0, 4, 2), ("
          ("key", 4, 8), ("z", 2, 1), ("nk",), ("ss", 1, 8, 2), ("vg", 10, 2), ("key", 8, 12), ("ss", 2, 12, 1),
          ("vg", 13, 2), ("vg", 15, 1), ("key", 12, 16))
 START = (("mask", 0), ("add", V // 2, V), ("c0",), ("mask", 1), ("ask",), ("put", 0), ("get", 0), ("ca",), ("p", 0),
-         ("wrap", 0, 1, "B6"), ("put", 1), ("res",), ("da", 0), ("pre", 0), ("out", 0, 1, "B6"), ("db", 0), ("get", 1),
-         ("cb",), ("dc", 0), ("cc",), ("cs",), ("ch",))
+         ("put", 1), ("res",), ("da", 0), ("pre", 0), ("db", 0), ("get", 1), ("cc",), ("cs",), ("wrap", 0, 2, "B6"),
+         ("cb",), ("dc", 0), ("out", 0, 2, "B6"), ("ch",))
 TAIL = (("p", 1),)
-HOP = (("put", 2), ("get", 2))
+HOP = (("put", 2),)
 
 BF, F32, I32, U16, F16 = "bfloat16", "float32", "int32", "uint16", "float16"
 MATS = ("ID", "NID", "I256", "N256", "I8K", "I97", "N4K", "DG0", "DL", "NDL", "DJ", "GG", "G012", "G34", "LE0",
         "U0", "T1", "NT2", "D0", "EMN", "E0", "E1", "E2", "E3", "F0", "F1", "F2", "F3")
 WRAPS = ("BU", "B012", "BW", "QP", "QN")
-COLS = ("PM", "G16", "G15", "BX", "NZ15", "B15", "MB", "NG2", "WCOL", "A4", "GM", "QM", "L2", "C3", "CL", "PB", "CJ0",
-        "CJ")
+COLS = ("BX", "NZ15", "B15", "MB", "WCOL", "QM", "CL", "PB", "CJ0")
+COLB = ("PM", "G16", "NG2", "A4", "GM", "L2", "C3", "CJ")
 SCRATCH = {
     "XB": ("sbuf", [128, S + V], BF), "Y": ("sbuf", [128, V], BF),
     "trk": ("sbuf", [128, 64], I32), "cnd": ("sbuf", [128, 1024], I32), "p16": ("sbuf", [128, 1024], F16),
@@ -37,11 +37,12 @@ SCRATCH = {
     "vin": ("sbuf", [128, S * RO], BF), "lin": ("sbuf", [128, S * RO], BF), "vout": ("sbuf", [128, VP * RO], BF),
     "jin": ("sbuf", [128, 48], U16), "jout": ("sbuf", [128, 48], U16),
     "cmp": ("sbuf", [128, K * S], BF), "xg": ("sbuf", [128, 512 * 3], BF), "eq": ("sbuf", [128, 16 * S], BF),
-    "iq": ("sbuf", [128, 8], I32), "qf": ("sbuf", [128, 4], F32), "ix": ("sbuf", [128, 144], BF),
+    "iq": ("sbuf", [128, 8], I32), "qf": ("sbuf", [128, 4], BF), "ix": ("sbuf", [128, 144], BF),
     "ig": ("sbuf", [128, 512], BF), "iw": ("sbuf", [128, 512], F32),
     "ia": ("sbuf", [128, S], BF), "kc": ("sbuf", [128, S], BF), "i16": ("sbuf", [128, 16], F32),
     "jr": ("sbuf", [128, S], BF), "i4": ("sbuf", [128, 64], BF), "r4": ("sbuf", [128, 4], F32),
-    "iv": ("sbuf", [128, 144], BF), "oh": ("sbuf", [128, 32], F32),
+    "iv": ("sbuf", [128, 144], BF), "oh": ("sbuf", [128, 32], BF), "of": ("sbuf", [128, 4], F32),
+    "colb": ("sbuf", [128, 8 * len(COLB)], BF),
     "cols": ("sbuf", [128, 4 * len(COLS)], F32), "pmi": ("sbuf", [128, 16], I32),
     "mats": ("sbuf", [128, 128 * len(MATS)], BF), "wraps": ("sbuf", [128, 144 * len(WRAPS)], BF),
     "mlt": ("sbuf", [128, S], BF), "meq": ("sbuf", [128, S], BF),
@@ -53,7 +54,7 @@ SCRATCH = {
     "rr": ("sbuf", [128, S], BF), "bw": ("sbuf", [128, 16], BF), "b4": ("sbuf", [128, 64], BF),
     "qq": ("sbuf", [128, S], BF), "cu": ("sbuf", [128, S], U16), "kf": ("sbuf", [128, S], F16),
     "sc": ("sbuf", [128, 128], F32), "tr": ("sbuf", [128, 320], F32), "ki": ("sbuf", [128, 32], I32),
-    "dz": ("sbuf", [128, 64], F32), "dm": ("sbuf", [128, 128], F16),
+    "dz": ("sbuf", [128, 64], F32), "dm": ("sbuf", [128, 128], F16), "dh": ("sbuf", [128, 32], BF),
     "row": ("sbuf", [128, S], F16), "ab": ("sbuf", [128, S], BF),
     "ne": ("sbuf", [128, S], BF), "tl": ("sbuf", [128, 4 * S], BF), "tmp": ("sbuf", [128, S], BF),
     "tmp2": ("sbuf", [128, S], BF), "nes": ("sbuf", [128, S], BF), "nn": ("sbuf", [128, S], BF),
@@ -149,10 +150,10 @@ def rank_program(g, core, T, topo):
         else:
             add("g", lambda: g.iota(o[0], pattern, base, cm), [], o)
 
-    def dma(q, o, i):
+    def dma(q, o, i, after=None):
         sem = "dma%d" % ndma[0]
         ndma[0] += 1
-        add(q, lambda: Q[q].dma_start(o[0], i[0]), [i], o, "d", sem)
+        add(q, lambda: Q[q].dma_start(o[0], i[0]), [i, after], o, "d", sem)
 
     def hbm(t, a, b):
         return (t[:, a:b], [])
@@ -178,8 +179,9 @@ def rank_program(g, core, T, topo):
         add(None, ENGINES // writes, [], o, "a", sem)
 
     c = {k: ap("cols", 4 * j, 4 * j + 1) for j, k in enumerate(COLS)}
+    c.update({k: ap("colb", 8 * j, 8 * j + 1) for j, k in enumerate(COLB)})
     c.update({k: ap("qf", j, j + 1) for j, k in enumerate(("QM2", "QM1", "QF", "QP1"))})
-    c.update({"T0": ap("oh", 0, 1), "T1": ap("oh", 1, 2), "T2": ap("oh", 2, 3), "T15": ap("oh", 15, 16),
+    c.update({"T0": ap("of", 0, 1), "T1": ap("of", 1, 2), "T2": ap("of", 2, 3), "T15": ap("oh", 15, 16),
               "BY": ap("oh", 16, 17), "NZ0": ap("oh", 31, 32)})
     m = {k: ap("mats", 128 * j, 128 * (j + 1)) for j, k in enumerate(MATS)}
     wr = {k: ap("wraps", 144 * j, 144 * (j + 1)) for j, k in enumerate(WRAPS)}
@@ -227,15 +229,17 @@ def rank_program(g, core, T, topo):
     for a, b in LOADS:
         dma("y", ap("XB", S + a, S + b), hbm(T.days, a, b))
     dma("y", blk("cnd", 0), hbm(T.cand, 0, S))
-    dma("y", ap("cnd", S, RO * S), hbm(T.cand, S, RO * S))
 
     iota(ap("iq", 0, 1), [[0, 1]], 0, 1, small=False)
     iota(ap("qf"), [[1, 4]], -2, 1)
     iota(ap("ia"), [[0, 16], [1, 16]], 0, 0)
     iota(ap("i16"), [[16, 16]], V, 0)
     iota(ap("ix"), [[1, 144]], 0, 0)
-    iota(ap("jr"), [[-1, S]], S, 0)
     iota(ap("ig"), [[1024, 4], [16, 8], [0, 16]], 0, 0)
+    iota(ap("jr"), [[-1, S]], S, 0)
+    iota(ap("r4"), [[4, 4]], 0, 0)
+    iota(ap("i4"), [[0, 16], [1, 4]], 0, 0)
+    iota(ap("kc"), [[1, 16], [0, 16]], 0, 0)
     pm, p1, m3, a4 = [ap("pmi", 4 * j, 4 * j + 1) for j in range(4)]
     ix, ig = ap("ix", 0, 128), ap("ig", 0, 128)
     vts(pm, ap("iq", 0, 1), 15, A.bitwise_and)
@@ -244,20 +248,20 @@ def rank_program(g, core, T, topo):
     vcopy(c["PM"], pm)
     act(ap("mlt"), ap("ia"), F.Sigmoid, bias=c["MB"], scale=-256.0)
     vts(ap("oh", 0, 16), ap("ia", 0, 16), c["PM"], A.is_equal)
-    vts(c["G15"], pm, -1.0, A.mult, c["QF"], A.add)
+    vts(c["G16"], pm, -1.0, A.mult, c["QF"], A.add)
+    vcopy(ap("of"), ap("oh", 0, 4))
     vts(ap("so", 0, 16), ap("i16"), c["PM"], A.add)
     vts(m["ID"], ix, c["QF"], A.is_equal)
     vts(ap("so", 16, 32), ap("trk", 0, 16), float(W), A.is_lt, BIG, A.mult)
     vts(ap("uu"), ap("trk", 16, 64), -float(W), A.add)
     vtt(ap("so", 32, 48), ap("so", 16, 32), ap("trk", 0, 16), A.add)
-    vts(wr["BU"], ap("ix"), -15.0, A.add, c["G15"], A.is_equal)
+    vts(wr["BU"], ap("ix"), -15.0, A.add, c["G16"], A.is_equal)
     vtt(ap("so", 48, 64), ap("so", 32, 48), ap("so", 0, 16), A.min)
     vcopy(su(0), ap("trk", 0, 16))
     vts(ap("s0"), ap("so", 48, 64), -float(W), A.add)
-    c["G16"] = c["G15"]
 
     def tag_put(t):
-        vts(ap("tv"), ap("jr"), c["T%d" % t], A.mult)
+        vts(ap("tv"), ap("jr"), ap("oh", t, t + 1), A.mult)
         vcopy(ind(ap("TG"), uu(t) if t else ap("s0")), ap("tv"))
 
     def tag_get(t):
@@ -283,8 +287,6 @@ def rank_program(g, core, T, topo):
         vts(m["GG"], ig, c["G16"], A.is_equal)
         vts(m["U0"], ix, c["QM1"], A.is_equal, c["BY"], A.mult)
         vtt(m["D0"], m["I256"], m["U0"], A.subtract)
-        iota(ap("r4"), [[4, 4]], 0, 0)
-        iota(ap("i4"), [[0, 16], [1, 4]], 0, 0)
 
     def mask_chunk(k):
         a, b = LOADS[k]
@@ -297,18 +299,22 @@ def rank_program(g, core, T, topo):
         add("g", lambda: g.dma_start(o[0], i[0], accum_op=A.add, max_dma_last_dim=4096), [i, o], o, "d", sem)
 
     def constants_a():
-        vts(c["NZ15"], c["NZ0"], 1.0 / 256, A.mult)
-        vts(c["B15"], c["T15"], 256.0, A.mult)
-        vts(c["WCOL"], c["T15"], 15 * 65536.0, A.mult, 65536.0, A.add)
         vts(ap("rep", 0, 4), ap("r4"), 0.0, A.mult, c["PM"], A.add)
         diag("I97", float(M))
         diag("N4K", -float(W))
-        vts(wr["BW"], wr["BU"], c["WCOL"], A.mult)
+        act(c["NZ15"], c["NZ0"], F.Identity, scale=1.0 / 256)
+        act(c["B15"], c["T15"], F.Identity, scale=256.0)
+        act(c["WCOL"], c["T15"], F.Identity, scale=15 * 65536.0, bias=65536.0)
+        act(c["CL"], c["T0"], F.Identity, scale=2 * BIG, bias=-BIG)
+        scaled("BW", "BU", c["WCOL"])
+        diag("I8K", BIG)
+        diag("N256", -256.0)
+        diag("DG0", c["T0"])
+        diag("DL", c["CL"])
 
     def constants_b():
         vts(a4, pm, 2, A.arith_shift_right)
         vts(m3, pm, 3, A.bitwise_and)
-        diag("I8K", BIG)
         vts(ap("kf"), ap("kc"), W / BIG, A.mult, (2048.0 + W * QB) / BIG, A.add)
         vcopy(c["A4"], a4)
         vts(c["GM"], m3, 1024.0, A.mult, c["G16"], A.add)
@@ -323,17 +329,15 @@ def rank_program(g, core, T, topo):
         vts(ap("meq"), ap("ia"), c["PM"], A.is_equal, -0.25, A.mult)
         vts(m["NT2"], ix, c["QM2"], A.is_equal, c["NG2"], A.mult)
         vts(wr["QP"], ap("iv"), c["G16"], A.is_equal, BIG / 16 / 256, A.mult)
-        diag("N256", -256.0)
 
     def constants_h():
-        vts(ap("mb"), ap("i4"), c["A4"], A.not_equal, -2 * BIG, A.mult)
+        act(ap("mb"), ap("mn"), F.Identity, scale=BIG)
         vts(ap("uf", 0, 48), ap("trk", 16, 64), -float(W), A.add)
-        vts(wr["QN"], ap("iv"), c["G16"], A.is_equal, -BIG / 16, A.mult)
+        scaled("QN", "QP", -256.0)
         vset(ap("vout", S, VP), 0.0)
 
     def constants_c():
         vts(p1, pm, 1, A.bitwise_and)
-        vts(c["CL"], c["T0"], 2 * BIG, A.mult, -BIG, A.add)
         vts(m["T1"], ix, c["QP1"], A.is_equal, c["NZ0"], A.mult)
         vts(c["CJ0"], p1, -2 * BIG / 256, A.mult, BIG / 256, A.add)
         vts(c["PB"], p1, BIG, A.mult, -BIG, A.add)
@@ -344,13 +348,11 @@ def rank_program(g, core, T, topo):
         vtt(m["EMN"], m["I256"], m["T1"], A.subtract)
 
     def constants_s():
-        diag("DG0", c["T0"])
-        diag("DL", c["CL"])
-        diag("DJ", c["CJ"])
+        vts(m["DJ"], ix, c["QF"], A.is_equal, c["CJ"], A.mult)
         vts(m["NDL"], m["DL"], -1.0 / 256, A.mult)
         vts(m["G012"], m["GG"], c["L2"], A.mult)
         vts(wr["B012"], wr["BU"], c["L2"], A.mult)
-        scaled("G34", "GG", c["C3"])
+        vts(m["G34"], m["GG"], c["C3"], A.mult)
         vset(ap("ge", S, VP), 0.0)
 
     def constants_d():
@@ -369,9 +371,9 @@ def rank_program(g, core, T, topo):
         act(ap("fout"), ap("B4", 0, S), F.Relu, bias=-256.0)
         send((STEP[0], ap("fin"), ap("fout"), "top"))
         add_days(0, V // 2)
-        iota(ap("kc"), [[1, 16], [0, 16]], 0, 0)
-        iota(ap("iv"), [[16, 9], [0, 4], [-1024, 4]], 3072, 0)
+        dma("y", ap("cnd", S, RO * S), hbm(T.cand, S, RO * S), Y)
         iota(ap("iw"), [[1024, 4], [1, 128]], 0, 0)
+        iota(ap("iv"), [[16, 9], [0, 4], [-1024, 4]], 3072, 0)
         mms(ap("B5", 0, S), [("GG", ap("fout"))], False, True)
         act(uo(0, 2), ap("B5", 0, S), F.Relu, bias=-256.0)
 
@@ -475,7 +477,9 @@ def rank_program(g, core, T, topo):
         if t == 0:
             for s in TAIL:
                 steps[s[0]](*s[1:])
-            vtt(blk("uw", t, 64), ind(blk("uf", t, 16), rep4), ap("mb"), A.add)
+        if t == 2:
+            vts(ap("uf", 48, 64), ap("so", 0, 16), -1.0, A.mult, float(V), A.add)
+        vtt(blk("uw", t, 64), ind(blk("uf", t, 16), rep4), ap("mb"), A.add)
         vcopy(ap("tr", 0, 64), ap("B2", 0, 64))
         vtt(ap("tr", 64, 128), ap("B2", 64, 128), ap("tr", 0, 64), A.min)
         vtt(ap("tr", 128, 192), ap("B2", 128, 192), ap("tr", 64, 128), A.min)
@@ -494,6 +498,8 @@ def rank_program(g, core, T, topo):
                 mms(ap("B5", s, S, 4), [(name % s, ap("dm", 0, 64))], False, False)
         if not last:
             mms(ap("B4", S, 2 * S), [("D0", nes), ("NID", cY(t))])
+        vcopy(ap("dh", 0, 16), dzb)
+        vtt(ap("dh", 16, 32), dzb, ap("dh", 0, 16), A.subtract)
         vcopy(ap("row"), ap("B2", 0, S))
         vcopy(ap("dm", 64, 128), ind(dzb, rep4))
         for s in range(4):
@@ -504,9 +510,11 @@ def rank_program(g, core, T, topo):
         act(blk("eq", 15), ap("ab"), F.Relu, bias=1.0, scale=-1.0)
         if not last:
             act(dg, ap("B4", S, 2 * S), F.Relu)
+        if t == 1:
+            tag_get(2)
         for j in range(15):
             e = ap("eq", S * j + 16 * (j + 1), S * (j + 1))
-            vts(e, ap("row", 16 * (j + 1), S), ap("dz", 16 + j, 17 + j), A.is_equal)
+            vts(e, ap("row", 16 * (j + 1), S), ap("dh", j, j + 1), A.subtract, ap("dh", 16 + j, 17 + j), A.is_equal)
             mms(ap("B1", 16 * (j + 1), S), [("GG", e)], j == 0, j == 14)
             if j == 14 and not last:
                 mms(ap("B3", 0, S), [("NID", cU), ("GG", blk("tl", 0))])
@@ -516,6 +524,12 @@ def rank_program(g, core, T, topo):
                 mms(ap("B1", 16, S), [("GG", blk("eq", 15, S - 16, S, 16))], False, False)
         if t < 2:
             p_half(t + 2)
+        elif t == 2:
+            constants_d()
+        if last:
+            vts(dzq, dzf, -1.0, A.mult, -2048.0 - S, A.add)
+        else:
+            vts(dzq, dzf, -2048.0, A.add)
         vtt(go(t), cnt, nk, A.is_le)
         verdict = (-STEP[t], blk("vin", t), go(t), "ver%d" % t)
         if last:
@@ -528,15 +542,15 @@ def rank_program(g, core, T, topo):
         mms(wg, [("ID", blk("uw", t, 64))], True, False)
         wrap(wg, "QP", nk, False, False, 4)
         wrap(wg, "QN", go(t), False, True, 4)
+        if t == 1:
+            tag_wrap(2, 1, "B6")
         if last:
-            vts(dzq, dzf, -1.0, A.mult, -2048.0 - S, A.add)
             mms(dg, [("U0", nes), ("ID", nes)])
         else:
             if t:
                 vtt(ap("ge", 0, S), go(t), ap("B0", S, 2 * S), A.is_gt)
-            vts(dzq, dzf, -2048.0, A.add)
-            if t < 2:
-                arrives(ap("jin", 16 * t, 16 + 32 * t), "tag%d" % t)
+            if t != 1:
+                arrives(ap("jin", 16 * t, 32 + 8 * t), "tag%d" % t)
             act(ap("tl", 2 * S, 4 * S), ap("B3"), F.Relu)
             act(ap("gj"), ind(ap("ge") if t else ap("vout", 0, VP), blk("jin", t, 16)), F.Copy)
         vmax4(ap("sc", 64, 128), wg)
@@ -554,14 +568,10 @@ def rank_program(g, core, T, topo):
             for j in range(4):
                 mm(ap("B0", 0, S), shift("BU", j + 1), blk("tl", j), False, False)
             mms(ap("B0", 0, S), [("DJ", ap("gj"))], False, False)
+        if t == 1:
+            tag_out(2, 1, "B6")
         if t:
             vtt(ind(X, su(t - 1)), cY(t - 1), ap("nn"), A.mult)
-        if t == 1:
-            vts(ap("uf", 48, 64), ap("so", 0, 16), -1.0, A.mult, float(V), A.add)
-        if t == 2:
-            constants_d()
-        if not last:
-            vtt(blk("uw", t + 1, 64), ind(blk("uf", t + 1, 16), rep4), ap("mb"), A.add)
 
     def settle(t):
         v, dS, zl = blk("vin", t), ap("B5", 0, S), ap("B4", 0, S)
@@ -572,18 +582,14 @@ def rank_program(g, core, T, topo):
             vtt(ind(Y, su(t)), cY(t), tmp, A.add)
             day_a(t + 1)
             vts(ne, ind(Y, su(t + 1)), 256.0, A.is_lt)
-            act(colg, ind(Y, su(t + 1)), F.Copy)
             mms(zl, [("EMN", ne)], False, True)
-            mms(dS, [("LE0", brow(t)), ("I256", go(t)), ("NID", uo(t, 3)), ("NID", colg)])
+            day_b(t + 1)
+            act(colg, ind(Y, su(t + 1)), F.Copy)
             if t + 2 < RO:
                 vcopy(uo(t + 1, 1), ind(ap("Y", W, V), uu(t + 2)))
             vts(tmp2, zl, c["BY"], A.add, 0.0, A.min)
             vtt(ind(Y, su(t + 1)), colg, tmp2, A.add)
-            if t == 0:
-                tag_wrap(1, 2, "B2")
-            day_b(t + 1)
-            if t == 0:
-                tag_out(1, 2, "B2")
+            mms(dS, [("LE0", brow(t)), ("I256", go(t)), ("NID", uo(t, 3)), ("NID", colg)])
             day_c(t + 1)
             act(uo(t + 1, 2), dS, F.Relu, bias=-256.0)
             send_ask(t + 1)

from concourse.bass import DstId, RemoteDMATransfer
from concourse.mybir import AluOpType, ActivationFunctionType

W, R, S, K, M = 4096, 1024, 256, 16, 97
V = W + R
STEP = (1, 1, 1, 1)
RO = len(STEP)
LOADS = ((V // 2, V), (0, V // 2))
FUSE = 2
EDJ = 11
ENGINES = 16
KLAST = 12
VP = S + 16
BIG = 8192.0
QB = 192.0
SCHED = (("pre", 0, 2), ("c",), ("pre", 1, 2), ("vg", 0, 2), ("sg", 0, 4, 2), ("old",), ("z", 0, 2), ("sg", 1, 8, 2),
         ("vg", 2, 2), ("key", 0, 4), ("z", 1, 2), ("ss", 0, 4, 2), ("pre", 2, 1), ("vg", 6, 2), ("sg", 2, 12, 1),
         ("key", 4, 8), ("z", 2, 1), ("nk",), ("ss", 1, 8, 2), ("vg", 10, 2), ("key", 8, 12), ("ss", 2, 12, 1),
         ("vg", 13, 2), ("vg", 15, 1), ("key", 12, 16))
START = (("mask", 0), ("add", V // 2, V), ("c0",), ("mask", 1), ("ask",), ("put", 0), ("get", 0), ("ca",), ("p", 0),
         ("put", 1), ("res",), ("da", 0), ("pre", 0), ("db", 0), ("get", 1), ("cc",), ("cs",), ("wrap", 0, 2, "B6"),
         ("cb",), ("dc", 0), ("out", 0, 2, "B6"), ("ch",))
TAIL = (("p", 1),)
HOP = (("put", 2),)

BF, F32, I32, U16, F16 = "bfloat16", "float32", "int32", "uint16", "float16"
MATS = ("ID", "NID", "I256", "N256", "I8K", "I97", "N4K", "DG0", "DL", "NDL", "DJ", "GG", "G012", "G34", "LE0",
        "U0", "T1", "NT2", "D0", "EMN", "E0", "E1", "E2", "E3", "F0", "F1", "F2", "F3")
WRAPS = ("BU", "B012", "BW", "QP", "QN")
COLS = ("BX", "NZ15", "B15", "MB", "WCOL", "QM", "CL", "PB", "CJ0")
COLB = ("PM", "G16", "NG2", "A4", "GM", "L2", "C3", "CJ")
SCRATCH = {
    "XB": ("sbuf", [128, S + V], BF), "Y": ("sbuf", [128, V], BF),
    "trk": ("sbuf", [128, 64], I32), "cnd": ("sbuf", [128, 1024], I32), "p16": ("sbuf", [128, 1024], F16),
    "fin": ("sbuf", [128, S], BF), "fout": ("sbuf", [128, S], BF),
    "uin": ("sbuf", [128, 4 * S * RO], BF), "uout": ("sbuf", [128, 6 * S * (RO + 1)], BF),
    "vin": ("sbuf", [128, S * RO], BF), "lin": ("sbuf", [128, S * RO], BF), "vout": ("sbuf", [128, VP * RO], BF),
    "jin": ("sbuf", [128, 48], U16), "jout": ("sbuf", [128, 48], U16),
    "cmp": ("sbuf", [128, K * S], BF), "xg": ("sbuf", [128, 512 * 3], BF), "eq": ("sbuf", [128, 16 * S], BF),
    "iq": ("sbuf", [128, 8], I32), "qf": ("sbuf", [128, 4], BF), "ix": ("sbuf", [128, 144], BF),
    "ig": ("sbuf", [128, 512], BF), "iw": ("sbuf", [128, 512], F32),
    "ia": ("sbuf", [128, S], BF), "kc": ("sbuf", [128, S], BF), "i16": ("sbuf", [128, 16], F32),
    "jr": ("sbuf", [128, S], BF), "i4": ("sbuf", [128, 64], BF), "r4": ("sbuf", [128, 4], F32),
    "iv": ("sbuf", [128, 144], BF), "oh": ("sbuf", [128, 32], BF), "of": ("sbuf", [128, 4], F32),
    "colb": ("sbuf", [128, 8 * len(COLB)], BF),
    "cols": ("sbuf", [128, 4 * len(COLS)], F32), "pmi": ("sbuf", [128, 16], I32),
    "mats": ("sbuf", [128, 128 * len(MATS)], BF), "wraps": ("sbuf", [128, 144 * len(WRAPS)], BF),
    "mlt": ("sbuf", [128, S], BF), "meq": ("sbuf", [128, S], BF),
    "m4": ("sbuf", [128, 64], F32), "mn": ("sbuf", [128, 64], BF), "mb": ("sbuf", [128, 64], F32),
    "rst": ("sbuf", [128, 64], F32), "rep": ("sbuf", [128, 8], U16), "uf": ("sbuf", [128, 64], F32),
    "su": ("sbuf", [128, 160], U16), "uu": ("sbuf", [128, 48], U16), "uw": ("sbuf", [128, 256], F16),
    "TG": ("sbuf", [128, R + S], BF), "tv": ("sbuf", [128, S], BF), "tg": ("sbuf", [128, 3 * S], BF),
    "so": ("sbuf", [128, 64], F32), "s0": ("sbuf", [128, 16], U16),
    "rr": ("sbuf", [128, S], BF), "bw": ("sbuf", [128, 16], BF), "b4": ("sbuf", [128, 64], BF),
    "qq": ("sbuf", [128, S], BF), "cu": ("sbuf", [128, S], U16), "kf": ("sbuf", [128, S], F16),
    "sc": ("sbuf", [128, 128], F32), "tr": ("sbuf", [128, 320], F32), "ki": ("sbuf", [128, 32], I32),
    "dz": ("sbuf", [128, 64], F32), "dm": ("sbuf", [128, 128], F16), "dh": ("sbuf", [128, 32], BF),
    "row": ("sbuf", [128, S], F16), "ab": ("sbuf", [128, S], BF),
    "ne": ("sbuf", [128, S], BF), "tl": ("sbuf", [128, 4 * S], BF), "tmp": ("sbuf", [128, S], BF),
    "tmp2": ("sbuf", [128, S], BF), "nes": ("sbuf", [128, S], BF), "nn": ("sbuf", [128, S], BF),
    "cY": ("sbuf", [128, 2 * S], BF), "neU": ("sbuf", [128, S], BF),
    "ge": ("sbuf", [128, VP], BF), "gj": ("sbuf", [128, S], BF),
}
BANKS = tuple("B%d" % i for i in range(8))
for _b in BANKS:
    SCRATCH[_b] = ("psum", [128, 512], F32)
QUEUES = ("v", "s", "p", "g", "y")
SEMAPHORES = (["q_" + q for q in QUEUES] + [m + str(t) for m in ("ask", "ver", "sel", "opt", "tag") for t in range(RO)]
              + ["top", "sent"] + ["dma%d" % i for i in range(16)])

A = AluOpType
F = ActivationFunctionType


def rank_program(g, core, T, topo):
    rank = T.rank_of(core)
    if rank is None:
        return
    n = len(T.cores)
    Q = {"v": g.vector, "s": g.scalar, "p": g.tensor, "g": g, "y": g.sync}
    ops = []
    ndma = [0]

    def ap(name, a=0, b=None, st=1):
        if b is None:
            b = SCRATCH[name][1][1]
        p = T[name][:, a:b] if st == 1 else T[name][:, a:b:st]
        return (p, [(name, a, b)])

    def blk(name, t, w=S, stride=None, off=0):
        a = t * (stride or w) + off
        return ap(name, a, a + w)

    def ind(win, off):
        return (win[0].indirect(off[0]), win[1] + off[1], win[1], off[1])

    def add(q, emit, ins, out, kind="c", sem=None):
        rd, wr = [], []
        for x in ins:
            if isinstance(x, tuple):
                rd += x[1]
        if out is not None:
            if len(out) == 4:
                wr += out[2]
                rd += out[3]
            else:
                wr += out[1]
        ops.append((q, emit, rd, wr, kind, sem))

    def val(x):
        return x[0] if isinstance(x, tuple) else x

    def vcopy(o, i):
        add("v", lambda: g.vector.tensor_copy(o[0], i[0]), [i], o)

    def vtt(o, a, b, op):
        add("v", lambda: g.vector.tensor_tensor(o[0], a[0], b[0], op), [a, b], o)

    def vts(o, a, s1, op0, s2=None, op1=None):
        if op1 is None:
            add("v", lambda: g.vector.tensor_scalar(o[0], a[0], val(s1), None, op0), [a, s1], o)
        else:
            add("v", lambda: g.vector.tensor_scalar(o[0], a[0], val(s1), val(s2), op0, op1), [a, s1, s2], o)

    def vmax4(o, i):
        rst = ap("rst")
        add("v", lambda: g.vector.tensor_tensor_scan(o[0], rst[0], i[0], 0.0, A.add, A.max), [rst, i], o)

    def vset(o, c):
        add("v", lambda: g.vector.memset(o[0], c), [], o)

    def act(o, i, func, bias=None, scale=None):
        kw = {}
        if bias is not None:
            kw["bias"] = val(bias)
        if scale is not None:
            kw["scale"] = val(scale)
        add("s", lambda: g.scalar.activation(o[0], i[0], func, **kw), [i, bias, scale], o)

    def mm(o, l, r, start, stop):
        add("p", lambda: g.tensor.matmul(o[0], l[0], r[0], start, stop), [l, r], o)

    def mms(o, terms, start=True, stop=True):
        for j, (l, r) in enumerate(terms):
            mm(o, m[l], r, start and j == 0, stop and j == len(terms) - 1)

    def iota(o, pattern, base, cm, small=True):
        if small:
            add("g", lambda: g.iota(o[0], pattern, base, cm, allow_small_or_imprecise_dtypes=True), [], o)
        else:
            add("g", lambda: g.iota(o[0], pattern, base, cm), [], o)

    def dma(q, o, i, after=None):
        sem = "dma%d" % ndma[0]
        ndma[0] += 1
        add(q, lambda: Q[q].dma_start(o[0], i[0]), [i, after], o, "d", sem)

    def hbm(t, a, b):
        return (t[:, a:b], [])

    def send(*writes):
        k = ENGINES // len(writes)
        trs = []
        for j, (step, o, i, sem) in enumerate(writes):
            dst = T.cores[(rank + step) % n]
            rid, pid, _ = topo.addr(dst)
            mask = sum(1 << e for e in topo.engines(core, dst)[j * k:(j + 1) * k])
            trs.append((o[0], i[0], T.sem[sem], pid, rid, mask))
        if len(trs) == 1:
            o, i, sem, pid, rid, mask = trs[0]
            emit = lambda: g.remote_dma(o, i, sem, T.sem.sent, pid, rid, mask)
        else:
            emit = lambda: g.remote_dma_fused(
                [RemoteDMATransfer(dst_ids=[DstId(rid=rid, pnc=pid)], dma_engine_mask=mask, remote_sem=sem, src=i, dst=o)
                 for (o, i, sem, pid, rid, mask) in trs], local_sem=T.sem.sent)
        add("g", emit, [w[2] for w in writes], None, "r")

    def arrives(o, sem, writes=1):
        add(None, ENGINES // writes, [], o, "a", sem)

    c = {k: ap("cols", 4 * j, 4 * j + 1) for j, k in enumerate(COLS)}
    c.update({k: ap("colb", 8 * j, 8 * j + 1) for j, k in enumerate(COLB)})
    c.update({k: ap("qf", j, j + 1) for j, k in enumerate(("QM2", "QM1", "QF", "QP1"))})
    c.update({"T0": ap("of", 0, 1), "T1": ap("of", 1, 2), "T2": ap("of", 2, 3), "T15": ap("oh", 15, 16),
              "BY": ap("oh", 16, 17), "NZ0": ap("oh", 31, 32)})
    m = {k: ap("mats", 128 * j, 128 * (j + 1)) for j, k in enumerate(MATS)}
    wr = {k: ap("wraps", 144 * j, 144 * (j + 1)) for j, k in enumerate(WRAPS)}

    def four(name):
        j = 128 * MATS.index(name)
        return ap("mats", j, j + 512)

    def shift(name, a, top=15):
        j = 144 * WRAPS.index(name) + top - a
        return ap("wraps", j, j + 128)

    def wrap(o, name, src, start, stop, parts=16):
        buf, a0, a1 = src[1][0]
        for a in range(parts):
            mm(o, shift(name, a, parts - 1), ap(buf, a0 + a, a1, parts), start and a == 0, stop and a == parts - 1)

    X = ap("XB", S, S + V)
    Y = ap("Y")
    ne, tmp, tmp2, nes, neU = ap("ne"), ap("tmp"), ap("tmp2"), ap("nes"), ap("neU")
    rep4 = ap("rep", 4, 8)

    def su(t):
        return blk("su", t, 16, 32)

    def uu(t):
        return blk("uu", t - 1, 16)

    def go(t):
        return blk("vout", t, S, VP)

    def uo(t, j, w=1):
        return blk("uout", t, w * S, 6 * S, j * S)

    def ui(t, j, w=1):
        return blk("uin", t, w * S, 4 * S, (j - 1) * S)

    def brow(t, w=S):
        return uo(t, 4, w // S)

    def cY(t):
        return blk("cY", t % 2)

    dma("s", ap("trk"), hbm(T.trucks, 0, 64))
    for a, b in LOADS:
        dma("y", ap("XB", S + a, S + b), hbm(T.days, a, b))
    dma("y", blk("cnd", 0), hbm(T.cand, 0, S))

    iota(ap("iq", 0, 1), [[0, 1]], 0, 1, small=False)
    iota(ap("qf"), [[1, 4]], -2, 1)
    iota(ap("ia"), [[0, 16], [1, 16]], 0, 0)
    iota(ap("i16"), [[16, 16]], V, 0)
    iota(ap("ix"), [[1, 144]], 0, 0)
    iota(ap("ig"), [[1024, 4], [16, 8], [0, 16]], 0, 0)
    iota(ap("jr"), [[-1, S]], S, 0)
    iota(ap("r4"), [[4, 4]], 0, 0)
    iota(ap("i4"), [[0, 16], [1, 4]], 0, 0)
    iota(ap("kc"), [[1, 16], [0, 16]], 0, 0)
    pm, p1, m3, a4 = [ap("pmi", 4 * j, 4 * j + 1) for j in range(4)]
    ix, ig = ap("ix", 0, 128), ap("ig", 0, 128)
    vts(pm, ap("iq", 0, 1), 15, A.bitwise_and)
    vset(ap("TG"), 0.0)
    vts(c["MB"], pm, -0.5, A.add, 256.0, A.mult)
    vcopy(c["PM"], pm)
    act(ap("mlt"), ap("ia"), F.Sigmoid, bias=c["MB"], scale=-256.0)
    vts(ap("oh", 0, 16), ap("ia", 0, 16), c["PM"], A.is_equal)
    vts(c["G16"], pm, -1.0, A.mult, c["QF"], A.add)
    vcopy(ap("of"), ap("oh", 0, 4))
    vts(ap("so", 0, 16), ap("i16"), c["PM"], A.add)
    vts(m["ID"], ix, c["QF"], A.is_equal)
    vts(ap("so", 16, 32), ap("trk", 0, 16), float(W), A.is_lt, BIG, A.mult)
    vts(ap("uu"), ap("trk", 16, 64), -float(W), A.add)
    vtt(ap("so", 32, 48), ap("so", 16, 32), ap("trk", 0, 16), A.add)
    vts(wr["BU"], ap("ix"), -15.0, A.add, c["G16"], A.is_equal)
    vtt(ap("so", 48, 64), ap("so", 32, 48), ap("so", 0, 16), A.min)
    vcopy(su(0), ap("trk", 0, 16))
    vts(ap("s0"), ap("so", 48, 64), -float(W), A.add)

    def tag_put(t):
        vts(ap("tv"), ap("jr"), ap("oh", t, t + 1), A.mult)
        vcopy(ind(ap("TG"), uu(t) if t else ap("s0")), ap("tv"))

    def tag_get(t):
        act(blk("tg", t), ind(ap("TG"), uu(t + 1)), F.Identity, scale=c["T%d" % t])

    def tag_wrap(t, k, bank):
        wrap(ap(bank, 0, 16 * k), "BU", ap("tg", t * S, (t + k) * S), True, True)

    def tag_out(t, k, bank):
        vts(ap("jout", 16 * t, 16 * (t + k)), ap(bank, 0, 16 * k), -1.0, A.mult, float(S), A.add)
        send((STEP[t], ap("jin", 16 * t, 16 * (t + k)), ap("jout", 16 * t, 16 * (t + k)), "tag%d" % t))

    def scaled(name, src, k):
        act(m[name] if name in m else wr[name], m[src] if src in m else wr[src], F.Identity, scale=k)

    def diag(name, k):
        scaled(name, "ID", k)

    def constants_0():
        vts(ap("oh", 16, 32), ap("ia", 0, 16), c["PM"], A.not_equal, 256.0, A.mult)
        scaled("I256", "ID", 256.0)
        scaled("NID", "ID", -1.0)
        vts(m["GG"], ig, c["G16"], A.is_equal)
        vts(m["U0"], ix, c["QM1"], A.is_equal, c["BY"], A.mult)
        vtt(m["D0"], m["I256"], m["U0"], A.subtract)

    def mask_chunk(k):
        a, b = LOADS[k]
        vts(ap("Y", a, b), ap("XB", S + a, S + b), 0.0, A.is_equal, 256.0, A.mult)

    def add_days(a, b):
        o, i = ap("Y", a, b), ap("XB", S + a, S + b)
        sem = "dma%d" % ndma[0]
        ndma[0] += 1
        add("g", lambda: g.dma_start(o[0], i[0], accum_op=A.add, max_dma_last_dim=4096), [i, o], o, "d", sem)

    def constants_a():
        vts(ap("rep", 0, 4), ap("r4"), 0.0, A.mult, c["PM"], A.add)
        diag("I97", float(M))
        diag("N4K", -float(W))
        act(c["NZ15"], c["NZ0"], F.Identity, scale=1.0 / 256)
        act(c["B15"], c["T15"], F.Identity, scale=256.0)
        act(c["WCOL"], c["T15"], F.Identity, scale=15 * 65536.0, bias=65536.0)
        act(c["CL"], c["T0"], F.Identity, scale=2 * BIG, bias=-BIG)
        scaled("BW", "BU", c["WCOL"])
        diag("I8K", BIG)
        diag("N256", -256.0)
        diag("DG0", c["T0"])
        diag("DL", c["CL"])

    def constants_b():
        vts(a4, pm, 2, A.arith_shift_right)
        vts(m3, pm, 3, A.bitwise_and)
        vts(ap("kf"), ap("kc"), W / BIG, A.mult, (2048.0 + W * QB) / BIG, A.add)
        vcopy(c["A4"], a4)
        vts(c["GM"], m3, 1024.0, A.mult, c["G16"], A.add)
        vts(c["QM"], m3, 1024.0, A.mult, c["QF"], A.add)
        vts(c["NG2"], pm, 2.0, A.is_ge, -256.0, A.mult)
        vts(rep4, ap("r4"), c["A4"], A.add)
        vts(ap("m4"), ap("i4"), c["A4"], A.is_equal)
        vts(ap("mn"), ap("i4"), c["A4"], A.not_equal, -2.0, A.mult)
        vts(ap("rst"), ap("i4"), 0.0, A.is_equal, -8 * BIG, A.mult)
        vts(four("E0"), ap("ig"), c["GM"], A.is_equal)
        vts(four("F0"), ap("iw"), c["QM"], A.is_equal)
        vts(ap("meq"), ap("ia"), c["PM"], A.is_equal, -0.25, A.mult)
        vts(m["NT2"], ix, c["QM2"], A.is_equal, c["NG2"], A.mult)
        vts(wr["QP"], ap("iv"), c["G16"], A.is_equal, BIG / 16 / 256, A.mult)

    def constants_h():
        act(ap("mb"), ap("mn"), F.Identity, scale=BIG)
        vts(ap("uf", 0, 48), ap("trk", 16, 64), -float(W), A.add)
        scaled("QN", "QP", -256.0)
        vset(ap("vout", S, VP), 0.0)

    def constants_c():
        vts(p1, pm, 1, A.bitwise_and)
        vts(m["T1"], ix, c["QP1"], A.is_equal, c["NZ0"], A.mult)
        vts(c["CJ0"], p1, -2 * BIG / 256, A.mult, BIG / 256, A.add)
        vts(c["PB"], p1, BIG, A.mult, -BIG, A.add)
        vtt(c["CJ"], c["CJ0"], c["BY"], A.mult)
        vts(c["L2"], pm, 2.0, A.is_le)
        vts(c["C3"], pm, 3.0, A.is_ge)
        vts(m["LE0"], ig, c["QF"], A.is_equal)
        vtt(m["EMN"], m["I256"], m["T1"], A.subtract)

    def constants_s():
        vts(m["DJ"], ix, c["QF"], A.is_equal, c["CJ"], A.mult)
        vts(m["NDL"], m["DL"], -1.0 / 256, A.mult)
        vts(m["G012"], m["GG"], c["L2"], A.mult)
        vts(wr["B012"], wr["BU"], c["L2"], A.mult)
        vts(m["G34"], m["GG"], c["C3"], A.mult)
        vset(ap("ge", S, VP), 0.0)

    def constants_d():
        vts(c["BX"], c["BY"], -1.0, A.mult, -256.0, A.add)
        vset(ap("XB", 0, S), 0.0)

    def p_half(t, k=1):
        vts(blk("p16", t, k * S, S), blk("cnd", t, k * S, S), -2048.0, A.add)

    def first_ask():
        colg = uo(0, 0)
        act(colg, ind(X, su(0)), F.Copy)
        act(ne, colg, F.Sign)
        mms(ap("B4", 0, S), [("ID", colg), ("D0", ne)])
        mms(ap("B5", 0, S), [("NID", colg), ("I256", ne)], True, False)
        act(ap("fout"), ap("B4", 0, S), F.Relu, bias=-256.0)
        send((STEP[0], ap("fin"), ap("fout"), "top"))
        add_days(0, V // 2)
        dma("y", ap("cnd", S, RO * S), hbm(T.cand, S, RO * S), Y)
        iota(ap("iw"), [[1024, 4], [1, 128]], 0, 0)
        iota(ap("iv"), [[16, 9], [0, 4], [-1024, 4]], 3072, 0)
        mms(ap("B5", 0, S), [("GG", ap("fout"))], False, True)
        act(uo(0, 2), ap("B5", 0, S), F.Relu, bias=-256.0)

    def send_ask(t):
        j, w = (1, 2) if t < RO - 1 else (2, 1)
        send((STEP[t], ui(t, j, w), uo(t, j, w), "ask%d" % t))

    def reserve():
        act(uo(0, 1), ind(ap("Y", W, V), uu(1)), F.Copy)
        send_ask(0)

    s1, s2 = ap("B3", 0, S), ap("B7", 0, S)
    na = 16 * KLAST
    kb = ap("B4", 0, S - na)

    def preload(t):
        mms(s2, [("ID", blk("p16", t))], True, False)
        mms(s1, [("ID", blk("p16", t))], True, False)

    def day_a(t):
        if t == 0:
            src = ap("fin")
            arrives(src, "top")
        else:
            src = ap("rr")
            arrives(blk("lin", t - 1), "sel%d" % (t - 1), FUSE)
            mms(ap("B0", 0, S), [("DL", blk("lin", t - 1))], False, True)
            act(src, ap("B0", 0, S), F.Relu, bias=c["PB"])
            mms(ap("B4", 0, S), [("LE0", brow(t - 1)), ("N256", go(t - 1)), ("ID", uo(t - 1, 3))], True, False)
            preload(t)
        wrap(ap("B0", 0, 16), "B012" if t else "BU", src, True, True)
        for h in range(2):
            mms(blk("B1", h), [("G012" if t else "GG", src)])

    def day_b(t):
        act(ap("bw"), ap("B0", 0, 16), F.Copy)
        act(ap("b4"), ind(ap("bw"), ap("rep", 0, 4)), F.Copy)
        for bank in ("B3", "B7"):
            for k in range(4):
                mms(blk(bank, k, 64), [("I97", ap("b4"))], False, bank == "B3" and k == 3)

    def day_c(t):
        act(ap("qq"), s1, F.Identity, bias=QB + 2.0 ** -13, scale=1.0 / W)
        mms(s2, [("N4K", ap("qq"))], False, True)
        act(brow(t, 2 * S), ap("B1"), F.Identity, bias=c["B15"], scale=c["NZ15"])

    def score(t):
        zb = ("B0", "B1", "B0")
        vts(ap("cu"), s2, 2048.0 + W * QB, A.add)

        last_a = max(i for i, s in enumerate(SCHED) if s[0] == "key" and s[1] < KLAST)
        for i, s in enumerate(SCHED):
            if s[0] == "c":
                for bank, a, b in (("B2", 0, na), ("B4", na, S)):
                    mms(ap(bank, 0, b - a), [("ID", blk("p16", t, b - a, S, a)), ("I8K", ap("kf", a, b)),
                                             ("N4K", ap("qq", a, b))], True, False)
                    for k in range((b - a) // 64):
                        mms(blk(bank, k, 64), [("I97", ap("b4"))], False, False)
            elif s[0] == "pre":
                mms(ap(zb[s[1]], 0, S * s[2]), [("NID", brow(t, S * s[2]))], True, False)
            elif s[0] == "old":
                if t:
                    mms(ap("B6", 0, S), [("ID", cY(t - 1)), ("ID", tmp)])
            elif s[0] == "sg":
                act(blk("xg", s[1], S * s[3], 512), ind(Y, ap("cu", 16 * s[2], 16 * (s[2] + s[3]))), F.Copy)
            elif s[0] == "z":
                mms(ap(zb[s[1]], 0, S * s[2]), [("ID", blk("xg", s[1], S * s[2], 512))], False, True)
            elif s[0] == "ss":
                act(ap("cmp", S * s[2], S * (s[2] + s[3])), ap(zb[s[1]], 0, S * s[3]), F.Sigmoid, bias=-128.0, scale=-256.0)
            elif s[0] == "vg":
                vtt(ap("cmp", S * s[1], S * (s[1] + s[2])), ind(Y, ap("cu", 16 * s[1], 16 * (s[1] + s[2]))),
                    brow(t, S * s[2]), A.is_lt)
            elif s[0] == "nk":
                arrives(ui(t, 1, 2), "ask%d" % t)
                mms(ap("B6", S, 2 * S), [("GG", ui(t, 2))] + ([("G34", ap("rr"))] if t else []))
            elif s[1] < KLAST:
                wrap(ap("B2", 16 * s[1], 16 * s[2]), "BW", ap("cmp", S * s[1], S * s[2]), False, i == last_a)
            else:
                wrap(kb, "BW", ap("cmp", S * s[1], S * s[2]), False, True)

    def choose(t):
        last = t == RO - 1
        cnt, dg, wg, nw = ap("B1", 0, S), ap("B5", 0, S), ap("B7", 0, 64), ap("B0", 0, 64)
        dzf, dzb, dzq = ap("dz", 0, 16), ap("dz", 16, 32), ap("dz", 32, 48)
        nk, cU, zl = uo(t, 3), ui(t, 1), ap("B4", 0, S)
        act(nk, ap("B6", S, 2 * S), F.Relu, bias=256.0, scale=-256.0)
        mms(nw, [("I8K", ap("mn"))], True, False)
        wrap(nw, "QP", nk, False, True, 4)
        mms(dg, [("I8K", ap("mlt")), ("I8K", ap("meq"))], True, False)
        if not last:
            send((STEP[t + 1], ui(t, 3, 2), uo(t, 3, 2), "opt%d" % t))
            act(neU, cU, F.Sign, bias=256.0, scale=-1.0)
            mms(ap("B3", 0, S), [("ID", cU), ("D0", neU)])
            mms(ap("B3", S, 2 * S), [("ID", cU), ("U0", neU), ("NT2", neU)])
        act(cY(t), ind(Y, su(t)), F.Copy)
        act(nes, cY(t), F.Sign, bias=256.0, scale=-1.0)
        if not last:
            act(ap("tl", 0, 2 * S), ap("B3"), F.Relu, bias=-256.0)
        if t:
            act(ap("nn"), ap("B6", 0, S), F.Sign, bias=256.0, scale=-1.0)
        if t == 0:
            for s in TAIL:
                steps[s[0]](*s[1:])
        if t == 2:
            vts(ap("uf", 48, 64), ap("so", 0, 16), -1.0, A.mult, float(V), A.add)
        vtt(blk("uw", t, 64), ind(blk("uf", t, 16), rep4), ap("mb"), A.add)
        vcopy(ap("tr", 0, 64), ap("B2", 0, 64))
        vtt(ap("tr", 64, 128), ap("B2", 64, 128), ap("tr", 0, 64), A.min)
        vtt(ap("tr", 128, 192), ap("B2", 128, 192), ap("tr", 64, 128), A.min)
        vtt(ap("tr", 192, 256), ap("B4", 0, 64), ap("tr", 128, 192), A.min)
        vtt(ap("tr", 256, 288), ap("tr", 192, 224), ap("tr", 224, 256), A.min)
        vtt(ap("ki", 0, 16), ap("tr", 256, 272), ap("tr", 272, 288), A.min)
        vts(ap("ki", 16, 32), ap("ki", 0, 16), 0x100FFF, A.bitwise_and)
        vts(dzf, ap("ki", 16, 32), float(W), A.min, -2048.0, A.add)
        vtt(ap("dm", 0, 64), ind(dzf, rep4), ap("m4"), A.mult)
        vmax4(ap("sc", 0, 64), nw)
        vtt(dzb, dzf, ap("sc", 3, 64, 4), A.subtract)
        for s in range(4):
            mm(ap("B2", s, S, 4), m["E%d" % s], ap("dm", 0, 64), True, True)
        for name in ("E%d", "F%d"):
            for s in range(4):
                mms(ap("B5", s, S, 4), [(name % s, ap("dm", 0, 64))], False, False)
        if not last:
            mms(ap("B4", S, 2 * S), [("D0", nes), ("NID", cY(t))])
        vcopy(ap("dh", 0, 16), dzb)
        vtt(ap("dh", 16, 32), dzb, ap("dh", 0, 16), A.subtract)
        vcopy(ap("row"), ap("B2", 0, S))
        vcopy(ap("dm", 64, 128), ind(dzb, rep4))
        for s in range(4):
            mms(ap("B5", s, S, 4), [("NID", ap("dm", 64, 128))], False, s == 3)
        if 0 < t < RO - 1:
            mms(ap("B0", S, 2 * S), [("I256", blk("lin", t - 1)), ("NID", ui(t - 1, 3))])
        act(ap("ab"), dg, F.Abs)
        act(blk("eq", 15), ap("ab"), F.Relu, bias=1.0, scale=-1.0)
        if not last:
            act(dg, ap("B4", S, 2 * S), F.Relu)
        if t == 1:
            tag_get(2)
        for j in range(15):
            e = ap("eq", S * j + 16 * (j + 1), S * (j + 1))
            vts(e, ap("row", 16 * (j + 1), S), ap("dh", j, j + 1), A.subtract, ap("dh", 16 + j, 17 + j), A.is_equal)
            mms(ap("B1", 16 * (j + 1), S), [("GG", e)], j == 0, j == 14)
            if j == 14 and not last:
                mms(ap("B3", 0, S), [("NID", cU), ("GG", blk("tl", 0))])
                mms(ap("B3", S, 2 * S), [("NID", cU), ("U0", neU), ("N256", neU), ("GG", blk("tl", 1))])
            if j == EDJ:
                mms(ap("B1", 0, 16), [("GG", blk("eq", 15, 16, S))], False, False)
                mms(ap("B1", 16, S), [("GG", blk("eq", 15, S - 16, S, 16))], False, False)
        if t < 2:
            p_half(t + 2)
        elif t == 2:
            constants_d()
        if last:
            vts(dzq, dzf, -1.0, A.mult, -2048.0 - S, A.add)
        else:
            vts(dzq, dzf, -2048.0, A.add)
        vtt(go(t), cnt, nk, A.is_le)
        verdict = (-STEP[t], blk("vin", t), go(t), "ver%d" % t)
        if last:
            send(verdict)
        elif FUSE == 2:
            send(verdict, (STEP[t + 1], blk("lin", t), go(t), "sel%d" % t))
        else:
            send(verdict)
            send((STEP[t + 1], blk("lin", t), go(t), "sel%d" % t))
        mms(wg, [("ID", blk("uw", t, 64))], True, False)
        wrap(wg, "QP", nk, False, False, 4)
        wrap(wg, "QN", go(t), False, True, 4)
        if t == 1:
            tag_wrap(2, 1, "B6")
        if last:
            mms(dg, [("U0", nes), ("ID", nes)])
        else:
            if t:
                vtt(ap("ge", 0, S), go(t), ap("B0", S, 2 * S), A.is_gt)
            if t != 1:
                arrives(ap("jin", 16 * t, 32 + 8 * t), "tag%d" % t)
            act(ap("tl", 2 * S, 4 * S), ap("B3"), F.Relu)
            act(ap("gj"), ind(ap("ge") if t else ap("vout", 0, VP), blk("jin", t, 16)), F.Copy)
        vmax4(ap("sc", 64, 128), wg)
        vtt(ap("dz", 48, 64), ap("sc", 67, 128, 4), dzq, A.max)
        if last:
            vts(su(t + 1), ap("dz", 48, 64), -1.0, A.mult)
            mms(zl, [("LE0", brow(t)), ("I256", go(t)), ("NID", nk)], True, False)
        else:
            vts(su(t + 1), ap("dz", 48, 64), float(W), A.add)
            if t == 0:
                for s in HOP:
                    steps[s[0]](*s[1:])
            arrives(ui(t, 3, 2), "opt%d" % t)
            mms(ap("B0", 0, S), [("DG0", ui(t, 4)), ("NDL", ui(t, 3))], True, False)
            for j in range(4):
                mm(ap("B0", 0, S), shift("BU", j + 1), blk("tl", j), False, False)
            mms(ap("B0", 0, S), [("DJ", ap("gj"))], False, False)
        if t == 1:
            tag_out(2, 1, "B6")
        if t:
            vtt(ind(X, su(t - 1)), cY(t - 1), ap("nn"), A.mult)

    def settle(t):
        v, dS, zl = blk("vin", t), ap("B5", 0, S), ap("B4", 0, S)
        colg = uo(t + 1, 0)
        arrives(v, "ver%d" % t, FUSE if t < RO - 1 else 1)
        if t < RO - 1:
            vtt(tmp, v, dS, A.mult)
            vtt(ind(Y, su(t)), cY(t), tmp, A.add)
            day_a(t + 1)
            vts(ne, ind(Y, su(t + 1)), 256.0, A.is_lt)
            mms(zl, [("EMN", ne)], False, True)
            day_b(t + 1)
            act(colg, ind(Y, su(t + 1)), F.Copy)
            if t + 2 < RO:
                vcopy(uo(t + 1, 1), ind(ap("Y", W, V), uu(t + 2)))
            vts(tmp2, zl, c["BY"], A.add, 0.0, A.min)
            vtt(ind(Y, su(t + 1)), colg, tmp2, A.add)
            mms(dS, [("LE0", brow(t)), ("I256", go(t)), ("NID", uo(t, 3)), ("NID", colg)])
            day_c(t + 1)
            act(uo(t + 1, 2), dS, F.Relu, bias=-256.0)
            send_ask(t + 1)
        else:
            vtt(tmp, v, dS, A.is_lt)
            vtt(ind(X, su(t)), cY(t), tmp, A.mult)
            dma("y", hbm(T.y, W, V), ap("XB", S + W, S + V))
            xw = ap("XB", 0, S + W)
            vts(ne, ind(xw, su(t + 1)), 0.0, A.is_gt)
            act(colg, ind(xw, su(t + 1)), F.Copy)
            mms(zl, [("T1", ne), ("N256", ne)], False, True)
            vts(tmp2, zl, c["BX"], A.add, 0.0, A.max)
            vtt(ind(xw, su(t + 1)), colg, tmp2, A.add)
            dma("s", hbm(T.y, 0, W), ap("XB", S, S + W))

    steps = {"mask": mask_chunk, "add": add_days, "c0": constants_0, "ca": constants_a, "cb": constants_b,
             "put": tag_put, "get": tag_get, "wrap": tag_wrap, "out": tag_out, "ask": first_ask, "p": p_half,
             "pre": preload, "da": day_a, "db": day_b, "dc": day_c, "res": reserve, "ch": constants_h,
             "cc": constants_c, "cs": constants_s}
    for s in START:
        steps[s[0]](*s[1:])
    for t in range(RO):
        score(t)
        choose(t)
        settle(t)

    emit_all(g, T, Q, ops)


def emit_all(g, T, Q, ops):
    hist = {}
    need = []
    signal = set()
    known = {q: ({}, set()) for q in QUEUES}
    clock = []
    for j, (q, emit, rd, wr, kind, sem) in enumerate(ops):
        deps = set()
        for acc, is_w in ((rd, False), (wr, True)):
            for (name, a, b) in acc:
                bank = name in BANKS
                for (a2, b2, i, w2) in hist.get(name, []):
                    q2 = ops[i][0]
                    if bank and q2 != q:
                        deps.add(i)
                    elif bank and q == "p":
                        continue
                    elif a < b2 and a2 < b and (is_w or w2):
                        deps.add(i)
        for acc, is_w in ((rd, False), (wr, True)):
            for (name, a, b) in acc:
                hist.setdefault(name, []).append((a, b, j, is_w))
        if kind == "a":
            need.append([])
            clock.append(({}, {j}))
            continue
        eng, ext = known[q]
        waits = []
        for i in sorted(deps, reverse=True):
            qi, ki = ops[i][0], ops[i][4]
            if (ki == "c" and eng.get(qi, -1) >= i) or (ki != "c" and i in ext) or ki == "r":
                continue
            waits.append(i)
            ce, cx = clock[i]
            for e, x in ce.items():
                if eng.get(e, -1) < x:
                    eng[e] = x
            ext.update(cx)
        need.append(waits)
        signal.update(waits)
        ce, cx = dict(eng), set(ext)
        if kind == "c":
            ce[q] = j
        else:
            cx.add(j)
        clock.append((ce, cx))
    count = {q: 0 for q in QUEUES}
    value = {}
    waited = set()
    nsent = 0
    for j, (q, emit, rd, wr, kind, sem) in enumerate(ops):
        if kind == "a":
            value[j] = (sem, emit)
            continue
        for i in need[j]:
            Q[q].wait_ge(T.sem[value[i][0]], value[i][1])
            waited.add(value[i][0])
        ins = emit()
        if kind == "c" and j in signal:
            count[q] += 1
            value[j] = ("q_" + q, count[q])
            ins.then_inc(T.sem["q_" + q], 1)
        elif kind == "d":
            value[j] = (sem, 16)
            ins.then_inc(T.sem[sem], 16)
        elif kind == "r":
            nsent += 1
    g.wait_ge(T.sem.sent, nsent * ENGINES)
    for j, (q, emit, rd, wr, kind, sem) in enumerate(ops):
        if kind in ("d", "a") and sem not in waited:
            g.wait_ge(T.sem[sem], value[j][1])
